import numpy as np
import ml_dtypes


def mxq(x, axis, fmt="e4m3"):
    dtype, down = {"e4m3": (ml_dtypes.float8_e4m3fn, 7), "e5m2": (ml_dtypes.float8_e5m2, 14)}[fmt]
    v = np.moveaxis(np.asarray(x, np.float32).astype(ml_dtypes.bfloat16).astype(np.float64), axis, -1)
    blocks = v.reshape(v.shape[:-1] + (-1, 32))
    amax = np.abs(blocks).max(-1, keepdims=True)
    byte = np.maximum(np.where(amax > 0, np.frexp(amax)[1] - 1 + 127, 0) - down, 1)
    scale = np.exp2(byte - 127.0)
    codes = (blocks / scale).astype(np.float32).astype(dtype).astype(np.float64)
    return np.moveaxis((codes * scale).reshape(v.shape), -1, axis)


WIDE = False


def mx_kscale(k):
    if not WIDE:
        return np.ones(k)
    levels = np.array([10, -10, 5, -5, 0])
    if k % 512:
        return np.exp2(np.random.permutation(np.resize(levels, k // 32))).repeat(32)
    a = np.empty((k // 512, 16))
    for p in range(k // 512):
        a[p, :8] = np.random.permutation(np.resize(levels, 8))
        for g in range(8):
            far = levels[np.abs(levels - a[p, g]) >= 10]
            a[p, g + 8] = far[np.random.randint(len(far))]
    return np.exp2(a.ravel()).repeat(32)


BF16 = ml_dtypes.bfloat16


def bf(x):
    return np.asarray(x, np.float32).astype(BF16)


def f64(x):
    return np.asarray(x).astype(np.float64)


E2M1 = np.array([0.0, 0.5, 1.0, 1.5, 2.0, 3.0, 4.0, 6.0, -0.0, -0.5, -1.0, -1.5, -2.0, -3.0, -4.0, -6.0])


def pack_weight(w, fmt):
    k, n = w.shape
    w = f64(bf(w)).reshape(k // 32, 32, n)
    amax = np.abs(w).max(1)
    if fmt == "e4m3":
        byte = np.frexp(amax)[1] - 1 + 127 - 7
    else:
        mant, ex = np.frexp(amax / 6.0)
        byte = np.where(mant > 0.5, ex, ex - 1) + 127
    byte = np.clip(np.where(amax > 0, byte, 1), 1, 254)
    scaled = (w * np.exp2(127.0 - byte)[:, None, :]).reshape(k, n).astype(np.float32)
    by_word = np.ascontiguousarray(scaled.reshape(k // 512, 128, 4, n).transpose(0, 1, 3, 2))
    if fmt == "e4m3":
        words = by_word.astype(ml_dtypes.float8_e4m3fn).view(np.uint8)
    else:
        c = by_word.astype(ml_dtypes.float4_e2m1fn).view(np.uint8) & 0xF
        words = c[..., 0::2] | (c[..., 1::2] << 4)
    return np.ascontiguousarray(words), np.ascontiguousarray(byte.astype(np.uint8).reshape(k // 512, 16, n))


def unpack_weight(words, scales, fmt):
    g, p, n, _ = words.shape
    if fmt == "e4m3":
        vals = np.ascontiguousarray(words).view(ml_dtypes.float8_e4m3fn).astype(np.float64)
    else:
        nib = np.empty((g, p, n, 4), np.uint8)
        nib[..., 0::2] = words & 0xF
        nib[..., 1::2] = words >> 4
        vals = E2M1[nib]
    vals = vals * np.repeat(np.exp2(scales.astype(np.float64) - 127.0), 8, axis=1)[..., None]
    return vals.transpose(0, 1, 3, 2).reshape(g * 512, n)
def pack4(w):
    words, scales = pack_weight(w, "e2m1")
    return words.reshape(words.shape[0], 128, -1), scales


def unpack4(words, scales):
    return unpack_weight(words.reshape(words.shape[0], 128, -1, 2), scales, "e2m1")


D, P, B = 2048, 1024, 512


def draw0():
    s, t = mx_kscale(P), mx_kscale(D)
    pattern = np.random.standard_normal((D, P))
    decode = (pattern + np.random.standard_normal((D, P))) / np.sqrt(2 * D)
    dec_words, dec_scales = pack4(decode / t[:, None])
    noise = np.exp(0.3 * np.random.standard_normal((D, B)))
    return {"mask": bf(pattern / np.sqrt(P) * s),
            "scenes": bf(np.random.standard_normal((B, P)) / s),
            "dark": bf(0.3 * np.random.standard_normal(D)),
            "inv_sigma": bf(noise * t[:, None]),
            "dec_words": dec_words,
            "dec_scales": dec_scales}


def core(mask, scenes, dark, inv_sigma, dec_words, dec_scales):
    a = mxq(f64(mask), 1, "e4m3")
    x = mxq(f64(scenes), 1, "e4m3")
    y = a @ x.T
    z = (y - f64(dark)[:, None]) * f64(inv_sigma)
    g = unpack4(dec_words, dec_scales)
    image = g.T @ mxq(z, 0, "e4m3")
    return image


def e4m3fn_bytes(y):
    return np.clip(np.asarray(y, np.float64), -448.0, 448.0).astype(np.float32).astype(ml_dtypes.float8_e4m3fn).view(np.uint8)


def e4m3fn_values(b):
    return np.asarray(b, np.uint8).view(ml_dtypes.float8_e4m3fn).astype(np.float64)


def setup_inputs():
    d = draw0()
    x0 = np.asarray(d['mask']).astype(np.float64)
    s = (np.max(np.abs(x0), axis=(0,), keepdims=True) / 448.0).astype(np.float32)
    out = {}
    for k, v in d.items():
        if k == 'mask':
            out['mask_bytes'] = e4m3fn_bytes(x0 / s.astype(np.float64))
            out['mask_scale'] = s
        else:
            out[k] = v
    return out


def reference(mask_bytes, mask_scale, scenes, dark, inv_sigma, dec_words, dec_scales):
    return core(e4m3fn_values(mask_bytes) * mask_scale.astype(np.float64), scenes, dark, inv_sigma, dec_words, dec_scales)

@@ -1,0 +1,375 @@
+import concourse.mybir as mybir
+from concourse.masks import make_identity
+from contextlib import ExitStack
+
+F32 = mybir.dt.float32
+BF16 = mybir.dt.bfloat16
+U32 = mybir.dt.uint32
+I32 = mybir.dt.int32
+U8 = mybir.dt.uint8
+FP8 = mybir.dt.float8_e4m3fn
+E4M3X4 = mybir.dt.float8_e4m3fn_x4
+E2M1X4 = mybir.dt.float4_e2m1fn_x4
+ALU = mybir.AluOpType
+COPY = mybir.ActivationFunctionType.Copy
+
+D, P, B = 2048, 1024, 512
+FLOPS = 2 * 2 * D * P * B
+
+NP = 128
+NG = D // 512
+NPAIR = 2 * NG
+NC = P // 512
+NM = P // 128
+S_UNITS = []
+WARM0 = 6
+WARM1 = 1
+WC0 = 0
+WC1 = 1
+SPLIT = 1
+
+
+def tile_coded_aperture_backprojection_s13_kernel(
+    tc, mask_bytes, mask_scale, scenes, dark, inv_sigma, dec_words, dec_scales, out
+):
+    nc = tc.nc
+    with ExitStack() as ctx, tc.manual_schedule():
+        keep = ctx.enter_context(tc.tile_pool(name="keep", bufs=1))
+        work = ctx.enter_context(tc.tile_pool(name="work", bufs=2))
+        psum = ctx.enter_context(tc.psum_pool(name="psum", bufs=1))
+
+        zeros = keep.tile([NP, 512], BF16, name="zeros")
+        nc.vector.memset(zeros[:], 0.0)
+        mscale = keep.tile([NP, NC, 2, 2], F32, name="mscale")
+        nc.scalar.dma_start(
+            out=mscale[:], in_=mask_scale.rearrange("o (c p u e) -> p (o c) u e", c=NC, p=NP, u=2, e=2)
+        )
+        first = keep.tile([NP, 2], BF16, name="first")
+        nc.scalar.copy(out=first[:], in_=zeros[:, 0:2])
+        darks = keep.tile([NP, NG, 4], BF16, name="darks")
+        nc.scalar.dma_start(out=darks[:], in_=dark.rearrange("(g p t) -> p g t", g=NG, p=NP, t=4))
+        ident = keep.tile([NP, NP], F32, name="ident")
+        make_identity(nc, ident[:])
+        gsc = keep.tile([NP, NG, P], U8, name="gsc", align_bytes=64)
+        nc.gpsimd.memset(gsc[:].bitcast(I32), 0)
+
+        mask_v = mask_bytes.rearrange("(g p t) k -> g p t k", g=NG, p=NP, t=4)
+        sig_v = inv_sigma.rearrange("(g p t) b -> g p t b", g=NG, p=NP, t=4)
+        scn_v = scenes.rearrange("(r p) k -> r p k", p=NP)
+
+        mb = [keep.tile([NP, 2, P], U8, name=f"mb{j}", align_bytes=64) for j in range(NPAIR)]
+        sig = [keep.tile([NP, 4, B], BF16, name=f"sig{g}", align_bytes=64) for g in range(NG)]
+        scn = [keep.tile([NP, P], BF16, name=f"scn{r}", align_bytes=64) for r in range(4)]
+        gw = [keep.tile([NP, 2 * P], U8, name=f"gw{g}", align_bytes=64) for g in range(NG)]
+
+        def load_mask(j):
+            g, h = divmod(j, 2)
+            nc.sync.dma_start(out=mb[j][:], in_=mask_v[g][:, 2 * h : 2 * h + 2, :])
+
+        for j in range(2):
+            for t in range(2):
+                nc.sync.dma_start(out=mb[j][:, t, :], in_=mask_v[0][:, 2 * j + t, :])
+        for r in range(2):
+            nc.sync.dma_start(out=scn[r][:], in_=scn_v[r])
+        load_mask(2)
+        for r in range(2, 4):
+            nc.sync.dma_start(out=scn[r][:], in_=scn_v[r])
+        load_mask(3)
+        nc.sync.dma_start(out=sig[0][:], in_=sig_v[0])
+        for j in range(4, 8):
+            load_mask(j)
+            if j % 2 == 1:
+                nc.sync.dma_start(out=sig[j // 2 - 1][:], in_=sig_v[j // 2 - 1])
+        nc.sync.dma_start(out=sig[3][:], in_=sig_v[3])
+        for q in range(4):
+            nc.sync.dma_start(
+                out=gsc[32 * q : 32 * q + 4].bitcast(I32),
+                in_=dec_scales[:, 4 * q : 4 * q + 4, :].bitcast(I32).rearrange("g q n -> q g n"),
+            )
+        for g in range(NG):
+            nc.sync.dma_start(out=gw[g][:].bitcast(I32), in_=dec_words[g].bitcast(I32))
+
+        scodes = keep.tile([NP, NC, B], U32, name="scodes", align_bytes=64)
+        sscales = keep.tile([NP, NC, B], U8, name="sscales", align_bytes=64)
+        zcodes = [keep.tile([NP, B], U32, name=f"zcodes{g}", align_bytes=64) for g in range(NG)]
+        zscales = [keep.tile([NP, B], U8, name=f"zscales{g}", align_bytes=64) for g in range(NG)]
+        sq = [keep.tile([NP, B, 4], BF16, name=f"sq{c}", align_bytes=64) for c in range(NC)]
+
+        wide = {}
+        tbank = {}
+        qin = {}
+        codes = {}
+        scales = {}
+        ybank = {}
+        zt = {}
+        zq = {}
+        img = {}
+        part = {}
+        pbank = {}
+        sbank = {}
+
+        def bank(tag, shape, name):
+            t = psum.tile(shape, F32, name=name, tag=tag)
+            return t
+
+        def warm(bk, n):
+            for i in range(n):
+                nc.tensor.matmul(out=bk, lhsT=zeros[:, 0:128], rhs=zeros[:], start=True, stop=True)
+
+        def widen(j, t, c0, c1, engine):
+            if j not in wide:
+                wide[j] = work.tile([NP, 2, P], BF16, name=f"wide{j}", tag="wide", bufs=4, align_bytes=64)
+            src = mb[j][:, t, c0:c1].bitcast(FP8)
+            if engine == "v":
+                nc.vector.tensor_copy(out=wide[j][:, t, c0:c1], in_=src)
+            else:
+                nc.scalar.copy(out=wide[j][:, t, c0:c1], in_=src)
+
+        def widen_pair(j):
+            wide[j] = work.tile([NP, 2, P], BF16, name=f"wide{j}", tag="wide", bufs=4, align_bytes=64)
+            nc.scalar.copy(
+                out=wide[j][:].rearrange("p t k -> p (t k)"), in_=mb[j][:].rearrange("p t k -> p (t k)").bitcast(FP8)
+            )
+
+        def turn(bk, tiles, c):
+            for t in range(2):
+                for u in range(2):
+                    nc.tensor.transpose(
+                        bk[:, u, 128 * t : 128 * t + 128], tiles[t][:, 256 * c + u : 256 * (c + 1) : 2], ident[:]
+                    )
+
+        def turn_mask(j, c, n=0):
+            w = wide[j][:].bitcast(F32)
+            bk = bank(f"t{c}", [NP, 2, 256], f"tb{j}_{c}")
+            tbank[j, c] = bk
+            warm(bk[:].rearrange("p u x -> p (u x)"), n)
+            turn(bk, [w[:, 0, :], w[:, 1, :]], c)
+
+        def turn_scenes(h, c, n=0):
+            bk = bank(f"m{2 * h + c}", [NP, 2, 256], f"sb{h}_{c}")
+            sbank[h, c] = bk
+            warm(bk[:].rearrange("p u x -> p (u x)"), n)
+            turn(bk, [scn[2 * h][:].bitcast(F32), scn[2 * h + 1][:].bitcast(F32)], c)
+
+        def empty_scenes(h, c):
+            dst = sq[c][:, 256 * h : 256 * (h + 1), :].rearrange("p x t -> p (x t)").bitcast(F32)
+            nc.scalar.copy(
+                out=dst.rearrange("p (x u) -> p x u", u=2), in_=sbank[h, c][:].rearrange("p u x -> p x u")
+            )
+
+        def quant_scenes(c):
+            nc.vector.quantize_mx(
+                out=scodes[:, c, :].bitcast(E4M3X4),
+                scales=sscales[:, c, :],
+                in_=sq[c][:].rearrange("p x t -> p (x t)"),
+            )
+
+        def product(j, c):
+            if j not in qin:
+                qin[j] = work.tile([NP, NC, 256, 4], BF16, name=f"qin{j}", tag="qin", bufs=3, align_bytes=64)
+            src = tbank[j, c][:].bitcast(BF16).rearrange("p u (x e) -> p x u e", e=2)
+            if (j, c) in S_UNITS:
+                scale_mask_scalar(src, j, c)
+                return
+            nc.vector.tensor_tensor(
+                out=qin[j][:, c].rearrange("p x (u e) -> p x u e", u=2),
+                in0=src,
+                in1=mscale[:, c : c + 1].to_broadcast([NP, 256, 2, 2]),
+                op=ALU.mult,
+            )
+
+        def scale_mask_scalar(src, j, c):
+            for u in range(2):
+                for e in range(2):
+                    nc.scalar.activation(
+                        out=qin[j][:, c, :, 2 * u + e],
+                        in_=src[:, :, u, e],
+                        func=COPY,
+                        scale=mscale[:, c, u, e : e + 1],
+                    )
+
+        def quant_mask(j):
+            codes[j] = work.tile([NP, NC, 256], U32, name=f"codes{j}", tag="codes", bufs=4, align_bytes=64)
+            scales[j] = work.tile([NP, NC, 256], U8, name=f"scales{j}", tag="scales", bufs=4, align_bytes=64)
+            nc.vector.quantize_mx(
+                out=codes[j][:].rearrange("p c x -> p (c x)").bitcast(E4M3X4),
+                scales=scales[j][:].rearrange("p c x -> p (c x)"),
+                in_=qin[j][:].rearrange("p c x t -> p (c x t)"),
+            )
+
+        def project(j, t):
+            ybank[j, t] = bank(f"y{t}", [NP, B], f"y{j}_{t}")
+            cols = slice(128 * t, 128 * t + 128)
+            for c in range(NC):
+                nc.tensor.matmul_mx(
+                    out=ybank[j, t][:],
+                    lhsT=codes[j][:, c, cols].bitcast(E4M3X4),
+                    lhsT_scale=scales[j][:, c, cols],
+                    rhs=scodes[:, c, :].bitcast(E4M3X4),
+                    rhs_scale=sscales[:, c, :],
+                    start=(c == 0),
+                    stop=(c == NC - 1),
+                )
+
+        def whiten(j, t):
+            g, h = divmod(j, 2)
+            s = 2 * h + t
+            if g not in zt:
+                zt[g] = work.tile([NP, 4, B], BF16, name=f"zt{g}", tag="zt", bufs=2, align_bytes=64)
+            nc.vector.scalar_tensor_tensor(
+                out=zt[g][:, s, :],
+                in0=ybank[j, t][:],
+                scalar=darks[:, g, s : s + 1],
+                in1=sig[g][:, s, :],
+                op0=ALU.subtract,
+                op1=ALU.mult,
+            )
+
+        def interleave(g, b0, b1, engine):
+            if g not in zq:
+                zq[g] = work.tile([NP, B, 4], BF16, name=f"zq{g}", tag="zq", bufs=2, align_bytes=64)
+            dst = zq[g][:, b0:b1, :].rearrange("p (c i) t -> p c t i", i=4)
+            src = zt[g][:, :, b0:b1].rearrange("p t (c i) -> p c t i", i=4)
+            if engine == "v":
+                nc.vector.tensor_copy(out=dst, in_=src)
+            else:
+                nc.scalar.copy(out=dst, in_=src)
+
+        def quant_z(g, b0=0, b1=B):
+            nc.vector.quantize_mx(
+                out=zcodes[g][:, b0:b1].bitcast(E4M3X4),
+                scales=zscales[g][:, b0:b1],
+                in_=zq[g][:, b0:b1, :].rearrange("p b t -> p (b t)"),
+            )
+
+        IMG_TAG = ["m0", "m1", "m2", "m3", "t0", "t1", "y0", "y1"]
+        LAST = NG - 1
+
+        def image_pass(bk, m, g, start, stop):
+            nc.tensor.matmul_mx(
+                out=bk[:],
+                lhsT=gw[g][:, 256 * m : 256 * (m + 1)].bitcast(E2M1X4),
+                lhsT_scale=gsc[:, g, 128 * m : 128 * (m + 1)],
+                rhs=zcodes[g][:].bitcast(E4M3X4),
+                rhs_scale=zscales[g][:],
+                start=start,
+                stop=stop,
+            )
+
+        def early(m, g):
+            if g == 0:
+                pbank[m] = bank(f"m{m - 4}", [NP, B], f"early{m}")
+            image_pass(pbank[m], m, g, g == 0, g == 1)
+
+        def park(m):
+            part[m] = keep.tile([NP, B], F32, name=f"part{m}")
+            nc.scalar.copy(out=part[m][:], in_=pbank[m][:])
+
+        def backproject(m, g):
+            g0 = 0 if m < 4 else 2
+            if g == g0:
+                img[m] = bank(IMG_TAG[m], [NP, B], f"img{m}")
+            image_pass(img[m], m, g, g == g0, g == LAST)
+
+        wb = bank("y0", [NP, B], "warmbank")
+        warm(wb[:], WARM0)
+        widen(0, 0, 0, 512, "v")
+        widen(0, 1, 0, 512, "s")
+        widen(0, 0, 512, P, "v")
+        widen(0, 1, 512, P, "v")
+        widen(1, 0, 0, 512, "v")
+        widen(1, 0, 512, P, "s")
+        widen(1, 1, 0, P, "s")
+        turn_mask(0, 0)
+        turn_mask(0, 1)
+        product(0, 0)
+        turn_scenes(0, 0, WARM1)
+        turn_scenes(0, 1)
+        turn_mask(1, 0, WARM1)
+        product(0, 1)
+        turn_mask(1, 1)
+        quant_mask(0)
+        empty_scenes(0, 0)
+        empty_scenes(0, 1)
+        widen_pair(2)
+        turn_scenes(1, 0, WARM1)
+        turn_scenes(1, 1)
+        empty_scenes(1, 0)
+        empty_scenes(1, 1)
+        product(1, 0)
+        turn_mask(2, 0, WARM1)
+        product(1, 1)
+        turn_mask(2, 1)
+        quant_scenes(0)
+        quant_scenes(1)
+        widen_pair(3)
+        quant_mask(1)
+        project(0, 0)
+        project(0, 1)
+
+        for j in range(2, NPAIR):
+            if j == 6:
+                for m in range(4, NM):
+                    early(m, 1)
+            product(j, 0)
+            if j == 2:
+                whiten(0, 0)
+                project(1, 0)
+            if j + 1 < NPAIR:
+                turn_mask(j + 1, 0, WC0)
+            product(j, 1)
+            if j == 2:
+                whiten(0, 1)
+            if j == 2 or SPLIT:
+                project(j - 1, 1)
+            if j == 4:
+                early(4, 0)
+                early(5, 0)
+            if j + 1 < NPAIR:
+                turn_mask(j + 1, 1, WC1)
+            if j + 2 < NPAIR:
+                widen_pair(j + 2)
+            if j == 6:
+                for m in range(4, NM):
+                    park(m)
+            whiten(j - 1, 0)
+            quant_mask(j)
+            whiten(j - 1, 1)
+            if j == 4:
+                early(6, 0)
+                early(7, 0)
+            if j == NPAIR - 1:
+                for m in range(2):
+                    backproject(m, 0)
+                    backproject(m, 1)
+            project(j, 0)
+            if not SPLIT or j == NPAIR - 1:
+                project(j, 1)
+            if j == 6:
+                for m in range(2, 4):
+                    backproject(m, 0)
+                    backproject(m, 1)
+            if j % 2 == 0:
+                g = j // 2 - 1
+                interleave(g, 0, 256, "s")
+                interleave(g, 256, B, "s")
+            else:
+                quant_z((j - 3) // 2)
+
+        whiten(NPAIR - 1, 0)
+        whiten(NPAIR - 1, 1)
+        interleave(LAST, 0, 320, "v")
+        interleave(LAST, 320, B, "s")
+        for m in range(NM):
+            backproject(m, 2)
+        quant_z(LAST, 0, 256)
+        quant_z(LAST, 256, B)
+        out_v = out.rearrange("(m p) b -> m p b", p=NP)
+        for m in (0, 4, 1, 5, 2, 6, 3, 7):
+            backproject(m, LAST)
+            res = work.tile([NP, B], F32, name=f"res{m}", tag="res", bufs=8)
+            if m < 4:
+                nc.scalar.copy(out=res[:], in_=img[m][:])
+            else:
+                nc.vector.tensor_tensor(out=res[:], in0=img[m][:], in1=part[m][:], op=ALU.add)
+            nc.sync.dma_start(out=out_v[m], in_=res[:])

@@ -127,9 +127,8 @@ def tile_coded_aperture_backprojection_s13_kernel(
 
         def widen_pair(j):
             wide[j] = work.tile([NP, 2, P], BF16, name=f"wide{j}", tag="wide", bufs=4, align_bytes=64)
-            nc.scalar.copy(
-                out=wide[j][:].rearrange("p t k -> p (t k)"), in_=mb[j][:].rearrange("p t k -> p (t k)").bitcast(FP8)
-            )
+            nc.scalar.copy(out=wide[j][:, 0, :], in_=mb[j][:, 0, :].bitcast(FP8))
+            nc.gpsimd.tensor_copy(out=wide[j][:, 1, :], in_=mb[j][:, 1, :].bitcast(FP8))
 
         def turn(bk, tiles, c):
             for t in range(2):
@@ -173,8 +172,8 @@ def tile_coded_aperture_backprojection_s13_kernel(
                 return
             nc.vector.tensor_tensor(
                 out=qin[j][:, c].rearrange("p x (u e) -> p x u e", u=2),
-                in0=src,
-                in1=mscale[:, c : c + 1].to_broadcast([NP, 256, 2, 2]),
+                in0=mscale[:, c : c + 1].to_broadcast([NP, 256, 2, 2]),
+                in1=src,
                 op=ALU.mult,
             )
 

@@ -1,6 +1,7 @@
+from contextlib import ExitStack
+
 import concourse.mybir as mybir
 from concourse.masks import make_identity
-from contextlib import ExitStack
 
 F32 = mybir.dt.float32
 BF16 = mybir.dt.bfloat16
@@ -21,12 +22,9 @@ NG = D // 512
 NPAIR = 2 * NG
 NC = P // 512
 NM = P // 128
-S_UNITS = []
-WARM0 = 6
-WARM1 = 1
-WC0 = 0
-WC1 = 1
-SPLIT = 1
+NR = B // 128
+HELD = 4
+WIDE_TAG = ["w0", "w1", "w2", "w3", "q1", "q3", "w6", "q4"]
 
 
 def tile_coded_aperture_backprojection_s13_kernel(
@@ -38,97 +36,74 @@ def tile_coded_aperture_backprojection_s13_kernel(
         work = ctx.enter_context(tc.tile_pool(name="work", bufs=2))
         psum = ctx.enter_context(tc.psum_pool(name="psum", bufs=1))
 
-        zeros = keep.tile([NP, 512], BF16, name="zeros")
-        nc.vector.memset(zeros[:], 0.0)
-        mscale = keep.tile([NP, NC, 2, 2], F32, name="mscale")
-        nc.scalar.dma_start(
-            out=mscale[:], in_=mask_scale.rearrange("o (c p u e) -> p (o c) u e", c=NC, p=NP, u=2, e=2)
-        )
-        first = keep.tile([NP, 2], BF16, name="first")
-        nc.scalar.copy(out=first[:], in_=zeros[:, 0:2])
-        darks = keep.tile([NP, NG, 4], BF16, name="darks")
-        nc.scalar.dma_start(out=darks[:], in_=dark.rearrange("(g p t) -> p g t", g=NG, p=NP, t=4))
-        ident = keep.tile([NP, NP], F32, name="ident")
-        make_identity(nc, ident[:])
-        gsc = keep.tile([NP, NG, P], U8, name="gsc", align_bytes=64)
-        nc.gpsimd.memset(gsc[:].bitcast(I32), 0)
-
         mask_v = mask_bytes.rearrange("(g p t) k -> g p t k", g=NG, p=NP, t=4)
         sig_v = inv_sigma.rearrange("(g p t) b -> g p t b", g=NG, p=NP, t=4)
         scn_v = scenes.rearrange("(r p) k -> r p k", p=NP)
+        out_v = out.rearrange("(m p) b -> m p b", p=NP)
 
+        mscale = keep.tile([NP, NC, 2, 2], F32, name="mscale")
+        darks = keep.tile([NP, NG, 4], BF16, name="darks")
+        ident = keep.tile([NP, NP], F32, name="ident")
+        gsc = keep.tile([NP, NG, P], U8, name="gsc", align_bytes=64)
         mb = [keep.tile([NP, 2, P], U8, name=f"mb{j}", align_bytes=64) for j in range(NPAIR)]
         sig = [keep.tile([NP, 4, B], BF16, name=f"sig{g}", align_bytes=64) for g in range(NG)]
-        scn = [keep.tile([NP, P], BF16, name=f"scn{r}", align_bytes=64) for r in range(4)]
+        scn = [keep.tile([NP, P], BF16, name=f"scn{r}", align_bytes=64) for r in range(NR)]
         gw = [keep.tile([NP, 2 * P], U8, name=f"gw{g}", align_bytes=64) for g in range(NG)]
+        sq = [keep.tile([NP, B, 4], BF16, name=f"sq{c}", align_bytes=64) for c in range(NC)]
+        scodes = keep.tile([NP, NC, B], U32, name="scodes", align_bytes=64)
+        sscales = keep.tile([NP, NC, B], U8, name="sscales", align_bytes=64)
+        zcodes = [keep.tile([NP, B], U32, name=f"zcodes{g}", align_bytes=64) for g in range(NG)]
+        zscales = [keep.tile([NP, B], U8, name=f"zscales{g}", align_bytes=64) for g in range(NG)]
 
-        def load_mask(j):
+        make_identity(nc, ident[:])
+        nc.vector.memset(gsc[:].bitcast(I32), 0)
+
+        def load_pair(j):
             g, h = divmod(j, 2)
             nc.sync.dma_start(out=mb[j][:], in_=mask_v[g][:, 2 * h : 2 * h + 2, :])
 
-        for j in range(2):
-            for t in range(2):
-                nc.sync.dma_start(out=mb[j][:, t, :], in_=mask_v[0][:, 2 * j + t, :])
+        for t in range(2):
+            nc.sync.dma_start(out=mb[0][:, t, :], in_=mask_v[0][:, t, :])
+        nc.sync.dma_start(
+            out=mscale[:], in_=mask_scale.rearrange("o (c p u e) -> p (o c) u e", c=NC, p=NP, u=2, e=2)
+        )
+        load_pair(1)
         for r in range(2):
             nc.sync.dma_start(out=scn[r][:], in_=scn_v[r])
-        load_mask(2)
-        for r in range(2, 4):
+        load_pair(2)
+        for r in range(2, NR):
             nc.sync.dma_start(out=scn[r][:], in_=scn_v[r])
-        load_mask(3)
+        load_pair(3)
+        nc.sync.dma_start(out=darks[:], in_=dark.rearrange("(g p t) -> p g t", g=NG, p=NP, t=4))
         nc.sync.dma_start(out=sig[0][:], in_=sig_v[0])
-        for j in range(4, 8):
-            load_mask(j)
-            if j % 2 == 1:
-                nc.sync.dma_start(out=sig[j // 2 - 1][:], in_=sig_v[j // 2 - 1])
-        nc.sync.dma_start(out=sig[3][:], in_=sig_v[3])
+        load_pair(4)
+        load_pair(6)
+        load_pair(5)
+        nc.sync.dma_start(out=sig[1][:], in_=sig_v[1])
+        load_pair(7)
         for q in range(4):
             nc.sync.dma_start(
                 out=gsc[32 * q : 32 * q + 4].bitcast(I32),
                 in_=dec_scales[:, 4 * q : 4 * q + 4, :].bitcast(I32).rearrange("g q n -> q g n"),
             )
-        for g in range(NG):
-            nc.sync.dma_start(out=gw[g][:].bitcast(I32), in_=dec_words[g].bitcast(I32))
+        nc.sync.dma_start(out=gw[0][:].bitcast(I32), in_=dec_words[0].bitcast(I32))
+        for g in range(2, NG):
+            nc.sync.dma_start(out=sig[g][:], in_=sig_v[g])
+            nc.sync.dma_start(out=gw[g - 1][:].bitcast(I32), in_=dec_words[g - 1].bitcast(I32))
+        nc.sync.dma_start(out=gw[NG - 1][:].bitcast(I32), in_=dec_words[NG - 1].bitcast(I32))
 
-        scodes = keep.tile([NP, NC, B], U32, name="scodes", align_bytes=64)
-        sscales = keep.tile([NP, NC, B], U8, name="sscales", align_bytes=64)
-        zcodes = [keep.tile([NP, B], U32, name=f"zcodes{g}", align_bytes=64) for g in range(NG)]
-        zscales = [keep.tile([NP, B], U8, name=f"zscales{g}", align_bytes=64) for g in range(NG)]
-        sq = [keep.tile([NP, B, 4], BF16, name=f"sq{c}", align_bytes=64) for c in range(NC)]
-
-        wide = {}
-        tbank = {}
-        qin = {}
-        codes = {}
-        scales = {}
-        ybank = {}
-        zt = {}
-        zq = {}
-        img = {}
-        part = {}
-        pbank = {}
-        sbank = {}
-
-        def bank(tag, shape, name):
-            t = psum.tile(shape, F32, name=name, tag=tag)
-            return t
-
-        def warm(bk, n):
-            for i in range(n):
-                nc.tensor.matmul(out=bk, lhsT=zeros[:, 0:128], rhs=zeros[:], start=True, stop=True)
+        wide, tbank, qin, planes, codes, scales, ybank, zt, zq, img, sbank, parked = ({} for i in range(12))
 
         def widen(j, t, c0, c1, engine):
             if j not in wide:
-                wide[j] = work.tile([NP, 2, P], BF16, name=f"wide{j}", tag="wide", bufs=4, align_bytes=64)
+                wide[j] = keep.tile([NP, 2, P], BF16, name=f"wide{j}", tag=WIDE_TAG[j], align_bytes=64)
             src = mb[j][:, t, c0:c1].bitcast(FP8)
             if engine == "v":
                 nc.vector.tensor_copy(out=wide[j][:, t, c0:c1], in_=src)
+            elif engine == "g":
+                nc.gpsimd.tensor_copy(out=wide[j][:, t, c0:c1], in_=src)
             else:
                 nc.scalar.copy(out=wide[j][:, t, c0:c1], in_=src)
-
-        def widen_pair(j):
-            wide[j] = work.tile([NP, 2, P], BF16, name=f"wide{j}", tag="wide", bufs=4, align_bytes=64)
-            nc.scalar.copy(out=wide[j][:, 0, :], in_=mb[j][:, 0, :].bitcast(FP8))
-            nc.gpsimd.tensor_copy(out=wide[j][:, 1, :], in_=mb[j][:, 1, :].bitcast(FP8))
 
         def turn(bk, tiles, c):
             for t in range(2):
@@ -137,18 +112,14 @@ def tile_coded_aperture_backprojection_s13_kernel(
                         bk[:, u, 128 * t : 128 * t + 128], tiles[t][:, 256 * c + u : 256 * (c + 1) : 2], ident[:]
                     )
 
-        def turn_mask(j, c, n=0):
+        def turn_mask(j, c, tag=None):
             w = wide[j][:].bitcast(F32)
-            bk = bank(f"t{c}", [NP, 2, 256], f"tb{j}_{c}")
-            tbank[j, c] = bk
-            warm(bk[:].rearrange("p u x -> p (u x)"), n)
-            turn(bk, [w[:, 0, :], w[:, 1, :]], c)
+            tbank[j, c] = psum.tile([NP, 2, 256], F32, name=f"tb{j}_{c}", tag=tag or f"t{c}")
+            turn(tbank[j, c], [w[:, 0, :], w[:, 1, :]], c)
 
-        def turn_scenes(h, c, n=0):
-            bk = bank(f"m{2 * h + c}", [NP, 2, 256], f"sb{h}_{c}")
-            sbank[h, c] = bk
-            warm(bk[:].rearrange("p u x -> p (u x)"), n)
-            turn(bk, [scn[2 * h][:].bitcast(F32), scn[2 * h + 1][:].bitcast(F32)], c)
+        def turn_scenes(h, c):
+            sbank[h, c] = psum.tile([NP, 2, 256], F32, name=f"sb{h}_{c}", tag=f"m{2 * h + c}")
+            turn(sbank[h, c], [scn[2 * h][:].bitcast(F32), scn[2 * h + 1][:].bitcast(F32)], c)
 
         def empty_scenes(h, c):
             dst = sq[c][:, 256 * h : 256 * (h + 1), :].rearrange("p x t -> p (x t)").bitcast(F32)
@@ -163,29 +134,38 @@ def tile_coded_aperture_backprojection_s13_kernel(
                 in_=sq[c][:].rearrange("p x t -> p (x t)"),
             )
 
-        def product(j, c):
+        def quant_input(j):
             if j not in qin:
-                qin[j] = work.tile([NP, NC, 256, 4], BF16, name=f"qin{j}", tag="qin", bufs=3, align_bytes=64)
-            src = tbank[j, c][:].bitcast(BF16).rearrange("p u (x e) -> p x u e", e=2)
-            if (j, c) in S_UNITS:
-                scale_mask_scalar(src, j, c)
-                return
+                qin[j] = keep.tile([NP, NC, 256, 4], BF16, name=f"qin{j}", tag=f"q{j}", align_bytes=64)
+            return qin[j]
+
+        def product(j, c):
             nc.vector.tensor_tensor(
-                out=qin[j][:, c].rearrange("p x (u e) -> p x u e", u=2),
+                out=quant_input(j)[:, c].rearrange("p x (u e) -> p x u e", u=2),
                 in0=mscale[:, c : c + 1].to_broadcast([NP, 256, 2, 2]),
-                in1=src,
+                in1=tbank[j, c][:].bitcast(BF16).rearrange("p u (x e) -> p x u e", e=2),
                 op=ALU.mult,
             )
 
-        def scale_mask_scalar(src, j, c):
+        def product_planes(j, c):
+            planes[j, c] = work.tile([NP, 4, 256], BF16, name=f"planes{j}_{c}", tag="planes", bufs=2, align_bytes=64)
+            src = tbank[j, c][:].bitcast(BF16).rearrange("p u (x e) -> p u e x", e=2)
             for u in range(2):
                 for e in range(2):
                     nc.scalar.activation(
-                        out=qin[j][:, c, :, 2 * u + e],
-                        in_=src[:, :, u, e],
-                        func=COPY,
-                        scale=mscale[:, c, u, e : e + 1],
+                        out=planes[j, c][:, 2 * u + e, :], in_=src[:, u, e, :], func=COPY, scale=mscale[:, c, u, e : e + 1]
                     )
+
+        def weave(dst, src, engine):
+            dst = dst.rearrange("p (c i) t -> p c t i", i=4)
+            src = src.rearrange("p t (c i) -> p c t i", i=4)
+            if engine == "v":
+                nc.vector.tensor_copy(out=dst, in_=src)
+            else:
+                nc.scalar.copy(out=dst, in_=src)
+
+        def weave_planes(j, c):
+            weave(quant_input(j)[:, c], planes[j, c][:], "s")
 
         def quant_mask(j):
             codes[j] = work.tile([NP, NC, 256], U32, name=f"codes{j}", tag="codes", bufs=4, align_bytes=64)
@@ -196,8 +176,8 @@ def tile_coded_aperture_backprojection_s13_kernel(
                 in_=qin[j][:].rearrange("p c x t -> p (c x t)"),
             )
 
-        def project(j, t):
-            ybank[j, t] = bank(f"y{t}", [NP, B], f"y{j}_{t}")
+        def project(j, t, tag=None):
+            ybank[j, t] = psum.tile([NP, B], F32, name=f"y{j}_{t}", tag=tag or f"y{t}")
             cols = slice(128 * t, 128 * t + 128)
             for c in range(NC):
                 nc.tensor.matmul_mx(
@@ -210,29 +190,24 @@ def tile_coded_aperture_backprojection_s13_kernel(
                     stop=(c == NC - 1),
                 )
 
-        def whiten(j, t):
+        def whiten(j, t, b0=0, b1=B):
             g, h = divmod(j, 2)
             s = 2 * h + t
             if g not in zt:
                 zt[g] = work.tile([NP, 4, B], BF16, name=f"zt{g}", tag="zt", bufs=2, align_bytes=64)
             nc.vector.scalar_tensor_tensor(
-                out=zt[g][:, s, :],
-                in0=ybank[j, t][:],
+                out=zt[g][:, s, b0:b1],
+                in0=ybank[j, t][:, b0:b1],
                 scalar=darks[:, g, s : s + 1],
-                in1=sig[g][:, s, :],
+                in1=sig[g][:, s, b0:b1],
                 op0=ALU.subtract,
                 op1=ALU.mult,
             )
 
-        def interleave(g, b0, b1, engine):
+        def weave_z(g, b0, b1, engine="s"):
             if g not in zq:
                 zq[g] = work.tile([NP, B, 4], BF16, name=f"zq{g}", tag="zq", bufs=2, align_bytes=64)
-            dst = zq[g][:, b0:b1, :].rearrange("p (c i) t -> p c t i", i=4)
-            src = zt[g][:, :, b0:b1].rearrange("p t (c i) -> p c t i", i=4)
-            if engine == "v":
-                nc.vector.tensor_copy(out=dst, in_=src)
-            else:
-                nc.scalar.copy(out=dst, in_=src)
+            weave(zq[g][:, b0:b1, :], zt[g][:, :, b0:b1], engine)
 
         def quant_z(g, b0=0, b1=B):
             nc.vector.quantize_mx(
@@ -241,134 +216,152 @@ def tile_coded_aperture_backprojection_s13_kernel(
                 in_=zq[g][:, b0:b1, :].rearrange("p b t -> p (b t)"),
             )
 
-        IMG_TAG = ["m0", "m1", "m2", "m3", "t0", "t1", "y0", "y1"]
-        LAST = NG - 1
+        img_tag = ["m0", "m1", "m2", "m3", "t0", "t1", "y0", "y1"]
+        last = NG - 1
 
-        def image_pass(bk, m, g, start, stop):
+        def park(m):
+            parked[m] = keep.tile([NP, B], F32, name=f"parked{m}")
+            nc.scalar.copy(out=parked[m][:], in_=img[m][:])
+
+        def backproject(m, g):
+            opens = g == 0 or (m >= HELD and g == 2)
+            closes = g == last or (m >= HELD and g == 1)
+            if opens:
+                tag = img_tag[m - HELD] if m >= HELD and g == 0 else img_tag[m]
+                img[m] = psum.tile([NP, B], F32, name=f"img{m}_{g}", tag=tag)
             nc.tensor.matmul_mx(
-                out=bk[:],
+                out=img[m][:],
                 lhsT=gw[g][:, 256 * m : 256 * (m + 1)].bitcast(E2M1X4),
                 lhsT_scale=gsc[:, g, 128 * m : 128 * (m + 1)],
                 rhs=zcodes[g][:].bitcast(E4M3X4),
                 rhs_scale=zscales[g][:],
-                start=start,
-                stop=stop,
+                start=opens,
+                stop=closes,
             )
 
-        def early(m, g):
-            if g == 0:
-                pbank[m] = bank(f"m{m - 4}", [NP, B], f"early{m}")
-            image_pass(pbank[m], m, g, g == 0, g == 1)
+        def widen_pair(j, engine="g"):
+            for t in range(2):
+                widen(j, t, 0, P, engine)
 
-        def park(m):
-            part[m] = keep.tile([NP, B], F32, name=f"part{m}")
-            nc.scalar.copy(out=part[m][:], in_=pbank[m][:])
+        def whiten_and_project(j):
+            for t in range(2):
+                whiten(j, t)
+                project(j + 1, t)
 
-        def backproject(m, g):
-            g0 = 0 if m < 4 else 2
-            if g == g0:
-                img[m] = bank(IMG_TAG[m], [NP, B], f"img{m}")
-            image_pass(img[m], m, g, g == g0, g == LAST)
-
-        wb = bank("y0", [NP, B], "warmbank")
-        warm(wb[:], WARM0)
         widen(0, 0, 0, 512, "v")
-        widen(0, 1, 0, 512, "s")
-        widen(0, 0, 512, P, "v")
+        widen(0, 0, 512, P, "s")
+        widen(0, 1, 0, 512, "v")
         widen(0, 1, 512, P, "v")
-        widen(1, 0, 0, 512, "v")
-        widen(1, 0, 512, P, "s")
-        widen(1, 1, 0, P, "s")
+        widen(1, 0, 0, P, "s")
+        widen(1, 1, 0, P, "g")
+        widen(2, 0, 0, P, "s")
+        widen(2, 1, 0, P, "g")
+        for c in range(NC):
+            for t in range(2):
+                widen(3, t, 512 * c, 512 * (c + 1), "g")
         turn_mask(0, 0)
         turn_mask(0, 1)
         product(0, 0)
-        turn_scenes(0, 0, WARM1)
-        turn_scenes(0, 1)
-        turn_mask(1, 0, WARM1)
         product(0, 1)
-        turn_mask(1, 1)
         quant_mask(0)
-        empty_scenes(0, 0)
-        empty_scenes(0, 1)
-        widen_pair(2)
-        turn_scenes(1, 0, WARM1)
+        turn_mask(1, 0, "y0")
+        turn_scenes(0, 0)
+        turn_mask(1, 1, "y1")
+        turn_scenes(0, 1)
+        turn_scenes(1, 0)
         turn_scenes(1, 1)
-        empty_scenes(1, 0)
-        empty_scenes(1, 1)
+        for c in range(NC):
+            for h in range(2):
+                empty_scenes(h, c)
         product(1, 0)
-        turn_mask(2, 0, WARM1)
         product(1, 1)
+        turn_mask(3, 0, "m0")
+        turn_mask(2, 0)
         turn_mask(2, 1)
+        turn_mask(3, 1, "m1")
         quant_scenes(0)
         quant_scenes(1)
-        widen_pair(3)
         quant_mask(1)
+        widen_pair(4)
+        widen(6, 0, 0, P, "g")
         project(0, 0)
         project(0, 1)
-
-        for j in range(2, NPAIR):
-            if j == 6:
-                for m in range(4, NM):
-                    early(m, 1)
-            product(j, 0)
-            if j == 2:
-                whiten(0, 0)
-                project(1, 0)
-            if j + 1 < NPAIR:
-                turn_mask(j + 1, 0, WC0)
-            product(j, 1)
-            if j == 2:
-                whiten(0, 1)
-            if j == 2 or SPLIT:
-                project(j - 1, 1)
-            if j == 4:
-                early(4, 0)
-                early(5, 0)
-            if j + 1 < NPAIR:
-                turn_mask(j + 1, 1, WC1)
-            if j + 2 < NPAIR:
-                widen_pair(j + 2)
-            if j == 6:
-                for m in range(4, NM):
-                    park(m)
-            whiten(j - 1, 0)
-            quant_mask(j)
-            whiten(j - 1, 1)
-            if j == 4:
-                early(6, 0)
-                early(7, 0)
-            if j == NPAIR - 1:
-                for m in range(2):
-                    backproject(m, 0)
-                    backproject(m, 1)
-            project(j, 0)
-            if not SPLIT or j == NPAIR - 1:
-                project(j, 1)
-            if j == 6:
-                for m in range(2, 4):
-                    backproject(m, 0)
-                    backproject(m, 1)
-            if j % 2 == 0:
-                g = j // 2 - 1
-                interleave(g, 0, 256, "s")
-                interleave(g, 256, B, "s")
-            else:
-                quant_z((j - 3) // 2)
-
-        whiten(NPAIR - 1, 0)
-        whiten(NPAIR - 1, 1)
-        interleave(LAST, 0, 320, "v")
-        interleave(LAST, 320, B, "s")
-        for m in range(NM):
+        for c in range(NC):
+            product_planes(3, c)
+            weave_planes(3, c)
+        widen(6, 1, 0, P, "s")
+        product(2, 0)
+        product(2, 1)
+        whiten_and_project(0)
+        turn_mask(4, 0)
+        turn_mask(4, 1)
+        quant_mask(2)
+        quant_mask(3)
+        widen_pair(5)
+        whiten_and_project(1)
+        turn_mask(6, 0, "m0")
+        turn_mask(6, 1, "m1")
+        weave_z(0, 0, 256)
+        weave_z(0, 256, B)
+        for c in range(NC):
+            product_planes(6, c)
+            weave_planes(6, c)
+        product(4, 0)
+        product(4, 1)
+        turn_mask(5, 0)
+        turn_mask(5, 1)
+        whiten_and_project(2)
+        quant_mask(4)
+        quant_z(0)
+        widen_pair(7)
+        for m in (6, 7, 4, 5):
+            backproject(m, 0)
+        product(5, 0)
+        product(5, 1)
+        whiten_and_project(3)
+        turn_mask(7, 0)
+        turn_mask(7, 1)
+        weave_z(1, 0, 256)
+        weave_z(1, 256, B)
+        quant_mask(5)
+        quant_mask(6)
+        whiten_and_project(4)
+        product(7, 0)
+        quant_z(1)
+        for m in range(HELD, NM):
+            backproject(m, 1)
+            park(m)
+        product(7, 1)
+        for m in range(2):
+            backproject(m, 0)
+        whiten_and_project(5)
+        for m in range(2, HELD):
+            backproject(m, 0)
+        weave_z(2, 0, 256)
+        weave_z(2, 256, B)
+        quant_mask(7)
+        project(7, 0, "t0")
+        project(7, 1, "t1")
+        for m in range(HELD):
+            backproject(m, 1)
+        j = NPAIR - 1
+        whiten(j - 1, 0)
+        whiten(j - 1, 1)
+        whiten(j, 0)
+        whiten(j, 1)
+        quant_z(2)
+        weave_z(last, 0, 192)
+        weave_z(last, 192, B, "v")
+        for m in range(HELD):
             backproject(m, 2)
-        quant_z(LAST, 0, 256)
-        quant_z(LAST, 256, B)
-        out_v = out.rearrange("(m p) b -> m p b", p=NP)
+        quant_z(last)
         for m in (0, 4, 1, 5, 2, 6, 3, 7):
-            backproject(m, LAST)
-            res = work.tile([NP, B], F32, name=f"res{m}", tag="res", bufs=8)
-            if m < 4:
-                nc.scalar.copy(out=res[:], in_=img[m][:])
+            if m >= HELD:
+                backproject(m, 2)
+            backproject(m, last)
+            res = work.tile([NP, B], F32, name=f"res{m}", tag="res", bufs=NM)
+            if m >= HELD:
+                nc.vector.tensor_tensor(out=res[:], in0=img[m][:], in1=parked[m][:], op=ALU.add)
             else:
-                nc.vector.tensor_tensor(out=res[:], in0=img[m][:], in1=part[m][:], op=ALU.add)
+                nc.scalar.copy(out=res[:], in_=img[m][:])
             nc.sync.dma_start(out=out_v[m], in_=res[:])

@@ -24,7 +24,8 @@ NC = P // 512
 NM = P // 128
 NR = B // 128
 HELD = 4
-WIDE_TAG = ["w0", "w1", "w2", "w3", "q1", "q3", "w6", "q4"]
+HALVED = [(0, 0), (0, 1), (3, 0), (3, 1), (5, 1), (6, 0)]
+WIDE_TAG = {(4, 0, 0): "sq1", (6, 1, 0): "q2", (5, 0, 0): "q3", (7, 0, 0): "z0"}
 
 
 def tile_coded_aperture_backprojection_s13_kernel(
@@ -55,6 +56,8 @@ def tile_coded_aperture_backprojection_s13_kernel(
         zcodes = [keep.tile([NP, B], U32, name=f"zcodes{g}", align_bytes=64) for g in range(NG)]
         zscales = [keep.tile([NP, B], U8, name=f"zscales{g}", align_bytes=64) for g in range(NG)]
 
+        zeros = keep.tile([NP, 256], F32, name="zeros")
+        nc.vector.memset(zeros[:], 0.0)
         make_identity(nc, ident[:])
         nc.vector.memset(gsc[:].bitcast(I32), 0)
 
@@ -68,15 +71,12 @@ def tile_coded_aperture_backprojection_s13_kernel(
             out=mscale[:], in_=mask_scale.rearrange("o (c p u e) -> p (o c) u e", c=NC, p=NP, u=2, e=2)
         )
         load_pair(1)
-        for r in range(2):
+        for r in range(NR):
             nc.sync.dma_start(out=scn[r][:], in_=scn_v[r])
-        load_pair(2)
-        for r in range(2, NR):
-            nc.sync.dma_start(out=scn[r][:], in_=scn_v[r])
-        load_pair(3)
+        for j in range(2, 5):
+            load_pair(j)
         nc.sync.dma_start(out=darks[:], in_=dark.rearrange("(g p t) -> p g t", g=NG, p=NP, t=4))
         nc.sync.dma_start(out=sig[0][:], in_=sig_v[0])
-        load_pair(4)
         load_pair(6)
         load_pair(5)
         nc.sync.dma_start(out=sig[1][:], in_=sig_v[1])
@@ -95,31 +95,40 @@ def tile_coded_aperture_backprojection_s13_kernel(
         wide, tbank, qin, planes, codes, scales, ybank, zt, zq, img, sbank, parked = ({} for i in range(12))
 
         def widen(j, t, c0, c1, engine):
-            if j not in wide:
-                wide[j] = keep.tile([NP, 2, P], BF16, name=f"wide{j}", tag=WIDE_TAG[j], align_bytes=64)
+            for c in range(c0 // 512, c1 // 512):
+                if (j, t, c) not in wide and (j, t) in HALVED:
+                    wide[j, t, c] = keep.tile([NP, 512], BF16, name=f"wide{j}{t}{c}", tag=WIDE_TAG.get((j, t, c), f"wide{j}{t}{c}"), align_bytes=64)
+            if (j, t) not in HALVED:
+                whole = keep.tile([NP, P], BF16, name=f"wide{j}{t}", tag=WIDE_TAG.get((j, t, 0), f"wide{j}{t}"), align_bytes=64)
+                wide[j, t, 0] = whole[:, 0:512]
+                wide[j, t, 1] = whole[:, 512:P]
+                dst = whole[:]
+            else:
+                dst = wide[j, t, c0 // 512][:]
             src = mb[j][:, t, c0:c1].bitcast(FP8)
             if engine == "v":
-                nc.vector.tensor_copy(out=wide[j][:, t, c0:c1], in_=src)
+                nc.vector.tensor_copy(out=dst, in_=src)
             elif engine == "g":
-                nc.gpsimd.tensor_copy(out=wide[j][:, t, c0:c1], in_=src)
+                nc.gpsimd.tensor_copy(out=dst, in_=src)
             else:
-                nc.scalar.copy(out=wide[j][:, t, c0:c1], in_=src)
+                nc.scalar.copy(out=dst, in_=src)
 
-        def turn(bk, tiles, c):
+        def turn(bk, tiles, warm):
+            for i in range(warm):
+                nc.tensor.matmul(out=bk[:, 0, :], lhsT=zeros[:, 0:NP], rhs=zeros[:], start=True, stop=True)
             for t in range(2):
                 for u in range(2):
                     nc.tensor.transpose(
-                        bk[:, u, 128 * t : 128 * t + 128], tiles[t][:, 256 * c + u : 256 * (c + 1) : 2], ident[:]
+                        bk[:, u, 128 * t : 128 * t + 128], tiles[t][:, u : 256 : 2], ident[:]
                     )
 
-        def turn_mask(j, c, tag=None):
-            w = wide[j][:].bitcast(F32)
+        def turn_mask(j, c, tag=None, warm=0):
             tbank[j, c] = psum.tile([NP, 2, 256], F32, name=f"tb{j}_{c}", tag=tag or f"t{c}")
-            turn(tbank[j, c], [w[:, 0, :], w[:, 1, :]], c)
+            turn(tbank[j, c], [wide[j, t, c][:].bitcast(F32) for t in range(2)], warm)
 
-        def turn_scenes(h, c):
+        def turn_scenes(h, c, warm=0):
             sbank[h, c] = psum.tile([NP, 2, 256], F32, name=f"sb{h}_{c}", tag=f"m{2 * h + c}")
-            turn(sbank[h, c], [scn[2 * h][:].bitcast(F32), scn[2 * h + 1][:].bitcast(F32)], c)
+            turn(sbank[h, c], [scn[2 * h + t][:, 512 * c : 512 * (c + 1)].bitcast(F32) for t in range(2)], warm)
 
         def empty_scenes(h, c):
             dst = sq[c][:, 256 * h : 256 * (h + 1), :].rearrange("p x t -> p (x t)").bitcast(F32)
@@ -161,6 +170,8 @@ def tile_coded_aperture_backprojection_s13_kernel(
             src = src.rearrange("p t (c i) -> p c t i", i=4)
             if engine == "v":
                 nc.vector.tensor_copy(out=dst, in_=src)
+            elif engine == "g":
+                nc.gpsimd.tensor_copy(out=dst, in_=src)
             else:
                 nc.scalar.copy(out=dst, in_=src)
 
@@ -206,7 +217,7 @@ def tile_coded_aperture_backprojection_s13_kernel(
 
         def weave_z(g, b0, b1, engine="s"):
             if g not in zq:
-                zq[g] = work.tile([NP, B, 4], BF16, name=f"zq{g}", tag="zq", bufs=2, align_bytes=64)
+                zq[g] = keep.tile([NP, B, 4], BF16, name=f"zq{g}", tag=f"z{g}", align_bytes=64)
             weave(zq[g][:, b0:b1, :], zt[g][:, :, b0:b1], engine)
 
         def quant_z(g, b0=0, b1=B):
@@ -248,116 +259,139 @@ def tile_coded_aperture_backprojection_s13_kernel(
                 whiten(j, t)
                 project(j + 1, t)
 
+        def whiten_pair(j):
+            whiten(j, 0)
+            whiten(j, 1)
+
+        def project_pair(j, tags=(None, None)):
+            project(j, 0, tags[0])
+            project(j, 1, tags[1])
+
+        def weave_group(g):
+            weave_z(g, 0, 256)
+            weave_z(g, 256, B)
+
         widen(0, 0, 0, 512, "v")
         widen(0, 0, 512, P, "s")
         widen(0, 1, 0, 512, "v")
         widen(0, 1, 512, P, "v")
         widen(1, 0, 0, P, "s")
         widen(1, 1, 0, P, "g")
-        widen(2, 0, 0, P, "s")
         widen(2, 1, 0, P, "g")
-        for c in range(NC):
-            for t in range(2):
-                widen(3, t, 512 * c, 512 * (c + 1), "g")
-        turn_mask(0, 0)
+        turn_mask(0, 0, None, 3)
         turn_mask(0, 1)
-        product(0, 0)
-        product(0, 1)
-        quant_mask(0)
+        turn_scenes(0, 0, 1)
+        empty_scenes(0, 0)
+        widen(2, 0, 0, P, "s")
         turn_mask(1, 0, "y0")
-        turn_scenes(0, 0)
         turn_mask(1, 1, "y1")
+        turn_scenes(1, 0, 1)
         turn_scenes(0, 1)
-        turn_scenes(1, 0)
         turn_scenes(1, 1)
-        for c in range(NC):
-            for h in range(2):
-                empty_scenes(h, c)
-        product(1, 0)
-        product(1, 1)
-        turn_mask(3, 0, "m0")
-        turn_mask(2, 0)
+        empty_scenes(1, 0)
+        empty_scenes(0, 1)
+        empty_scenes(1, 1)
+        widen(3, 0, 512, P, "s")
+        widen(3, 1, 512, P, "s")
+        widen(3, 0, 0, 512, "s")
+        for j in range(2):
+            for c in range(NC):
+                product(j, c)
+        turn_mask(2, 0, None, 1)
         turn_mask(2, 1)
-        turn_mask(3, 1, "m1")
+        quant_mask(0)
         quant_scenes(0)
-        quant_scenes(1)
         quant_mask(1)
+        quant_scenes(1)
         widen_pair(4)
-        widen(6, 0, 0, P, "g")
-        project(0, 0)
-        project(0, 1)
-        for c in range(NC):
-            product_planes(3, c)
-            weave_planes(3, c)
-        widen(6, 1, 0, P, "s")
+        widen(3, 1, 0, 512, "g")
+        widen(6, 0, 512, P, "g")
+        turn_mask(3, 1, "m0", 1)
+        project_pair(0)
+        project_pair(1, ("m2", "m3"))
+        product_planes(3, 1)
+        weave_planes(3, 1)
         product(2, 0)
         product(2, 1)
-        whiten_and_project(0)
-        turn_mask(4, 0)
         turn_mask(4, 1)
+        turn_mask(3, 0)
+        product_planes(4, 1)
+        weave_planes(4, 1)
+        whiten_pair(0)
+        whiten_pair(1)
+        weave_group(0)
         quant_mask(2)
+        widen(6, 1, 0, P, "g")
+        widen(6, 0, 0, 512, "g")
+        project_pair(2)
+        product(3, 0)
+        turn_mask(4, 0)
+        turn_mask(6, 1)
+        product_planes(6, 1)
+        widen(5, 1, 512, P, "s")
+        weave_planes(6, 1)
+        whiten_pair(2)
         quant_mask(3)
-        widen_pair(5)
-        whiten_and_project(1)
-        turn_mask(6, 0, "m0")
-        turn_mask(6, 1, "m1")
-        weave_z(0, 0, 256)
-        weave_z(0, 256, B)
-        for c in range(NC):
-            product_planes(6, c)
-            weave_planes(6, c)
+        widen(5, 0, 0, P, "g")
+        widen(5, 1, 0, 512, "g")
+        project_pair(3)
         product(4, 0)
-        product(4, 1)
+        whiten_pair(3)
+        weave_group(1)
         turn_mask(5, 0)
         turn_mask(5, 1)
-        whiten_and_project(2)
         quant_mask(4)
         quant_z(0)
         widen_pair(7)
-        for m in (6, 7, 4, 5):
-            backproject(m, 0)
+        project_pair(4)
         product(5, 0)
+        backproject(4, 0)
+        backproject(5, 0)
         product(5, 1)
-        whiten_and_project(3)
-        turn_mask(7, 0)
         turn_mask(7, 1)
-        weave_z(1, 0, 256)
-        weave_z(1, 256, B)
+        turn_mask(6, 0)
+        backproject(6, 0)
+        backproject(7, 0)
+        product_planes(7, 1)
+        weave_planes(7, 1)
+        whiten_pair(4)
         quant_mask(5)
-        quant_mask(6)
-        whiten_and_project(4)
-        product(7, 0)
         quant_z(1)
+        project_pair(5)
+        product(6, 0)
         for m in range(HELD, NM):
             backproject(m, 1)
+            if m == HELD + 1:
+                turn_mask(7, 0)
             park(m)
-        product(7, 1)
-        for m in range(2):
-            backproject(m, 0)
-        whiten_and_project(5)
-        for m in range(2, HELD):
-            backproject(m, 0)
+        whiten_pair(5)
         weave_z(2, 0, 256)
-        weave_z(2, 256, B)
-        quant_mask(7)
-        project(7, 0, "t0")
-        project(7, 1, "t1")
-        for m in range(HELD):
+        quant_mask(6)
+        weave_z(2, 256, B, "g")
+        project_pair(6)
+        for m in range(HELD - 1):
+            backproject(m, 0)
             backproject(m, 1)
-        j = NPAIR - 1
-        whiten(j - 1, 0)
-        whiten(j - 1, 1)
-        whiten(j, 0)
-        whiten(j, 1)
+        product(7, 0)
+        whiten(6, 0)
+        quant_mask(7)
+        project_pair(7, ("t1", "t0"))
+        backproject(HELD - 1, 0)
+        backproject(HELD - 1, 1)
+        whiten(6, 1)
         quant_z(2)
-        weave_z(last, 0, 192)
-        weave_z(last, 192, B, "v")
-        for m in range(HELD):
+        for m in (0, 1, 2, 3, 6, 7):
             backproject(m, 2)
-        quant_z(last)
+        whiten(7, 0)
+        whiten(7, 1, 0, 256)
+        weave_z(last, 0, 256)
+        whiten(7, 1, 256, B)
+        weave_z(last, 256, B, "v")
+        for m in (5, 4):
+            backproject(m, 2)
+        quant_z(last, 256, B)
+        quant_z(last, 0, 256)
         for m in (0, 4, 1, 5, 2, 6, 3, 7):
-            if m >= HELD:
-                backproject(m, 2)
             backproject(m, last)
             res = work.tile([NP, B], F32, name=f"res{m}", tag="res", bufs=NM)
             if m >= HELD:

@@ -24,8 +24,8 @@ NC = P // 512
 NM = P // 128
 NR = B // 128
 HELD = 4
-HALVED = [(0, 0), (0, 1), (3, 0), (3, 1), (5, 1), (6, 0)]
-WIDE_TAG = {(4, 0, 0): "sq1", (6, 1, 0): "q2", (5, 0, 0): "q3", (7, 0, 0): "z0"}
+HALVED = [(0, 0), (0, 1), (3, 0), (3, 1), (5, 0), (6, 1), (7, 0), (7, 1)]
+WIDE_TAG = {(4, 0, 0): "sq1", (5, 1, 0): "q2", (6, 0, 0): "q3", (6, 1, 0): "z0", (7, 0, 0): "q5"}
 
 
 def tile_coded_aperture_backprojection_s13_kernel(
@@ -77,8 +77,8 @@ def tile_coded_aperture_backprojection_s13_kernel(
             load_pair(j)
         nc.sync.dma_start(out=darks[:], in_=dark.rearrange("(g p t) -> p g t", g=NG, p=NP, t=4))
         nc.sync.dma_start(out=sig[0][:], in_=sig_v[0])
-        load_pair(6)
         load_pair(5)
+        load_pair(6)
         nc.sync.dma_start(out=sig[1][:], in_=sig_v[1])
         load_pair(7)
         for q in range(4):
@@ -92,7 +92,7 @@ def tile_coded_aperture_backprojection_s13_kernel(
             nc.sync.dma_start(out=gw[g - 1][:].bitcast(I32), in_=dec_words[g - 1].bitcast(I32))
         nc.sync.dma_start(out=gw[NG - 1][:].bitcast(I32), in_=dec_words[NG - 1].bitcast(I32))
 
-        wide, tbank, qin, planes, codes, scales, ybank, zt, zq, img, sbank, parked = ({} for i in range(12))
+        wide, tbank, qin, planes, codes, scales, ybank, zt, zq, img, sbank = ({} for i in range(11))
 
         def widen(j, t, c0, c1, engine):
             for c in range(c0 // 512, c1 // 512):
@@ -166,12 +166,15 @@ def tile_coded_aperture_backprojection_s13_kernel(
                     )
 
         def weave(dst, src, engine):
+            if engine == "g":
+                nc.gpsimd.tensor_scalar(
+                    out=dst, in0=src.rearrange("p t x -> p x t"), scalar1=1.0, scalar2=0.0, op0=ALU.mult, op1=ALU.add
+                )
+                return
             dst = dst.rearrange("p (c i) t -> p c t i", i=4)
             src = src.rearrange("p t (c i) -> p c t i", i=4)
             if engine == "v":
                 nc.vector.tensor_copy(out=dst, in_=src)
-            elif engine == "g":
-                nc.gpsimd.tensor_copy(out=dst, in_=src)
             else:
                 nc.scalar.copy(out=dst, in_=src)
 
@@ -205,7 +208,7 @@ def tile_coded_aperture_backprojection_s13_kernel(
             g, h = divmod(j, 2)
             s = 2 * h + t
             if g not in zt:
-                zt[g] = work.tile([NP, 4, B], BF16, name=f"zt{g}", tag="zt", bufs=2, align_bytes=64)
+                zt[g] = work.tile([NP, 4, B], BF16, name=f"zt{g}", tag="zt", bufs=NG, align_bytes=64)
             nc.vector.scalar_tensor_tensor(
                 out=zt[g][:, s, b0:b1],
                 in0=ybank[j, t][:, b0:b1],
@@ -216,38 +219,37 @@ def tile_coded_aperture_backprojection_s13_kernel(
             )
 
         def weave_z(g, b0, b1, engine="s"):
-            if g not in zq:
+            h = b0 // 256
+            if (g, h) not in zq and g == 2:
+                half = keep.tile([NP, 256, 4], BF16, name=f"zq{g}{h}", tag=("z2", "q6")[h], align_bytes=64)
+                zq[g, h] = half[:]
+            elif (g, h) not in zq:
                 zq[g] = keep.tile([NP, B, 4], BF16, name=f"zq{g}", tag=f"z{g}", align_bytes=64)
-            weave(zq[g][:, b0:b1, :], zt[g][:, :, b0:b1], engine)
+                zq[g, 0] = zq[g][:, 0:256, :]
+                zq[g, 1] = zq[g][:, 256:B, :]
+            weave(zq[g, h][:, b0 - 256 * h : b1 - 256 * h, :], zt[g][:, :, b0:b1], engine)
 
         def quant_z(g, b0=0, b1=B):
             nc.vector.quantize_mx(
                 out=zcodes[g][:, b0:b1].bitcast(E4M3X4),
                 scales=zscales[g][:, b0:b1],
-                in_=zq[g][:, b0:b1, :].rearrange("p b t -> p (b t)"),
+                in_=(zq[g][:] if b1 - b0 == B else zq[g, b0 // 256]).rearrange("p b t -> p (b t)"),
             )
 
         img_tag = ["m0", "m1", "m2", "m3", "t0", "t1", "y0", "y1"]
         last = NG - 1
 
-        def park(m):
-            parked[m] = keep.tile([NP, B], F32, name=f"parked{m}")
-            nc.scalar.copy(out=parked[m][:], in_=img[m][:])
-
         def backproject(m, g):
-            opens = g == 0 or (m >= HELD and g == 2)
-            closes = g == last or (m >= HELD and g == 1)
-            if opens:
-                tag = img_tag[m - HELD] if m >= HELD and g == 0 else img_tag[m]
-                img[m] = psum.tile([NP, B], F32, name=f"img{m}_{g}", tag=tag)
+            if g == 0:
+                img[m] = psum.tile([NP, B], F32, name=f"img{m}", tag=img_tag[m])
             nc.tensor.matmul_mx(
                 out=img[m][:],
                 lhsT=gw[g][:, 256 * m : 256 * (m + 1)].bitcast(E2M1X4),
                 lhsT_scale=gsc[:, g, 128 * m : 128 * (m + 1)],
                 rhs=zcodes[g][:].bitcast(E4M3X4),
                 rhs_scale=zscales[g][:],
-                start=opens,
-                stop=closes,
+                start=(g == 0),
+                stop=(g == last),
             )
 
         def widen_pair(j, engine="g"):
@@ -266,6 +268,10 @@ def tile_coded_aperture_backprojection_s13_kernel(
         def project_pair(j, tags=(None, None)):
             project(j, 0, tags[0])
             project(j, 1, tags[1])
+
+        def scale_on_scalar(j):
+            product_planes(j, 1)
+            weave_planes(j, 1)
 
         def weave_group(g):
             weave_z(g, 0, 256)
@@ -305,97 +311,102 @@ def tile_coded_aperture_backprojection_s13_kernel(
         quant_scenes(1)
         widen_pair(4)
         widen(3, 1, 0, 512, "g")
-        widen(6, 0, 512, P, "g")
+        widen(5, 0, 512, P, "g")
         turn_mask(3, 1, "m0", 1)
         project_pair(0)
         project_pair(1, ("m2", "m3"))
-        product_planes(3, 1)
-        weave_planes(3, 1)
+        scale_on_scalar(3)
         product(2, 0)
         product(2, 1)
         turn_mask(4, 1)
         turn_mask(3, 0)
         product_planes(4, 1)
-        weave_planes(4, 1)
         whiten_pair(0)
         whiten_pair(1)
-        weave_group(0)
+        weave_z(0, 0, 256)
+        weave_planes(4, 1)
         quant_mask(2)
-        widen(6, 1, 0, P, "g")
-        widen(6, 0, 0, 512, "g")
+        widen(5, 1, 0, P, "g")
+        widen(5, 0, 0, 512, "g")
         project_pair(2)
         product(3, 0)
+        turn_mask(5, 1)
         turn_mask(4, 0)
-        turn_mask(6, 1)
-        product_planes(6, 1)
-        widen(5, 1, 512, P, "s")
-        weave_planes(6, 1)
+        product_planes(5, 1)
+        weave_z(0, 256, B)
+        weave_planes(5, 1)
         whiten_pair(2)
         quant_mask(3)
-        widen(5, 0, 0, P, "g")
-        widen(5, 1, 0, 512, "g")
+        widen(6, 0, 0, P, "g")
+        widen(6, 1, 512, P, "g")
         project_pair(3)
         product(4, 0)
-        whiten_pair(3)
-        weave_group(1)
         turn_mask(5, 0)
-        turn_mask(5, 1)
+        turn_mask(6, 1)
+        product_planes(6, 1)
+        whiten_pair(3)
+        weave_z(1, 0, 256)
+        weave_planes(6, 1)
         quant_mask(4)
         quant_z(0)
-        widen_pair(7)
+        widen(6, 1, 0, 512, "g")
+        widen(7, 0, 512, P, "g")
+        widen(7, 1, 512, P, "g")
         project_pair(4)
         product(5, 0)
-        backproject(4, 0)
-        backproject(5, 0)
-        product(5, 1)
-        turn_mask(7, 1)
+        backproject(0, 0)
+        backproject(1, 0)
         turn_mask(6, 0)
-        backproject(6, 0)
-        backproject(7, 0)
+        turn_mask(7, 1)
         product_planes(7, 1)
         weave_planes(7, 1)
+        weave_z(1, 256, B)
         whiten_pair(4)
         quant_mask(5)
-        quant_z(1)
+        widen(7, 0, 0, 512, "g")
+        widen(7, 1, 0, 512, "g")
         project_pair(5)
         product(6, 0)
-        for m in range(HELD, NM):
-            backproject(m, 1)
-            if m == HELD + 1:
-                turn_mask(7, 0)
-            park(m)
+        backproject(2, 0)
+        turn_mask(7, 0)
+        backproject(3, 0)
+        backproject(5, 0)
         whiten_pair(5)
         weave_z(2, 0, 256)
         quant_mask(6)
         weave_z(2, 256, B, "g")
         project_pair(6)
-        for m in range(HELD - 1):
-            backproject(m, 0)
-            backproject(m, 1)
         product(7, 0)
+        backproject(4, 0)
         whiten(6, 0)
         quant_mask(7)
-        project_pair(7, ("t1", "t0"))
-        backproject(HELD - 1, 0)
-        backproject(HELD - 1, 1)
+        project(7, 0)
         whiten(6, 1)
-        quant_z(2)
-        for m in (0, 1, 2, 3, 6, 7):
-            backproject(m, 2)
-        whiten(7, 0)
+        project(7, 1)
+        quant_z(1)
+        for m in range(6):
+            backproject(m, 1)
+        whiten(7, 0, 0, 256)
         whiten(7, 1, 0, 256)
         weave_z(last, 0, 256)
+        whiten(7, 0, 256, B)
         whiten(7, 1, 256, B)
-        weave_z(last, 256, B, "v")
-        for m in (5, 4):
+        quant_z(2, 0, 256)
+        quant_z(2, 256, B)
+        for m in range(4):
             backproject(m, 2)
-        quant_z(last, 256, B)
+        weave_z(last, 256, 320)
+        weave_z(last, 320, B, "v")
         quant_z(last, 0, 256)
-        for m in (0, 4, 1, 5, 2, 6, 3, 7):
+        quant_z(last, 256, B)
+        for m in range(NM):
+            if m >= 4:
+                for g in range(2 if m < 6 else 0, last):
+                    backproject(m, g)
             backproject(m, last)
             res = work.tile([NP, B], F32, name=f"res{m}", tag="res", bufs=NM)
-            if m >= HELD:
-                nc.vector.tensor_tensor(out=res[:], in0=img[m][:], in1=parked[m][:], op=ALU.add)
+            if m % 2 == 0:
+                nc.vector.tensor_copy(out=res[:], in_=img[m][:])
             else:
                 nc.scalar.copy(out=res[:], in_=img[m][:])
             nc.sync.dma_start(out=out_v[m], in_=res[:])

@@ -56,8 +56,6 @@ def tile_coded_aperture_backprojection_s13_kernel(
         zcodes = [keep.tile([NP, B], U32, name=f"zcodes{g}", align_bytes=64) for g in range(NG)]
         zscales = [keep.tile([NP, B], U8, name=f"zscales{g}", align_bytes=64) for g in range(NG)]
 
-        zeros = keep.tile([NP, 256], F32, name="zeros")
-        nc.vector.memset(zeros[:], 0.0)
         make_identity(nc, ident[:])
         nc.vector.memset(gsc[:].bitcast(I32), 0)
 
@@ -113,22 +111,20 @@ def tile_coded_aperture_backprojection_s13_kernel(
             else:
                 nc.scalar.copy(out=dst, in_=src)
 
-        def turn(bk, tiles, warm):
-            for i in range(warm):
-                nc.tensor.matmul(out=bk[:, 0, :], lhsT=zeros[:, 0:NP], rhs=zeros[:], start=True, stop=True)
+        def turn(bk, tiles):
             for t in range(2):
                 for u in range(2):
                     nc.tensor.transpose(
                         bk[:, u, 128 * t : 128 * t + 128], tiles[t][:, u : 256 : 2], ident[:]
                     )
 
-        def turn_mask(j, c, tag=None, warm=0):
+        def turn_mask(j, c, tag=None):
             tbank[j, c] = psum.tile([NP, 2, 256], F32, name=f"tb{j}_{c}", tag=tag or f"t{c}")
-            turn(tbank[j, c], [wide[j, t, c][:].bitcast(F32) for t in range(2)], warm)
+            turn(tbank[j, c], [wide[j, t, c][:].bitcast(F32) for t in range(2)])
 
-        def turn_scenes(h, c, warm=0):
+        def turn_scenes(h, c):
             sbank[h, c] = psum.tile([NP, 2, 256], F32, name=f"sb{h}_{c}", tag=f"m{2 * h + c}")
-            turn(sbank[h, c], [scn[2 * h + t][:, 512 * c : 512 * (c + 1)].bitcast(F32) for t in range(2)], warm)
+            turn(sbank[h, c], [scn[2 * h + t][:, 512 * c : 512 * (c + 1)].bitcast(F32) for t in range(2)])
 
         def empty_scenes(h, c):
             dst = sq[c][:, 256 * h : 256 * (h + 1), :].rearrange("p x t -> p (x t)").bitcast(F32)
@@ -284,14 +280,14 @@ def tile_coded_aperture_backprojection_s13_kernel(
         widen(1, 0, 0, P, "s")
         widen(1, 1, 0, P, "g")
         widen(2, 1, 0, P, "g")
-        turn_mask(0, 0, None, 3)
+        turn_mask(0, 0)
         turn_mask(0, 1)
-        turn_scenes(0, 0, 1)
+        turn_scenes(0, 0)
         empty_scenes(0, 0)
         widen(2, 0, 0, P, "s")
         turn_mask(1, 0, "y0")
         turn_mask(1, 1, "y1")
-        turn_scenes(1, 0, 1)
+        turn_scenes(1, 0)
         turn_scenes(0, 1)
         turn_scenes(1, 1)
         empty_scenes(1, 0)
@@ -303,7 +299,7 @@ def tile_coded_aperture_backprojection_s13_kernel(
         for j in range(2):
             for c in range(NC):
                 product(j, c)
-        turn_mask(2, 0, None, 1)
+        turn_mask(2, 0)
         turn_mask(2, 1)
         quant_mask(0)
         quant_scenes(0)
@@ -312,7 +308,7 @@ def tile_coded_aperture_backprojection_s13_kernel(
         widen_pair(4)
         widen(3, 1, 0, 512, "g")
         widen(5, 0, 512, P, "g")
-        turn_mask(3, 1, "m0", 1)
+        turn_mask(3, 1, "m0")
         project_pair(0)
         project_pair(1, ("m2", "m3"))
         scale_on_scalar(3)

@@ -24,8 +24,8 @@ NC = P // 512
 NM = P // 128
 NR = B // 128
 HELD = 4
-HALVED = [(0, 0), (0, 1), (3, 0), (3, 1), (5, 0), (6, 1), (7, 0), (7, 1)]
-WIDE_TAG = {(4, 0, 0): "sq1", (5, 1, 0): "q2", (6, 0, 0): "q3", (6, 1, 0): "z0", (7, 0, 0): "q5"}
+HALVED = [(0, 0), (0, 1), (1, 0), (1, 1), (3, 0), (3, 1), (6, 1), (7, 0), (7, 1)]
+WIDE_TAG = {(4, 0, 0): "sq1", (5, 1, 0): "q2", (6, 0, 0): "q3", (7, 0, 1): "z0", (7, 0, 0): "q5"}
 
 
 def tile_coded_aperture_backprojection_s13_kernel(
@@ -63,15 +63,19 @@ def tile_coded_aperture_backprojection_s13_kernel(
             g, h = divmod(j, 2)
             nc.sync.dma_start(out=mb[j][:], in_=mask_v[g][:, 2 * h : 2 * h + 2, :])
 
-        for t in range(2):
-            nc.sync.dma_start(out=mb[0][:, t, :], in_=mask_v[0][:, t, :])
+        nc.sync.dma_start(out=mb[0][:, 0, :], in_=mask_v[0][:, 0, :])
         nc.sync.dma_start(
             out=mscale[:], in_=mask_scale.rearrange("o (c p u e) -> p (o c) u e", c=NC, p=NP, u=2, e=2)
         )
-        load_pair(1)
-        for r in range(NR):
+        nc.sync.dma_start(out=mb[0][:, 1, :], in_=mask_v[0][:, 1, :])
+        for h in range(2):
+            load_pair(1 + h)
+            if h == 0:
+                for r in range(2):
+                    nc.sync.dma_start(out=scn[r][:], in_=scn_v[r])
+        for r in range(2, NR):
             nc.sync.dma_start(out=scn[r][:], in_=scn_v[r])
-        for j in range(2, 5):
+        for j in range(3, 5):
             load_pair(j)
         nc.sync.dma_start(out=darks[:], in_=dark.rearrange("(g p t) -> p g t", g=NG, p=NP, t=4))
         nc.sync.dma_start(out=sig[0][:], in_=sig_v[0])
@@ -90,7 +94,7 @@ def tile_coded_aperture_backprojection_s13_kernel(
             nc.sync.dma_start(out=gw[g - 1][:].bitcast(I32), in_=dec_words[g - 1].bitcast(I32))
         nc.sync.dma_start(out=gw[NG - 1][:].bitcast(I32), in_=dec_words[NG - 1].bitcast(I32))
 
-        wide, tbank, qin, planes, codes, scales, ybank, zt, zq, img, sbank = ({} for i in range(11))
+        wide, tbank, qin, planes, codes, scales, ybank, zt, zq, img, sbank, first = ({} for i in range(12))
 
         def widen(j, t, c0, c1, engine):
             for c in range(c0 // 512, c1 // 512):
@@ -149,6 +153,19 @@ def tile_coded_aperture_backprojection_s13_kernel(
                 out=quant_input(j)[:, c].rearrange("p x (u e) -> p x u e", u=2),
                 in0=mscale[:, c : c + 1].to_broadcast([NP, 256, 2, 2]),
                 in1=tbank[j, c][:].bitcast(BF16).rearrange("p u (x e) -> p x u e", e=2),
+                op=ALU.mult,
+            )
+
+        def turn_first(t, c):
+            first[t, c] = psum.tile([NP, 2, NP], F32, name=f"first{t}_{c}", tag=("y", "t")[t] + str(c))
+            for u in range(2):
+                nc.tensor.transpose(first[t, c][:, u, :], wide[0, t, c][:].bitcast(F32)[:, u:256:2], ident[:])
+
+        def product_first(t, c):
+            nc.vector.tensor_tensor(
+                out=quant_input(0)[:, c, NP * t : NP * (t + 1)].rearrange("p x (u e) -> p x u e", u=2),
+                in0=mscale[:, c : c + 1].to_broadcast([NP, NP, 2, 2]),
+                in1=first[t, c][:].bitcast(BF16).rearrange("p u (x e) -> p x u e", e=2),
                 op=ALU.mult,
             )
 
@@ -275,18 +292,24 @@ def tile_coded_aperture_backprojection_s13_kernel(
 
         widen(0, 0, 0, 512, "v")
         widen(0, 0, 512, P, "s")
-        widen(0, 1, 0, 512, "v")
+        widen(0, 1, 0, 512, "g")
+        turn_first(0, 0)
+        turn_first(0, 1)
         widen(0, 1, 512, P, "v")
-        widen(1, 0, 0, P, "s")
-        widen(1, 1, 0, P, "g")
-        widen(2, 1, 0, P, "g")
-        turn_mask(0, 0)
-        turn_mask(0, 1)
-        turn_scenes(0, 0)
-        empty_scenes(0, 0)
+        turn_first(1, 1)
+        turn_first(1, 0)
+        for c in range(NC):
+            widen(1, 0, 512 * c, 512 * (c + 1), "s")
+            widen(1, 1, 512 * c, 512 * (c + 1), "g")
         widen(2, 0, 0, P, "s")
+        widen(2, 1, 0, P, "g")
+        widen(3, 1, 0, 512, "g")
+        for t, c in ((0, 0), (0, 1), (1, 1), (1, 0)):
+            product_first(t, c)
         turn_mask(1, 0, "y0")
+        turn_scenes(0, 0)
         turn_mask(1, 1, "y1")
+        empty_scenes(0, 0)
         turn_scenes(1, 0)
         turn_scenes(0, 1)
         turn_scenes(1, 1)
@@ -296,9 +319,8 @@ def tile_coded_aperture_backprojection_s13_kernel(
         widen(3, 0, 512, P, "s")
         widen(3, 1, 512, P, "s")
         widen(3, 0, 0, 512, "s")
-        for j in range(2):
-            for c in range(NC):
-                product(j, c)
+        for c in range(NC):
+            product(1, c)
         turn_mask(2, 0)
         turn_mask(2, 1)
         quant_mask(0)
@@ -306,8 +328,7 @@ def tile_coded_aperture_backprojection_s13_kernel(
         quant_mask(1)
         quant_scenes(1)
         widen_pair(4)
-        widen(3, 1, 0, 512, "g")
-        widen(5, 0, 512, P, "g")
+        widen(5, 0, 0, P, "g")
         turn_mask(3, 1, "m0")
         project_pair(0)
         project_pair(1, ("m2", "m3"))
@@ -323,18 +344,18 @@ def tile_coded_aperture_backprojection_s13_kernel(
         weave_planes(4, 1)
         quant_mask(2)
         widen(5, 1, 0, P, "g")
-        widen(5, 0, 0, 512, "g")
+        widen(6, 1, 512, P, "g")
         project_pair(2)
         product(3, 0)
-        turn_mask(5, 1)
         turn_mask(4, 0)
+        turn_mask(5, 1)
         product_planes(5, 1)
         weave_z(0, 256, B)
         weave_planes(5, 1)
         whiten_pair(2)
         quant_mask(3)
         widen(6, 0, 0, P, "g")
-        widen(6, 1, 512, P, "g")
+        widen(6, 1, 0, 512, "g")
         project_pair(3)
         product(4, 0)
         turn_mask(5, 0)
@@ -345,7 +366,6 @@ def tile_coded_aperture_backprojection_s13_kernel(
         weave_planes(6, 1)
         quant_mask(4)
         quant_z(0)
-        widen(6, 1, 0, 512, "g")
         widen(7, 0, 512, P, "g")
         widen(7, 1, 512, P, "g")
         project_pair(4)
@@ -401,8 +421,11 @@ def tile_coded_aperture_backprojection_s13_kernel(
                     backproject(m, g)
             backproject(m, last)
             res = work.tile([NP, B], F32, name=f"res{m}", tag="res", bufs=NM)
-            if m % 2 == 0:
-                nc.vector.tensor_copy(out=res[:], in_=img[m][:])
-            else:
-                nc.scalar.copy(out=res[:], in_=img[m][:])
-            nc.sync.dma_start(out=out_v[m], in_=res[:])
+            pieces = 2 if m in (0, NM - 1) else 1
+            for h in range(pieces):
+                cols = slice(B // pieces * h, B // pieces * (h + 1))
+                if m % 2 == 0:
+                    nc.vector.tensor_copy(out=res[:, cols], in_=img[m][:, cols])
+                else:
+                    nc.scalar.copy(out=res[:, cols], in_=img[m][:, cols])
+                nc.sync.dma_start(out=out_v[m][:, cols], in_=res[:, cols])

@@ -23,9 +23,8 @@ NPAIR = 2 * NG
 NC = P // 512
 NM = P // 128
 NR = B // 128
-HELD = 4
-HALVED = [(0, 0), (0, 1), (1, 0), (1, 1), (3, 0), (3, 1), (6, 1), (7, 0), (7, 1)]
-WIDE_TAG = {(4, 0, 0): "sq1", (5, 1, 0): "q2", (6, 0, 0): "q3", (7, 0, 1): "z0", (7, 0, 0): "q5"}
+QIN_TAG = {}
+ZQ_TAG = {(0, 1): "q3", (1, 0): "z01", (1, 1): "q5", (2, 0): "z11"}
 
 
 def tile_coded_aperture_backprojection_s13_kernel(
@@ -96,17 +95,11 @@ def tile_coded_aperture_backprojection_s13_kernel(
 
         wide, tbank, qin, planes, codes, scales, ybank, zt, zq, img, sbank, first = ({} for i in range(12))
 
-        def widen(j, t, c0, c1, engine):
+        def widen(j, t, c0, c1, engine, tag=None):
+            piece = keep.tile([NP, c1 - c0], BF16, name=f"wide{j}{t}{c0 // 512}", tag=tag or f"wide{j}{t}{c0 // 512}", align_bytes=64)
             for c in range(c0 // 512, c1 // 512):
-                if (j, t, c) not in wide and (j, t) in HALVED:
-                    wide[j, t, c] = keep.tile([NP, 512], BF16, name=f"wide{j}{t}{c}", tag=WIDE_TAG.get((j, t, c), f"wide{j}{t}{c}"), align_bytes=64)
-            if (j, t) not in HALVED:
-                whole = keep.tile([NP, P], BF16, name=f"wide{j}{t}", tag=WIDE_TAG.get((j, t, 0), f"wide{j}{t}"), align_bytes=64)
-                wide[j, t, 0] = whole[:, 0:512]
-                wide[j, t, 1] = whole[:, 512:P]
-                dst = whole[:]
-            else:
-                dst = wide[j, t, c0 // 512][:]
+                wide[j, t, c] = piece[:, 512 * c - c0 : 512 * (c + 1) - c0]
+            dst = piece[:]
             src = mb[j][:, t, c0:c1].bitcast(FP8)
             if engine == "v":
                 nc.vector.tensor_copy(out=dst, in_=src)
@@ -124,7 +117,7 @@ def tile_coded_aperture_backprojection_s13_kernel(
 
         def turn_mask(j, c, tag=None):
             tbank[j, c] = psum.tile([NP, 2, 256], F32, name=f"tb{j}_{c}", tag=tag or f"t{c}")
-            turn(tbank[j, c], [wide[j, t, c][:].bitcast(F32) for t in range(2)])
+            turn(tbank[j, c], [wide[j, t, c].bitcast(F32) for t in range(2)])
 
         def turn_scenes(h, c):
             sbank[h, c] = psum.tile([NP, 2, 256], F32, name=f"sb{h}_{c}", tag=f"m{2 * h + c}")
@@ -145,7 +138,7 @@ def tile_coded_aperture_backprojection_s13_kernel(
 
         def quant_input(j):
             if j not in qin:
-                qin[j] = keep.tile([NP, NC, 256, 4], BF16, name=f"qin{j}", tag=f"q{j}", align_bytes=64)
+                qin[j] = keep.tile([NP, NC, 256, 4], BF16, name=f"qin{j}", tag=QIN_TAG.get(j, f"q{j}"), align_bytes=64)
             return qin[j]
 
         def product(j, c):
@@ -159,7 +152,7 @@ def tile_coded_aperture_backprojection_s13_kernel(
         def turn_first(t, c):
             first[t, c] = psum.tile([NP, 2, NP], F32, name=f"first{t}_{c}", tag=("y", "t")[t] + str(c))
             for u in range(2):
-                nc.tensor.transpose(first[t, c][:, u, :], wide[0, t, c][:].bitcast(F32)[:, u:256:2], ident[:])
+                nc.tensor.transpose(first[t, c][:, u, :], wide[0, t, c].bitcast(F32)[:, u:256:2], ident[:])
 
         def product_first(t, c):
             nc.vector.tensor_tensor(
@@ -170,7 +163,7 @@ def tile_coded_aperture_backprojection_s13_kernel(
             )
 
         def product_planes(j, c):
-            planes[j, c] = work.tile([NP, 4, 256], BF16, name=f"planes{j}_{c}", tag="planes", bufs=2, align_bytes=64)
+            planes[j, c] = work.tile([NP, 4, 256], BF16, name=f"planes{j}_{c}", tag="planes", bufs=3, align_bytes=64)
             src = tbank[j, c][:].bitcast(BF16).rearrange("p u (x e) -> p u e x", e=2)
             for u in range(2):
                 for e in range(2):
@@ -191,8 +184,8 @@ def tile_coded_aperture_backprojection_s13_kernel(
             else:
                 nc.scalar.copy(out=dst, in_=src)
 
-        def weave_planes(j, c):
-            weave(quant_input(j)[:, c], planes[j, c][:], "s")
+        def weave_planes(j, c, x0=0, x1=256, engine="s"):
+            weave(quant_input(j)[:, c, x0:x1], planes[j, c][:, :, x0:x1], engine)
 
         def quant_mask(j):
             codes[j] = work.tile([NP, NC, 256], U32, name=f"codes{j}", tag="codes", bufs=4, align_bytes=64)
@@ -233,26 +226,26 @@ def tile_coded_aperture_backprojection_s13_kernel(
 
         def weave_z(g, b0, b1, engine="s"):
             h = b0 // 256
-            if (g, h) not in zq and g == 2:
-                half = keep.tile([NP, 256, 4], BF16, name=f"zq{g}{h}", tag=("z2", "q6")[h], align_bytes=64)
-                zq[g, h] = half[:]
-            elif (g, h) not in zq:
-                zq[g] = keep.tile([NP, B, 4], BF16, name=f"zq{g}", tag=f"z{g}", align_bytes=64)
-                zq[g, 0] = zq[g][:, 0:256, :]
-                zq[g, 1] = zq[g][:, 256:B, :]
+            if (g, h) not in zq:
+                zq[g, h] = keep.tile([NP, 256, 4], BF16, name=f"zq{g}{h}", tag=ZQ_TAG.get((g, h), f"z{g}{h}"), align_bytes=64)
             weave(zq[g, h][:, b0 - 256 * h : b1 - 256 * h, :], zt[g][:, :, b0:b1], engine)
 
         def quant_z(g, b0=0, b1=B):
-            nc.vector.quantize_mx(
-                out=zcodes[g][:, b0:b1].bitcast(E4M3X4),
-                scales=zscales[g][:, b0:b1],
-                in_=(zq[g][:] if b1 - b0 == B else zq[g, b0 // 256]).rearrange("p b t -> p (b t)"),
-            )
+            for h in range(b0 // 256, b1 // 256):
+                cols = slice(256 * h, 256 * (h + 1))
+                nc.vector.quantize_mx(
+                    out=zcodes[g][:, cols].bitcast(E4M3X4),
+                    scales=zscales[g][:, cols],
+                    in_=zq[g, h][:].rearrange("p b t -> p (b t)"),
+                )
 
         img_tag = ["m0", "m1", "m2", "m3", "t0", "t1", "y0", "y1"]
         last = NG - 1
 
+        done = [0] * NM
+
         def backproject(m, g):
+            done[m] = g + 1
             if g == 0:
                 img[m] = psum.tile([NP, B], F32, name=f"img{m}", tag=img_tag[m])
             nc.tensor.matmul_mx(
@@ -265,15 +258,6 @@ def tile_coded_aperture_backprojection_s13_kernel(
                 stop=(g == last),
             )
 
-        def widen_pair(j, engine="g"):
-            for t in range(2):
-                widen(j, t, 0, P, engine)
-
-        def whiten_and_project(j):
-            for t in range(2):
-                whiten(j, t)
-                project(j + 1, t)
-
         def whiten_pair(j):
             whiten(j, 0)
             whiten(j, 1)
@@ -282,29 +266,20 @@ def tile_coded_aperture_backprojection_s13_kernel(
             project(j, 0, tags[0])
             project(j, 1, tags[1])
 
-        def scale_on_scalar(j):
-            product_planes(j, 1)
-            weave_planes(j, 1)
-
-        def weave_group(g):
-            weave_z(g, 0, 256)
-            weave_z(g, 256, B)
-
         widen(0, 0, 0, 512, "v")
         widen(0, 0, 512, P, "s")
-        widen(0, 1, 0, 512, "g")
         turn_first(0, 0)
         turn_first(0, 1)
+        widen(0, 1, 0, 512, "s")
         widen(0, 1, 512, P, "v")
-        turn_first(1, 1)
         turn_first(1, 0)
-        for c in range(NC):
-            widen(1, 0, 512 * c, 512 * (c + 1), "s")
-            widen(1, 1, 512 * c, 512 * (c + 1), "g")
+        turn_first(1, 1)
+        widen(1, 0, 0, P, "s")
+        widen(1, 1, 0, P, "s")
         widen(2, 0, 0, P, "s")
         widen(2, 1, 0, P, "g")
         widen(3, 1, 0, 512, "g")
-        for t, c in ((0, 0), (0, 1), (1, 1), (1, 0)):
+        for t, c in ((0, 0), (0, 1), (1, 0), (1, 1)):
             product_first(t, c)
         turn_mask(1, 0, "y0")
         turn_scenes(0, 0)
@@ -314,112 +289,114 @@ def tile_coded_aperture_backprojection_s13_kernel(
         turn_scenes(0, 1)
         turn_scenes(1, 1)
         empty_scenes(1, 0)
+        widen(3, 0, 0, P, "s")
         empty_scenes(0, 1)
         empty_scenes(1, 1)
-        widen(3, 0, 512, P, "s")
         widen(3, 1, 512, P, "s")
-        widen(3, 0, 0, 512, "s")
         for c in range(NC):
             product(1, c)
-        turn_mask(2, 0)
         turn_mask(2, 1)
+        turn_mask(2, 0)
         quant_mask(0)
         quant_scenes(0)
         quant_mask(1)
         quant_scenes(1)
-        widen_pair(4)
-        widen(5, 0, 0, P, "g")
+        widen(4, 0, 0, P, "g", "sq1")
+        widen(4, 1, 0, P, "g")
         turn_mask(3, 1, "m0")
         project_pair(0)
         project_pair(1, ("m2", "m3"))
-        scale_on_scalar(3)
+        product_planes(2, 1)
+        product_planes(3, 1)
+        weave_planes(2, 1)
         product(2, 0)
-        product(2, 1)
-        turn_mask(4, 1)
         turn_mask(3, 0)
+        turn_mask(4, 1)
+        widen(5, 0, 0, P, "s")
+        widen(5, 1, 0, P, "s")
+        weave_planes(3, 1)
         product_planes(4, 1)
         whiten_pair(0)
         whiten_pair(1)
-        weave_z(0, 0, 256)
-        weave_planes(4, 1)
         quant_mask(2)
-        widen(5, 1, 0, P, "g")
-        widen(6, 1, 512, P, "g")
+        weave_z(0, 0, 256, "g")
         project_pair(2)
         product(3, 0)
         turn_mask(4, 0)
-        turn_mask(5, 1)
+        turn_mask(5, 1, "m1")
+        widen(6, 0, 0, P, "s")
+        widen(6, 1, 0, P, "s")
+        weave_planes(4, 1)
         product_planes(5, 1)
-        weave_z(0, 256, B)
-        weave_planes(5, 1)
         whiten_pair(2)
         quant_mask(3)
-        widen(6, 0, 0, P, "g")
-        widen(6, 1, 0, 512, "g")
+        weave_z(0, 256, B, "g")
         project_pair(3)
         product(4, 0)
         turn_mask(5, 0)
         turn_mask(6, 1)
+        widen(7, 0, 512, P, "s")
+        widen(7, 1, 512, P, "s")
+        weave_planes(5, 1)
         product_planes(6, 1)
         whiten_pair(3)
-        weave_z(1, 0, 256)
-        weave_planes(6, 1)
         quant_mask(4)
         quant_z(0)
-        widen(7, 0, 512, P, "g")
-        widen(7, 1, 512, P, "g")
+        weave_z(1, 0, 256, "g")
         project_pair(4)
-        product(5, 0)
         backproject(0, 0)
         backproject(1, 0)
+        product(5, 0)
         turn_mask(6, 0)
-        turn_mask(7, 1)
+        turn_mask(7, 1, "m3")
+        widen(7, 0, 0, 512, "s")
+        widen(7, 1, 0, 512, "s")
+        weave_planes(6, 1)
         product_planes(7, 1)
-        weave_planes(7, 1)
-        weave_z(1, 256, B)
         whiten_pair(4)
         quant_mask(5)
-        widen(7, 0, 0, 512, "g")
-        widen(7, 1, 0, 512, "g")
+        weave_z(1, 256, B, "g")
         project_pair(5)
-        product(6, 0)
         backproject(2, 0)
-        turn_mask(7, 0)
-        backproject(3, 0)
         backproject(5, 0)
+        product(6, 0)
+        turn_mask(7, 0)
+        weave_planes(7, 1)
         whiten_pair(5)
-        weave_z(2, 0, 256)
+        weave_z(2, 256, B, "s")
         quant_mask(6)
-        weave_z(2, 256, B, "g")
+        quant_z(1)
+        weave_z(2, 0, 256, "g")
         project_pair(6)
+        backproject(3, 0)
+        for m in (0, 1, 2, 3, 5):
+            backproject(m, 1)
         product(7, 0)
-        backproject(4, 0)
         whiten(6, 0)
         quant_mask(7)
         project(7, 0)
         whiten(6, 1)
         project(7, 1)
-        quant_z(1)
+        quant_z(2)
+        backproject(4, 0)
+        backproject(4, 1)
         for m in range(6):
-            backproject(m, 1)
+            backproject(m, 2)
         whiten(7, 0, 0, 256)
         whiten(7, 1, 0, 256)
-        weave_z(last, 0, 256)
+        weave_z(last, 0, 160)
         whiten(7, 0, 256, B)
         whiten(7, 1, 256, B)
-        quant_z(2, 0, 256)
-        quant_z(2, 256, B)
-        for m in range(4):
-            backproject(m, 2)
-        weave_z(last, 256, 320)
-        weave_z(last, 320, B, "v")
+        for g in range(3):
+            backproject(6, g)
+        weave_z(last, 160, 256, "v")
+        weave_z(last, 256, 416, "v")
+        weave_z(last, 416, B, "s")
         quant_z(last, 0, 256)
         quant_z(last, 256, B)
         for m in range(NM):
-            if m >= 4:
-                for g in range(2 if m < 6 else 0, last):
-                    backproject(m, g)
-            backproject(m, last)
+            for g in range(done[m], NG):
+                backproject(m, g)
             res = work.tile([NP, B], F32, name=f"res{m}", tag="res", bufs=NM)
             pieces = 2 if m in (0, NM - 1) else 1
             for h in range(pieces):

@@ -95,6 +95,15 @@ def tile_coded_aperture_backprojection_s13_kernel(
 
         wide, tbank, qin, planes, codes, scales, ybank, zt, zq, img, sbank, first = ({} for i in range(12))
 
+        warm_src = ident[:].bitcast(BF16)
+
+        def warm(count, tag):
+            bank = psum.tile([NP, 2, 256], F32, name=f"warm_{tag}", tag=tag)
+            for i in range(count):
+                nc.tensor.matmul(
+                    bank[:], warm_src[:, 0:NP], warm_src.unsqueeze(1).to_broadcast([NP, 2, 256]), start=True, stop=True
+                )
+
         def widen(j, t, c0, c1, engine, tag=None):
             piece = keep.tile([NP, c1 - c0], BF16, name=f"wide{j}{t}{c0 // 512}", tag=tag or f"wide{j}{t}{c0 // 512}", align_bytes=64)
             for c in range(c0 // 512, c1 // 512):
@@ -268,6 +277,7 @@ def tile_coded_aperture_backprojection_s13_kernel(
 
         widen(0, 0, 0, 512, "v")
         widen(0, 0, 512, P, "s")
+        warm(6, "m3")
         turn_first(0, 0)
         turn_first(0, 1)
         widen(0, 1, 0, 512, "s")
@@ -281,10 +291,12 @@ def tile_coded_aperture_backprojection_s13_kernel(
         widen(3, 1, 0, 512, "g")
         for t, c in ((0, 0), (0, 1), (1, 0), (1, 1)):
             product_first(t, c)
+        warm(2, "m2")
         turn_mask(1, 0, "y0")
         turn_scenes(0, 0)
         turn_mask(1, 1, "y1")
         empty_scenes(0, 0)
+        warm(2, "m1")
         turn_scenes(1, 0)
         turn_scenes(0, 1)
         turn_scenes(1, 1)
@@ -295,6 +307,7 @@ def tile_coded_aperture_backprojection_s13_kernel(
         widen(3, 1, 512, P, "s")
         for c in range(NC):
             product(1, c)
+        warm(2, "t1")
         turn_mask(2, 1)
         turn_mask(2, 0)
         quant_mask(0)

@@ -23,8 +23,9 @@ NPAIR = 2 * NG
 NC = P // 512
 NM = P // 128
 NR = B // 128
+CUT = 224
 QIN_TAG = {}
-ZQ_TAG = {(0, 1): "q3", (1, 0): "z01", (1, 1): "q5", (2, 0): "z11"}
+ZQ_TAG = {(0, 1): "q3", (1, 1): "q5"}
 
 
 def tile_coded_aperture_backprojection_s13_kernel(
@@ -38,7 +39,7 @@ def tile_coded_aperture_backprojection_s13_kernel(
 
         mask_v = mask_bytes.rearrange("(g p t) k -> g p t k", g=NG, p=NP, t=4)
         sig_v = inv_sigma.rearrange("(g p t) b -> g p t b", g=NG, p=NP, t=4)
-        scn_v = scenes.rearrange("(r p) k -> r p k", p=NP)
+        scn_v = scenes.rearrange("(h t p) (c k) -> h c p t k", h=2, t=2, p=NP, c=NC)
         out_v = out.rearrange("(m p) b -> m p b", p=NP)
 
         mscale = keep.tile([NP, NC, 2, 2], F32, name="mscale")
@@ -47,7 +48,7 @@ def tile_coded_aperture_backprojection_s13_kernel(
         gsc = keep.tile([NP, NG, P], U8, name="gsc", align_bytes=64)
         mb = [keep.tile([NP, 2, P], U8, name=f"mb{j}", align_bytes=64) for j in range(NPAIR)]
         sig = [keep.tile([NP, 4, B], BF16, name=f"sig{g}", align_bytes=64) for g in range(NG)]
-        scn = [keep.tile([NP, P], BF16, name=f"scn{r}", align_bytes=64) for r in range(NR)]
+        scn = {(h, c): keep.tile([NP, 2, 512], BF16, name=f"scn{h}{c}", align_bytes=64) for h in range(2) for c in range(NC)}
         gw = [keep.tile([NP, 2 * P], U8, name=f"gw{g}", align_bytes=64) for g in range(NG)]
         sq = [keep.tile([NP, B, 4], BF16, name=f"sq{c}", align_bytes=64) for c in range(NC)]
         scodes = keep.tile([NP, NC, B], U32, name="scodes", align_bytes=64)
@@ -55,6 +56,8 @@ def tile_coded_aperture_backprojection_s13_kernel(
         zcodes = [keep.tile([NP, B], U32, name=f"zcodes{g}", align_bytes=64) for g in range(NG)]
         zscales = [keep.tile([NP, B], U8, name=f"zscales{g}", align_bytes=64) for g in range(NG)]
 
+        warm_src = keep.tile([NP, 512], BF16, name="warm_src", align_bytes=64)
+        nc.vector.memset(warm_src[:], 0.0)
         make_identity(nc, ident[:])
         nc.vector.memset(gsc[:].bitcast(I32), 0)
 
@@ -67,15 +70,12 @@ def tile_coded_aperture_backprojection_s13_kernel(
             out=mscale[:], in_=mask_scale.rearrange("o (c p u e) -> p (o c) u e", c=NC, p=NP, u=2, e=2)
         )
         nc.sync.dma_start(out=mb[0][:, 1, :], in_=mask_v[0][:, 1, :])
-        for h in range(2):
-            load_pair(1 + h)
-            if h == 0:
-                for r in range(2):
-                    nc.sync.dma_start(out=scn[r][:], in_=scn_v[r])
-        for r in range(2, NR):
-            nc.sync.dma_start(out=scn[r][:], in_=scn_v[r])
-        for j in range(3, 5):
-            load_pair(j)
+        load_pair(1)
+        load_pair(2)
+        for c in range(NC):
+            for h in range(2):
+                nc.sync.dma_start(out=scn[h, c][:], in_=scn_v[h, c])
+            load_pair(3 + c)
         nc.sync.dma_start(out=darks[:], in_=dark.rearrange("(g p t) -> p g t", g=NG, p=NP, t=4))
         nc.sync.dma_start(out=sig[0][:], in_=sig_v[0])
         load_pair(5)
@@ -95,14 +95,10 @@ def tile_coded_aperture_backprojection_s13_kernel(
 
         wide, tbank, qin, planes, codes, scales, ybank, zt, zq, img, sbank, first = ({} for i in range(12))
 
-        warm_src = ident[:].bitcast(BF16)
-
         def warm(count, tag):
-            bank = psum.tile([NP, 2, 256], F32, name=f"warm_{tag}", tag=tag)
+            bank = psum.tile([NP, 512], F32, name=f"warm_{tag}", tag=tag)
             for i in range(count):
-                nc.tensor.matmul(
-                    bank[:], warm_src[:, 0:NP], warm_src.unsqueeze(1).to_broadcast([NP, 2, 256]), start=True, stop=True
-                )
+                nc.tensor.matmul(bank[:], warm_src[:, 0:NP], warm_src[:], start=True, stop=True)
 
         def widen(j, t, c0, c1, engine, tag=None):
             piece = keep.tile([NP, c1 - c0], BF16, name=f"wide{j}{t}{c0 // 512}", tag=tag or f"wide{j}{t}{c0 // 512}", align_bytes=64)
@@ -130,7 +126,7 @@ def tile_coded_aperture_backprojection_s13_kernel(
 
         def turn_scenes(h, c):
             sbank[h, c] = psum.tile([NP, 2, 256], F32, name=f"sb{h}_{c}", tag=f"m{2 * h + c}")
-            turn(sbank[h, c], [scn[2 * h + t][:, 512 * c : 512 * (c + 1)].bitcast(F32) for t in range(2)])
+            turn(sbank[h, c], [scn[h, c][:, t, :].bitcast(F32) for t in range(2)])
 
         def empty_scenes(h, c):
             dst = sq[c][:, 256 * h : 256 * (h + 1), :].rearrange("p x t -> p (x t)").bitcast(F32)
@@ -205,10 +201,11 @@ def tile_coded_aperture_backprojection_s13_kernel(
                 in_=qin[j][:].rearrange("p c x t -> p (c x t)"),
             )
 
-        def project(j, t, tag=None):
-            ybank[j, t] = psum.tile([NP, B], F32, name=f"y{j}_{t}", tag=tag or f"y{t}")
+        def project(j, t, tag=None, passes=range(NC)):
+            if (j, t) not in ybank:
+                ybank[j, t] = psum.tile([NP, B], F32, name=f"y{j}_{t}", tag=tag or f"y{t}")
             cols = slice(128 * t, 128 * t + 128)
-            for c in range(NC):
+            for c in passes:
                 nc.tensor.matmul_mx(
                     out=ybank[j, t][:],
                     lhsT=codes[j][:, c, cols].bitcast(E4M3X4),
@@ -275,9 +272,9 @@ def tile_coded_aperture_backprojection_s13_kernel(
             project(j, 0, tags[0])
             project(j, 1, tags[1])
 
+        warm(5, "m3")
         widen(0, 0, 0, 512, "v")
         widen(0, 0, 512, P, "s")
-        warm(6, "m3")
         turn_first(0, 0)
         turn_first(0, 1)
         widen(0, 1, 0, 512, "s")
@@ -291,120 +288,139 @@ def tile_coded_aperture_backprojection_s13_kernel(
         widen(3, 1, 0, 512, "g")
         for t, c in ((0, 0), (0, 1), (1, 0), (1, 1)):
             product_first(t, c)
-        warm(2, "m2")
-        turn_mask(1, 0, "y0")
+        warm(2, "m3")
+        turn_mask(1, 0, "m3")
         turn_scenes(0, 0)
-        turn_mask(1, 1, "y1")
-        empty_scenes(0, 0)
-        warm(2, "m1")
         turn_scenes(1, 0)
+        turn_mask(1, 1, "t0")
+        widen(3, 0, 0, 512, "s")
+        empty_scenes(0, 0)
+        empty_scenes(1, 0)
+        warm(2, "t1")
+        product(1, 0)
         turn_scenes(0, 1)
         turn_scenes(1, 1)
-        empty_scenes(1, 0)
-        widen(3, 0, 0, P, "s")
+        quant_mask(0)
+        widen(3, 1, 512, P, "g", "q0")
+        widen(3, 0, 512, P, "s")
+        widen(4, 0, 0, P, "s")
         empty_scenes(0, 1)
         empty_scenes(1, 1)
-        widen(3, 1, 512, P, "s")
-        for c in range(NC):
-            product(1, c)
-        warm(2, "t1")
+        product(1, 1)
         turn_mask(2, 1)
         turn_mask(2, 0)
-        quant_mask(0)
         quant_scenes(0)
         quant_mask(1)
         quant_scenes(1)
-        widen(4, 0, 0, P, "g", "sq1")
-        widen(4, 1, 0, P, "g")
-        turn_mask(3, 1, "m0")
-        project_pair(0)
-        project_pair(1, ("m2", "m3"))
+        widen(4, 1, 0, P, "g", "sq1")
+        widen(5, 0, 0, P, "g")
+        project(0, 0, passes=[0])
+        project(0, 1, passes=[0])
+        project(0, 0, passes=[1])
+        project(0, 1, passes=[1])
         product_planes(2, 1)
-        product_planes(3, 1)
+        widen(5, 1, 0, P, "s")
         weave_planes(2, 1)
         product(2, 0)
+        project(1, 0, "m2")
+        turn_mask(3, 1, "m0")
+        project(1, 1, "m3")
         turn_mask(3, 0)
-        turn_mask(4, 1)
-        widen(5, 0, 0, P, "s")
-        widen(5, 1, 0, P, "s")
-        weave_planes(3, 1)
-        product_planes(4, 1)
-        whiten_pair(0)
-        whiten_pair(1)
-        quant_mask(2)
-        weave_z(0, 0, 256, "g")
-        project_pair(2)
-        product(3, 0)
-        turn_mask(4, 0)
-        turn_mask(5, 1, "m1")
+        product_planes(3, 1)
         widen(6, 0, 0, P, "s")
-        widen(6, 1, 0, P, "s")
-        weave_planes(4, 1)
-        product_planes(5, 1)
-        whiten_pair(2)
+        weave_planes(3, 1)
+        whiten_pair(0)
+        whiten(1, 0)
+        quant_mask(2)
+        project(2, 0)
+        turn_mask(4, 1)
+        product_planes(4, 1)
+        whiten(1, 1)
+        weave_z(0, 0, CUT, "g")
+        weave_z(0, CUT, 256, "s")
+        product(3, 0)
+        project(2, 1)
+        turn_mask(4, 0)
+        whiten(2, 0)
         quant_mask(3)
         weave_z(0, 256, B, "g")
-        project_pair(3)
+        project(3, 0)
+        turn_mask(5, 1, "m1")
+        weave_planes(4, 1)
+        widen(6, 1, 0, P, "s")
+        product_planes(5, 1)
+        whiten(2, 1)
         product(4, 0)
+        project(3, 1)
         turn_mask(5, 0)
-        turn_mask(6, 1)
-        widen(7, 0, 512, P, "s")
-        widen(7, 1, 512, P, "s")
-        weave_planes(5, 1)
-        product_planes(6, 1)
-        whiten_pair(3)
+        whiten(3, 0)
         quant_mask(4)
         quant_z(0)
-        weave_z(1, 0, 256, "g")
-        project_pair(4)
-        backproject(0, 0)
-        backproject(1, 0)
+        project(4, 0)
+        turn_mask(6, 1)
+        widen(7, 0, 512, P, "s")
+        weave_planes(5, 1)
+        widen(7, 1, 512, P, "s")
+        product_planes(6, 1)
+        whiten(3, 1)
+        weave_z(1, 0, CUT, "g")
+        weave_z(1, CUT, 256, "s")
         product(5, 0)
+        project(4, 1)
+        backproject(0, 0)
         turn_mask(6, 0)
+        whiten(4, 0)
+        quant_mask(5)
+        weave_z(1, 256, B, "g")
+        project(5, 0)
+        backproject(1, 0)
         turn_mask(7, 1, "m3")
         widen(7, 0, 0, 512, "s")
         widen(7, 1, 0, 512, "s")
         weave_planes(6, 1)
         product_planes(7, 1)
-        whiten_pair(4)
-        quant_mask(5)
-        weave_z(1, 256, B, "g")
-        project_pair(5)
-        backproject(2, 0)
-        backproject(5, 0)
+        whiten(4, 1)
         product(6, 0)
+        project(5, 1)
+        backproject(2, 0)
         turn_mask(7, 0)
-        weave_planes(7, 1)
-        whiten_pair(5)
-        weave_z(2, 256, B, "s")
+        whiten(5, 0)
         quant_mask(6)
         quant_z(1)
-        weave_z(2, 0, 256, "g")
-        project_pair(6)
-        backproject(3, 0)
-        for m in (0, 1, 2, 3, 5):
+        project(6, 0)
+        weave_planes(7, 1)
+        backproject(5, 0)
+        for m in (0, 1, 2, 5):
             backproject(m, 1)
+        whiten(5, 1)
+        weave_z(2, 0, CUT, "g")
+        weave_z(2, CUT, 256, "s")
         product(7, 0)
+        project(6, 1)
+        backproject(3, 0)
+        backproject(3, 1)
         whiten(6, 0)
         quant_mask(7)
+        weave_z(2, 256, B, "s")
         project(7, 0)
         whiten(6, 1)
         project(7, 1)
-        quant_z(2)
         backproject(4, 0)
         backproject(4, 1)
-        for m in range(6):
+        quant_z(2)
+        for m in range(4):
             backproject(m, 2)
         whiten(7, 0, 0, 256)
         whiten(7, 1, 0, 256)
         weave_z(last, 0, 160)
         whiten(7, 0, 256, B)
         whiten(7, 1, 256, B)
-        for g in range(3):
-            backproject(6, g)
         weave_z(last, 160, 256, "v")
         weave_z(last, 256, 416, "v")
         weave_z(last, 416, B, "s")
+        backproject(4, 2)
+        backproject(5, 2)
+        backproject(6, 0)
         quant_z(last, 0, 256)
         quant_z(last, 256, B)
         for m in range(NM):

@@ -23,7 +23,7 @@ NPAIR = 2 * NG
 NC = P // 512
 NM = P // 128
 NR = B // 128
-CUT = 224
+CUT = 208
 QIN_TAG = {}
 ZQ_TAG = {(0, 1): "q3", (1, 1): "q5"}
 
@@ -272,7 +272,7 @@ def tile_coded_aperture_backprojection_s13_kernel(
             project(j, 0, tags[0])
             project(j, 1, tags[1])
 
-        warm(5, "m3")
+        warm(4, "m3")
         widen(0, 0, 0, 512, "v")
         widen(0, 0, 512, P, "s")
         turn_first(0, 0)
@@ -291,12 +291,12 @@ def tile_coded_aperture_backprojection_s13_kernel(
         warm(2, "m3")
         turn_mask(1, 0, "m3")
         turn_scenes(0, 0)
+        warm(2, "m2")
         turn_scenes(1, 0)
         turn_mask(1, 1, "t0")
         widen(3, 0, 0, 512, "s")
         empty_scenes(0, 0)
         empty_scenes(1, 0)
-        warm(2, "t1")
         product(1, 0)
         turn_scenes(0, 1)
         turn_scenes(1, 1)
@@ -307,37 +307,42 @@ def tile_coded_aperture_backprojection_s13_kernel(
         empty_scenes(0, 1)
         empty_scenes(1, 1)
         product(1, 1)
-        turn_mask(2, 1)
+        warm(2, "t1")
         turn_mask(2, 0)
+        turn_mask(2, 1)
         quant_scenes(0)
         quant_mask(1)
         quant_scenes(1)
         widen(4, 1, 0, P, "g", "sq1")
         widen(5, 0, 0, P, "g")
+        widen(7, 0, 0, P, "g")
         project(0, 0, passes=[0])
         project(0, 1, passes=[0])
         project(0, 0, passes=[1])
         project(0, 1, passes=[1])
-        product_planes(2, 1)
         widen(5, 1, 0, P, "s")
-        weave_planes(2, 1)
-        product(2, 0)
-        project(1, 0, "m2")
+        widen(6, 0, 0, P, "s")
+        widen(6, 1, 0, P, "s")
+        widen(7, 1, 0, P, "s")
         turn_mask(3, 1, "m0")
+        product_planes(3, 1)
+        product(2, 0)
+        product(2, 1)
+        project(1, 0, "m2")
+        turn_mask(4, 1, "m1")
         project(1, 1, "m3")
         turn_mask(3, 0)
-        product_planes(3, 1)
-        widen(6, 0, 0, P, "s")
         weave_planes(3, 1)
+        product_planes(4, 1)
         whiten_pair(0)
         whiten(1, 0)
         quant_mask(2)
         project(2, 0)
-        turn_mask(4, 1)
-        product_planes(4, 1)
+        turn_mask(5, 1)
+        weave_planes(4, 1)
+        product_planes(5, 1)
         whiten(1, 1)
         weave_z(0, 0, CUT, "g")
-        weave_z(0, CUT, 256, "s")
         product(3, 0)
         project(2, 1)
         turn_mask(4, 0)
@@ -345,10 +350,10 @@ def tile_coded_aperture_backprojection_s13_kernel(
         quant_mask(3)
         weave_z(0, 256, B, "g")
         project(3, 0)
-        turn_mask(5, 1, "m1")
-        weave_planes(4, 1)
-        widen(6, 1, 0, P, "s")
-        product_planes(5, 1)
+        turn_mask(6, 1, "m1")
+        weave_z(0, CUT, 256, "s")
+        weave_planes(5, 1)
+        product_planes(6, 1)
         whiten(2, 1)
         product(4, 0)
         project(3, 1)
@@ -357,70 +362,61 @@ def tile_coded_aperture_backprojection_s13_kernel(
         quant_mask(4)
         quant_z(0)
         project(4, 0)
-        turn_mask(6, 1)
-        widen(7, 0, 512, P, "s")
-        weave_planes(5, 1)
-        widen(7, 1, 512, P, "s")
-        product_planes(6, 1)
+        turn_mask(7, 1)
+        weave_planes(6, 1)
+        product_planes(7, 1)
         whiten(3, 1)
         weave_z(1, 0, CUT, "g")
-        weave_z(1, CUT, 256, "s")
         product(5, 0)
         project(4, 1)
-        backproject(0, 0)
         turn_mask(6, 0)
+        turn_mask(7, 0, "m3")
         whiten(4, 0)
         quant_mask(5)
         weave_z(1, 256, B, "g")
         project(5, 0)
-        backproject(1, 0)
-        turn_mask(7, 1, "m3")
-        widen(7, 0, 0, 512, "s")
-        widen(7, 1, 0, 512, "s")
-        weave_planes(6, 1)
-        product_planes(7, 1)
+        for m in (0, 1, 2, 5):
+            backproject(m, 0)
+        product_planes(7, 0)
+        weave_z(1, CUT, 256, "s")
+        weave_planes(7, 1)
         whiten(4, 1)
         product(6, 0)
         project(5, 1)
-        backproject(2, 0)
-        turn_mask(7, 0)
+        backproject(4, 0)
+        weave_planes(7, 0)
         whiten(5, 0)
         quant_mask(6)
         quant_z(1)
         project(6, 0)
-        weave_planes(7, 1)
-        backproject(5, 0)
-        for m in (0, 1, 2, 5):
-            backproject(m, 1)
-        whiten(5, 1)
-        weave_z(2, 0, CUT, "g")
-        weave_z(2, CUT, 256, "s")
-        product(7, 0)
-        project(6, 1)
         backproject(3, 0)
-        backproject(3, 1)
+        backproject(0, 1)
+        whiten(5, 1)
+        weave_z(2, 0, 256, "s")
+        weave_z(2, 256, B, "s")
+        project(6, 1)
         whiten(6, 0)
         quant_mask(7)
-        weave_z(2, 256, B, "s")
+        backproject(1, 1)
+        backproject(2, 1)
         project(7, 0)
         whiten(6, 1)
         project(7, 1)
-        backproject(4, 0)
-        backproject(4, 1)
-        quant_z(2)
-        for m in range(4):
-            backproject(m, 2)
-        whiten(7, 0, 0, 256)
+        quant_z(2, 0, 256)
+        for m in range(3, 6):
+            backproject(m, 1)
+        whiten(7, 0)
         whiten(7, 1, 0, 256)
         weave_z(last, 0, 160)
-        whiten(7, 0, 256, B)
         whiten(7, 1, 256, B)
-        weave_z(last, 160, 256, "v")
-        weave_z(last, 256, 416, "v")
-        weave_z(last, 416, B, "s")
-        backproject(4, 2)
-        backproject(5, 2)
         backproject(6, 0)
+        backproject(6, 1)
+        quant_z(2, 256, B)
+        for m in range(4):
+            backproject(m, 2)
+        weave_z(last, 160, 256, "v")
+        weave_z(last, 256, 448, "v")
+        weave_z(last, 448, B, "s")
         quant_z(last, 0, 256)
         quant_z(last, 256, B)
         for m in range(NM):

@@ -24,8 +24,8 @@ NC = P // 512
 NM = P // 128
 NR = B // 128
 CUT = 208
-QIN_TAG = {}
-ZQ_TAG = {(0, 1): "q3", (1, 1): "q5"}
+QIN_TAG = {7: "q5"}
+ZQ_TAG = {(0, 1): "q3"}
 
 
 def tile_coded_aperture_backprojection_s13_kernel(
@@ -72,16 +72,18 @@ def tile_coded_aperture_backprojection_s13_kernel(
         nc.sync.dma_start(out=mb[0][:, 1, :], in_=mask_v[0][:, 1, :])
         load_pair(1)
         load_pair(2)
-        for c in range(NC):
-            for h in range(2):
-                nc.sync.dma_start(out=scn[h, c][:], in_=scn_v[h, c])
-            load_pair(3 + c)
+        nc.sync.dma_start(out=scn[0, 0][:], in_=scn_v[0, 0])
+        nc.sync.dma_start(out=scn[1, 0][:], in_=scn_v[1, 0])
+        load_pair(3)
+        nc.sync.dma_start(out=scn[0, 1][:], in_=scn_v[0, 1])
+        nc.sync.dma_start(out=scn[1, 1][:], in_=scn_v[1, 1])
+        load_pair(4)
+        load_pair(5)
         nc.sync.dma_start(out=darks[:], in_=dark.rearrange("(g p t) -> p g t", g=NG, p=NP, t=4))
         nc.sync.dma_start(out=sig[0][:], in_=sig_v[0])
-        load_pair(5)
         load_pair(6)
-        nc.sync.dma_start(out=sig[1][:], in_=sig_v[1])
         load_pair(7)
+        nc.sync.dma_start(out=sig[1][:], in_=sig_v[1])
         for q in range(4):
             nc.sync.dma_start(
                 out=gsc[32 * q : 32 * q + 4].bitcast(I32),
@@ -146,11 +148,11 @@ def tile_coded_aperture_backprojection_s13_kernel(
                 qin[j] = keep.tile([NP, NC, 256, 4], BF16, name=f"qin{j}", tag=QIN_TAG.get(j, f"q{j}"), align_bytes=64)
             return qin[j]
 
-        def product(j, c):
+        def product(j, c, x0=0, x1=256):
             nc.vector.tensor_tensor(
-                out=quant_input(j)[:, c].rearrange("p x (u e) -> p x u e", u=2),
-                in0=mscale[:, c : c + 1].to_broadcast([NP, 256, 2, 2]),
-                in1=tbank[j, c][:].bitcast(BF16).rearrange("p u (x e) -> p x u e", e=2),
+                out=quant_input(j)[:, c, x0:x1].rearrange("p x (u e) -> p x u e", u=2),
+                in0=mscale[:, c : c + 1].to_broadcast([NP, x1 - x0, 2, 2]),
+                in1=tbank[j, c][:].bitcast(BF16).rearrange("p u (x e) -> p x u e", e=2)[:, x0:x1],
                 op=ALU.mult,
             )
 
@@ -167,13 +169,13 @@ def tile_coded_aperture_backprojection_s13_kernel(
                 op=ALU.mult,
             )
 
-        def product_planes(j, c):
-            planes[j, c] = work.tile([NP, 4, 256], BF16, name=f"planes{j}_{c}", tag="planes", bufs=3, align_bytes=64)
+        def product_planes(j, c, x0=0, x1=256):
+            planes[j, c] = work.tile([NP, 4, 256], BF16, name=f"planes{j}_{c}", tag="planes", bufs=4, align_bytes=64)
             src = tbank[j, c][:].bitcast(BF16).rearrange("p u (x e) -> p u e x", e=2)
             for u in range(2):
                 for e in range(2):
                     nc.scalar.activation(
-                        out=planes[j, c][:, 2 * u + e, :], in_=src[:, u, e, :], func=COPY, scale=mscale[:, c, u, e : e + 1]
+                        out=planes[j, c][:, 2 * u + e, x0:x1], in_=src[:, u, e, x0:x1], func=COPY, scale=mscale[:, c, u, e : e + 1]
                     )
 
         def weave(dst, src, engine):
@@ -291,12 +293,12 @@ def tile_coded_aperture_backprojection_s13_kernel(
         warm(2, "m3")
         turn_mask(1, 0, "m3")
         turn_scenes(0, 0)
-        warm(2, "m2")
         turn_scenes(1, 0)
         turn_mask(1, 1, "t0")
         widen(3, 0, 0, 512, "s")
         empty_scenes(0, 0)
         empty_scenes(1, 0)
+        warm(2, "t1")
         product(1, 0)
         turn_scenes(0, 1)
         turn_scenes(1, 1)
@@ -358,59 +360,55 @@ def tile_coded_aperture_backprojection_s13_kernel(
         product(4, 0)
         project(3, 1)
         turn_mask(5, 0)
+        turn_mask(7, 1)
+        product_planes(7, 1)
         whiten(3, 0)
         quant_mask(4)
         quant_z(0)
         project(4, 0)
-        turn_mask(7, 1)
+        turn_mask(7, 0, "m3")
         weave_planes(6, 1)
-        product_planes(7, 1)
         whiten(3, 1)
         weave_z(1, 0, CUT, "g")
+        weave_z(1, CUT, 256, "s")
+        product_planes(7, 0)
         product(5, 0)
         project(4, 1)
         turn_mask(6, 0)
-        turn_mask(7, 0, "m3")
         whiten(4, 0)
         quant_mask(5)
-        weave_z(1, 256, B, "g")
+        weave_planes(7, 1, 0, 256, "g")
         project(5, 0)
         for m in (0, 1, 2, 5):
             backproject(m, 0)
-        product_planes(7, 0)
-        weave_z(1, CUT, 256, "s")
-        weave_planes(7, 1)
+        weave_planes(7, 0)
+        weave_z(1, 256, B, "s")
         whiten(4, 1)
         product(6, 0)
         project(5, 1)
+        backproject(3, 0)
         backproject(4, 0)
-        weave_planes(7, 0)
         whiten(5, 0)
         quant_mask(6)
-        quant_z(1)
+        quant_z(1, 0, 256)
         project(6, 0)
-        backproject(3, 0)
-        backproject(0, 1)
         whiten(5, 1)
         weave_z(2, 0, 256, "s")
-        weave_z(2, 256, B, "s")
         project(6, 1)
-        whiten(6, 0)
+        weave_z(2, 256, B, "s")
         quant_mask(7)
-        backproject(1, 1)
-        backproject(2, 1)
+        whiten(6, 0)
         project(7, 0)
         whiten(6, 1)
         project(7, 1)
-        quant_z(2, 0, 256)
-        for m in range(3, 6):
+        quant_z(1, 256, B)
+        for m in range(6):
             backproject(m, 1)
+        quant_z(2, 0, 256)
         whiten(7, 0)
         whiten(7, 1, 0, 256)
         weave_z(last, 0, 160)
         whiten(7, 1, 256, B)
-        backproject(6, 0)
-        backproject(6, 1)
         quant_z(2, 256, B)
         for m in range(4):
             backproject(m, 2)
@@ -419,15 +417,19 @@ def tile_coded_aperture_backprojection_s13_kernel(
         weave_z(last, 448, B, "s")
         quant_z(last, 0, 256)
         quant_z(last, 256, B)
+        res = keep.tile([NP, NM, B], F32, name="res")
+        out_rows = out.rearrange("(m p) b -> p m b", p=NP)
         for m in range(NM):
             for g in range(done[m], NG):
                 backproject(m, g)
-            res = work.tile([NP, B], F32, name=f"res{m}", tag="res", bufs=NM)
             pieces = 2 if m in (0, NM - 1) else 1
             for h in range(pieces):
                 cols = slice(B // pieces * h, B // pieces * (h + 1))
                 if m % 2 == 0:
-                    nc.vector.tensor_copy(out=res[:, cols], in_=img[m][:, cols])
+                    nc.vector.tensor_copy(out=res[:, m, cols], in_=img[m][:, cols])
                 else:
-                    nc.scalar.copy(out=res[:, cols], in_=img[m][:, cols])
-                nc.sync.dma_start(out=out_v[m][:, cols], in_=res[:, cols])
+                    nc.scalar.copy(out=res[:, m, cols], in_=img[m][:, cols])
+                if m in (3, 5):
+                    nc.sync.dma_start(out=out_rows[:, m - 1 : m + 1, :], in_=res[:, m - 1 : m + 1, :])
+                elif m not in (2, 4):
+                    nc.sync.dma_start(out=out_rows[:, m, cols], in_=res[:, m, cols])

@@ -250,6 +250,37 @@ def tile_coded_aperture_backprojection_s13_kernel(
         img_tag = ["m0", "m1", "m2", "m3", "t0", "t1", "y0", "y1"]
         last = NG - 1
 
+        def backproject_half(m, g, h):
+            done[m] = g + h
+            for q in range(2 * h, 2 * h + 2):
+                cols = slice(128 * q, 128 * (q + 1))
+                nc.tensor.matmul_mx(
+                    out=img[m][:, cols],
+                    lhsT=gw[g][:, 256 * m : 256 * (m + 1)].bitcast(E2M1X4),
+                    lhsT_scale=gsc[:, g, 128 * m : 128 * (m + 1)],
+                    rhs=zcodes[g][:, cols].bitcast(E4M3X4),
+                    rhs_scale=zscales[g][:, cols],
+                    start=False,
+                    stop=False,
+                )
+
+        def backproject_split(h, g):
+            if g == 0:
+                split[h] = psum.tile([NP, 2, 256], F32, name=f"split{h}", tag=img_tag[h])
+            for m in range(2):
+                for q in range(2):
+                    cols = slice(256 * h + 128 * q, 256 * h + 128 * (q + 1))
+                    nc.tensor.matmul_mx(
+                        out=split[h][:, m, 128 * q : 128 * (q + 1)],
+                        lhsT=gw[g][:, 256 * m : 256 * (m + 1)].bitcast(E2M1X4),
+                        lhsT_scale=gsc[:, g, 128 * m : 128 * (m + 1)],
+                        rhs=zcodes[g][:, cols].bitcast(E4M3X4),
+                        rhs_scale=zscales[g][:, cols],
+                        start=(g == 0 and m == 0 and q == 0),
+                        stop=(g == last and m == 1 and q == 1),
+                    )
+
+        split = {}
         done = [0] * NM
 
         def backproject(m, g):
@@ -379,8 +410,10 @@ def tile_coded_aperture_backprojection_s13_kernel(
         quant_mask(5)
         weave_planes(7, 1, 0, 256, "g")
         project(5, 0)
-        for m in (0, 1, 2, 5):
-            backproject(m, 0)
+        backproject_split(0, 0)
+        backproject_split(1, 0)
+        backproject(2, 0)
+        backproject(5, 0)
         weave_planes(7, 0)
         weave_z(1, 256, B, "s")
         whiten(4, 1)
@@ -395,6 +428,7 @@ def tile_coded_aperture_backprojection_s13_kernel(
         whiten(5, 1)
         weave_z(2, 0, 256, "s")
         project(6, 1)
+        backproject_split(0, 1)
         weave_z(2, 256, B, "s")
         quant_mask(7)
         whiten(6, 0)
@@ -402,27 +436,37 @@ def tile_coded_aperture_backprojection_s13_kernel(
         whiten(6, 1)
         project(7, 1)
         quant_z(1, 256, B)
-        for m in range(6):
+        backproject_split(1, 1)
+        for m in range(2, 6):
             backproject(m, 1)
         quant_z(2, 0, 256)
+        backproject_split(0, 2)
         whiten(7, 0)
         whiten(7, 1, 0, 256)
         weave_z(last, 0, 160)
         whiten(7, 1, 256, B)
         quant_z(2, 256, B)
-        for m in range(4):
-            backproject(m, 2)
+        backproject_split(1, 2)
+        backproject(2, 2)
+        backproject(3, 2)
         weave_z(last, 160, 256, "v")
         weave_z(last, 256, 448, "v")
         weave_z(last, 448, B, "s")
         quant_z(last, 0, 256)
+        backproject_split(0, last)
         quant_z(last, 256, B)
+        backproject_split(1, last)
         res = keep.tile([NP, NM, B], F32, name="res")
         out_rows = out.rearrange("(m p) b -> p m b", p=NP)
-        for m in range(NM):
+        for m in range(2):
+            nc.vector.tensor_copy(out=res[:, m, 0:256], in_=split[0][:, m, :])
+            nc.sync.dma_start(out=out_rows[:, m, 0:256], in_=res[:, m, 0:256])
+        nc.scalar.copy(out=res[:, 0:2, 256:B], in_=split[1][:])
+        nc.sync.dma_start(out=out_rows[:, 0:2, 256:B], in_=res[:, 0:2, 256:B])
+        for m in range(2, NM):
             for g in range(done[m], NG):
                 backproject(m, g)
-            pieces = 2 if m in (0, NM - 1) else 1
+            pieces = 2 if m == NM - 1 else 1
             for h in range(pieces):
                 cols = slice(B // pieces * h, B // pieces * (h + 1))
                 if m % 2 == 0:

@@ -21,11 +21,13 @@ NP = 128
 NG = D // 512
 NPAIR = 2 * NG
 NC = P // 512
-NM = P // 128
-NR = B // 128
-CUT = 208
-QIN_TAG = {7: "q5"}
-ZQ_TAG = {(0, 1): "q3"}
+NBANK = P // 256
+H = B // 2
+IMG = [
+    [("a0", (0, 1)), ("a1", (2, 3)), ("a2", (4, 5)), ("a3", (6, 7))],
+    [("t0", (0, 1)), ("t1", (2, 3)), ("y1", (4, 5)), ("y0", (6,)), ("a0", (7,))],
+]
+GATED = [(j, 1) for j in range(2, 7)]
 
 
 def tile_coded_aperture_backprojection_s13_kernel(
@@ -34,13 +36,12 @@ def tile_coded_aperture_backprojection_s13_kernel(
     nc = tc.nc
     with ExitStack() as ctx, tc.manual_schedule():
         keep = ctx.enter_context(tc.tile_pool(name="keep", bufs=1))
-        work = ctx.enter_context(tc.tile_pool(name="work", bufs=2))
         psum = ctx.enter_context(tc.psum_pool(name="psum", bufs=1))
 
         mask_v = mask_bytes.rearrange("(g p t) k -> g p t k", g=NG, p=NP, t=4)
         sig_v = inv_sigma.rearrange("(g p t) b -> g p t b", g=NG, p=NP, t=4)
         scn_v = scenes.rearrange("(h t p) (c k) -> h c p t k", h=2, t=2, p=NP, c=NC)
-        out_v = out.rearrange("(m p) b -> m p b", p=NP)
+        out_rows = out.rearrange("(m p) b -> p m b", p=NP)
 
         mscale = keep.tile([NP, NC, 2, 2], F32, name="mscale")
         darks = keep.tile([NP, NG, 4], BF16, name="darks")
@@ -50,12 +51,6 @@ def tile_coded_aperture_backprojection_s13_kernel(
         sig = [keep.tile([NP, 4, B], BF16, name=f"sig{g}", align_bytes=64) for g in range(NG)]
         scn = {(h, c): keep.tile([NP, 2, 512], BF16, name=f"scn{h}{c}", align_bytes=64) for h in range(2) for c in range(NC)}
         gw = [keep.tile([NP, 2 * P], U8, name=f"gw{g}", align_bytes=64) for g in range(NG)]
-        sq = [keep.tile([NP, B, 4], BF16, name=f"sq{c}", align_bytes=64) for c in range(NC)]
-        scodes = keep.tile([NP, NC, B], U32, name="scodes", align_bytes=64)
-        sscales = keep.tile([NP, NC, B], U8, name="sscales", align_bytes=64)
-        zcodes = [keep.tile([NP, B], U32, name=f"zcodes{g}", align_bytes=64) for g in range(NG)]
-        zscales = [keep.tile([NP, B], U8, name=f"zscales{g}", align_bytes=64) for g in range(NG)]
-
         warm_src = keep.tile([NP, 512], BF16, name="warm_src", align_bytes=64)
         nc.vector.memset(warm_src[:], 0.0)
         make_identity(nc, ident[:])
@@ -65,117 +60,114 @@ def tile_coded_aperture_backprojection_s13_kernel(
             g, h = divmod(j, 2)
             nc.sync.dma_start(out=mb[j][:], in_=mask_v[g][:, 2 * h : 2 * h + 2, :])
 
-        nc.sync.dma_start(out=mb[0][:, 0, :], in_=mask_v[0][:, 0, :])
-        nc.sync.dma_start(
-            out=mscale[:], in_=mask_scale.rearrange("o (c p u e) -> p (o c) u e", c=NC, p=NP, u=2, e=2)
-        )
-        nc.sync.dma_start(out=mb[0][:, 1, :], in_=mask_v[0][:, 1, :])
-        load_pair(1)
-        load_pair(2)
-        nc.sync.dma_start(out=scn[0, 0][:], in_=scn_v[0, 0])
-        nc.sync.dma_start(out=scn[1, 0][:], in_=scn_v[1, 0])
-        load_pair(3)
-        nc.sync.dma_start(out=scn[0, 1][:], in_=scn_v[0, 1])
-        nc.sync.dma_start(out=scn[1, 1][:], in_=scn_v[1, 1])
-        load_pair(4)
-        load_pair(5)
-        nc.sync.dma_start(out=darks[:], in_=dark.rearrange("(g p t) -> p g t", g=NG, p=NP, t=4))
-        nc.sync.dma_start(out=sig[0][:], in_=sig_v[0])
-        load_pair(6)
-        load_pair(7)
-        nc.sync.dma_start(out=sig[1][:], in_=sig_v[1])
-        for q in range(4):
-            nc.sync.dma_start(
-                out=gsc[32 * q : 32 * q + 4].bitcast(I32),
-                in_=dec_scales[:, 4 * q : 4 * q + 4, :].bitcast(I32).rearrange("g q n -> q g n"),
-            )
-        nc.sync.dma_start(out=gw[0][:].bitcast(I32), in_=dec_words[0].bitcast(I32))
-        for g in range(2, NG):
-            nc.sync.dma_start(out=sig[g][:], in_=sig_v[g])
-            nc.sync.dma_start(out=gw[g - 1][:].bitcast(I32), in_=dec_words[g - 1].bitcast(I32))
-        nc.sync.dma_start(out=gw[NG - 1][:].bitcast(I32), in_=dec_words[NG - 1].bitcast(I32))
+        def load_tile(j, t):
+            g, h = divmod(j, 2)
+            nc.sync.dma_start(out=mb[j][:, t, :], in_=mask_v[g][:, 2 * h + t, :])
 
-        wide, tbank, qin, planes, codes, scales, ybank, zt, zq, img, sbank, first = ({} for i in range(12))
+        def load_mscale():
+            nc.sync.dma_start(out=mscale[:], in_=mask_scale.rearrange("o (c p u e) -> p (o c) u e", c=NC, p=NP, u=2, e=2))
+
+        def load_scenes(h, c):
+            nc.sync.dma_start(out=scn[h, c][:], in_=scn_v[h, c])
+
+        def load_darks():
+            nc.sync.dma_start(out=darks[:], in_=dark.rearrange("(g p t) -> p g t", g=NG, p=NP, t=4))
+
+        def load_sig(g):
+            nc.sync.dma_start(out=sig[g][:], in_=sig_v[g])
+
+        def load_gscales():
+            for q in range(4):
+                nc.sync.dma_start(
+                    out=gsc[32 * q : 32 * q + 4].bitcast(I32),
+                    in_=dec_scales[:, 4 * q : 4 * q + 4, :].bitcast(I32).rearrange("g q n -> q g n"),
+                )
+
+        def load_gwords(g):
+            nc.sync.dma_start(out=gw[g][:].bitcast(I32), in_=dec_words[g].bitcast(I32))
+
+        wide, tbank, qin, planes, codes, scales, ybank, zt, zq, zcodes, zscales, img, sbank, first, sq, scodes, sscales, res = (
+            {} for i in range(18)
+        )
 
         def warm(count, tag):
             bank = psum.tile([NP, 512], F32, name=f"warm_{tag}", tag=tag)
             for i in range(count):
                 nc.tensor.matmul(bank[:], warm_src[:, 0:NP], warm_src[:], start=True, stop=True)
 
-        def widen(j, t, c0, c1, engine, tag=None):
-            piece = keep.tile([NP, c1 - c0], BF16, name=f"wide{j}{t}{c0 // 512}", tag=tag or f"wide{j}{t}{c0 // 512}", align_bytes=64)
-            for c in range(c0 // 512, c1 // 512):
-                wide[j, t, c] = piece[:, 512 * c - c0 : 512 * (c + 1) - c0]
-            dst = piece[:]
-            src = mb[j][:, t, c0:c1].bitcast(FP8)
+        def widen(j, x0, x1, engine, tag=None):
+            piece = keep.tile([NP, x1 - x0], BF16, name=f"wide{j}_{x0}", tag=tag or f"wide{j}_{x0}", align_bytes=64)
+            for q in range(x0 // 512, x1 // 512):
+                wide[j, q // 2, q % 2] = piece[:, 512 * q - x0 : 512 * (q + 1) - x0]
+            src = mb[j][:].rearrange("p t k -> p (t k)")[:, x0:x1].bitcast(FP8)
             if engine == "v":
-                nc.vector.tensor_copy(out=dst, in_=src)
+                nc.vector.tensor_copy(out=piece[:], in_=src)
             elif engine == "g":
-                nc.gpsimd.tensor_copy(out=dst, in_=src)
+                nc.gpsimd.tensor_copy(out=piece[:], in_=src)
             else:
-                nc.scalar.copy(out=dst, in_=src)
+                nc.scalar.copy(out=piece[:], in_=src)
 
         def turn(bk, tiles):
             for t in range(2):
                 for u in range(2):
-                    nc.tensor.transpose(
-                        bk[:, u, 128 * t : 128 * t + 128], tiles[t][:, u : 256 : 2], ident[:]
-                    )
+                    nc.tensor.transpose(bk[:, u, 128 * t : 128 * t + 128], tiles[t][:, u:256:2], ident[:])
 
-        def turn_mask(j, c, tag=None):
-            tbank[j, c] = psum.tile([NP, 2, 256], F32, name=f"tb{j}_{c}", tag=tag or f"t{c}")
+        def turn_mask(j, c, tag):
+            tbank[j, c] = psum.tile([NP, 2, 256], F32, name=f"tb{j}_{c}", tag=tag)
             turn(tbank[j, c], [wide[j, t, c].bitcast(F32) for t in range(2)])
 
-        def turn_scenes(h, c):
-            sbank[h, c] = psum.tile([NP, 2, 256], F32, name=f"sb{h}_{c}", tag=f"m{2 * h + c}")
+        def turn_scenes(h, c, tag):
+            sbank[h, c] = psum.tile([NP, 2, 256], F32, name=f"sb{h}_{c}", tag=tag)
             turn(sbank[h, c], [scn[h, c][:, t, :].bitcast(F32) for t in range(2)])
 
         def empty_scenes(h, c):
-            dst = sq[c][:, 256 * h : 256 * (h + 1), :].rearrange("p x t -> p (x t)").bitcast(F32)
-            nc.scalar.copy(
-                out=dst.rearrange("p (x u) -> p x u", u=2), in_=sbank[h, c][:].rearrange("p u x -> p x u")
-            )
+            if h not in sq:
+                sq[h] = keep.tile([NP, NC, H, 4], BF16, name=f"sq{h}", tag=f"sq{h}", align_bytes=64)
+            dst = sq[h][:, c].rearrange("p x t -> p (x t)").bitcast(F32)
+            nc.scalar.copy(out=dst.rearrange("p (x u) -> p x u", u=2), in_=sbank[h, c][:].rearrange("p u x -> p x u"))
 
-        def quant_scenes(c):
+        def quant_scenes(h):
+            scodes[h] = keep.tile([NP, NC, H], U32, name=f"scodes{h}", align_bytes=64)
+            sscales[h] = keep.tile([NP, NC, H], U8, name=f"sscales{h}", align_bytes=64)
             nc.vector.quantize_mx(
-                out=scodes[:, c, :].bitcast(E4M3X4),
-                scales=sscales[:, c, :],
-                in_=sq[c][:].rearrange("p x t -> p (x t)"),
+                out=scodes[h][:].rearrange("p c x -> p (c x)").bitcast(E4M3X4),
+                scales=sscales[h][:].rearrange("p c x -> p (c x)"),
+                in_=sq[h][:].rearrange("p c x t -> p (c x t)"),
             )
 
-        def quant_input(j):
-            if j not in qin:
-                qin[j] = keep.tile([NP, NC, 256, 4], BF16, name=f"qin{j}", tag=QIN_TAG.get(j, f"q{j}"), align_bytes=64)
-            return qin[j]
+        def quant_input(j, c):
+            if (j, c) not in qin:
+                qin[j, c] = keep.tile([NP, 256, 4], BF16, name=f"qin{j}{c}", tag="gated" if (j, c) in GATED else f"qin{j}{c}", align_bytes=64)
+            return qin[j, c]
 
-        def product(j, c, x0=0, x1=256):
+        def product(j, c):
             nc.vector.tensor_tensor(
-                out=quant_input(j)[:, c, x0:x1].rearrange("p x (u e) -> p x u e", u=2),
-                in0=mscale[:, c : c + 1].to_broadcast([NP, x1 - x0, 2, 2]),
-                in1=tbank[j, c][:].bitcast(BF16).rearrange("p u (x e) -> p x u e", e=2)[:, x0:x1],
+                out=quant_input(j, c)[:].rearrange("p x (u e) -> p x u e", u=2),
+                in0=mscale[:, c : c + 1].to_broadcast([NP, 256, 2, 2]),
+                in1=tbank[j, c][:].bitcast(BF16).rearrange("p u (x e) -> p x u e", e=2),
                 op=ALU.mult,
             )
 
-        def turn_first(t, c):
-            first[t, c] = psum.tile([NP, 2, NP], F32, name=f"first{t}_{c}", tag=("y", "t")[t] + str(c))
+        def turn_first(t, c, tag):
+            first[t, c] = psum.tile([NP, 2, NP], F32, name=f"first{t}_{c}", tag=tag)
             for u in range(2):
                 nc.tensor.transpose(first[t, c][:, u, :], wide[0, t, c].bitcast(F32)[:, u:256:2], ident[:])
 
         def product_first(t, c):
             nc.vector.tensor_tensor(
-                out=quant_input(0)[:, c, NP * t : NP * (t + 1)].rearrange("p x (u e) -> p x u e", u=2),
+                out=quant_input(0, c)[:, NP * t : NP * (t + 1)].rearrange("p x (u e) -> p x u e", u=2),
                 in0=mscale[:, c : c + 1].to_broadcast([NP, NP, 2, 2]),
                 in1=first[t, c][:].bitcast(BF16).rearrange("p u (x e) -> p x u e", e=2),
                 op=ALU.mult,
             )
 
-        def product_planes(j, c, x0=0, x1=256):
-            planes[j, c] = work.tile([NP, 4, 256], BF16, name=f"planes{j}_{c}", tag="planes", bufs=4, align_bytes=64)
+        def product_planes(j, c):
+            planes[j, c] = keep.tile([NP, 4, 256], BF16, name=f"planes{j}_{c}",  align_bytes=64)
             src = tbank[j, c][:].bitcast(BF16).rearrange("p u (x e) -> p u e x", e=2)
             for u in range(2):
                 for e in range(2):
                     nc.scalar.activation(
-                        out=planes[j, c][:, 2 * u + e, x0:x1], in_=src[:, u, e, x0:x1], func=COPY, scale=mscale[:, c, u, e : e + 1]
+                        out=planes[j, c][:, 2 * u + e, :], in_=src[:, u, e, :], func=COPY, scale=mscale[:, c, u, e : e + 1]
                     )
 
         def weave(dst, src, engine):
@@ -191,289 +183,251 @@ def tile_coded_aperture_backprojection_s13_kernel(
             else:
                 nc.scalar.copy(out=dst, in_=src)
 
-        def weave_planes(j, c, x0=0, x1=256, engine="s"):
-            weave(quant_input(j)[:, c, x0:x1], planes[j, c][:, :, x0:x1], engine)
+        def weave_planes(j, c, x0, x1, engine):
+            weave(quant_input(j, c)[:, x0:x1], planes[j, c][:, :, x0:x1], engine)
 
-        def quant_mask(j):
-            codes[j] = work.tile([NP, NC, 256], U32, name=f"codes{j}", tag="codes", bufs=4, align_bytes=64)
-            scales[j] = work.tile([NP, NC, 256], U8, name=f"scales{j}", tag="scales", bufs=4, align_bytes=64)
-            nc.vector.quantize_mx(
-                out=codes[j][:].rearrange("p c x -> p (c x)").bitcast(E4M3X4),
-                scales=scales[j][:].rearrange("p c x -> p (c x)"),
-                in_=qin[j][:].rearrange("p c x t -> p (c x t)"),
-            )
-
-        def project(j, t, tag=None, passes=range(NC)):
-            if (j, t) not in ybank:
-                ybank[j, t] = psum.tile([NP, B], F32, name=f"y{j}_{t}", tag=tag or f"y{t}")
-            cols = slice(128 * t, 128 * t + 128)
+        def quant_mask(j, passes=range(NC)):
+            if j not in codes:
+                codes[j] = keep.tile([NP, NC, 256], U32, name=f"codes{j}", align_bytes=64)
+                scales[j] = keep.tile([NP, NC, 256], U8, name=f"scales{j}", align_bytes=64)
             for c in passes:
-                nc.tensor.matmul_mx(
-                    out=ybank[j, t][:],
-                    lhsT=codes[j][:, c, cols].bitcast(E4M3X4),
-                    lhsT_scale=scales[j][:, c, cols],
-                    rhs=scodes[:, c, :].bitcast(E4M3X4),
-                    rhs_scale=sscales[:, c, :],
-                    start=(c == 0),
-                    stop=(c == NC - 1),
-                )
-
-        def whiten(j, t, b0=0, b1=B):
-            g, h = divmod(j, 2)
-            s = 2 * h + t
-            if g not in zt:
-                zt[g] = work.tile([NP, 4, B], BF16, name=f"zt{g}", tag="zt", bufs=NG, align_bytes=64)
-            nc.vector.scalar_tensor_tensor(
-                out=zt[g][:, s, b0:b1],
-                in0=ybank[j, t][:, b0:b1],
-                scalar=darks[:, g, s : s + 1],
-                in1=sig[g][:, s, b0:b1],
-                op0=ALU.subtract,
-                op1=ALU.mult,
-            )
-
-        def weave_z(g, b0, b1, engine="s"):
-            h = b0 // 256
-            if (g, h) not in zq:
-                zq[g, h] = keep.tile([NP, 256, 4], BF16, name=f"zq{g}{h}", tag=ZQ_TAG.get((g, h), f"z{g}{h}"), align_bytes=64)
-            weave(zq[g, h][:, b0 - 256 * h : b1 - 256 * h, :], zt[g][:, :, b0:b1], engine)
-
-        def quant_z(g, b0=0, b1=B):
-            for h in range(b0 // 256, b1 // 256):
-                cols = slice(256 * h, 256 * (h + 1))
                 nc.vector.quantize_mx(
-                    out=zcodes[g][:, cols].bitcast(E4M3X4),
-                    scales=zscales[g][:, cols],
-                    in_=zq[g, h][:].rearrange("p b t -> p (b t)"),
+                    out=codes[j][:, c, :].bitcast(E4M3X4), scales=scales[j][:, c, :], in_=qin[j, c][:].rearrange("p x t -> p (x t)")
                 )
 
-        img_tag = ["m0", "m1", "m2", "m3", "t0", "t1", "y0", "y1"]
-        last = NG - 1
-
-        def backproject_half(m, g, h):
-            done[m] = g + h
-            for q in range(2 * h, 2 * h + 2):
-                cols = slice(128 * q, 128 * (q + 1))
-                nc.tensor.matmul_mx(
-                    out=img[m][:, cols],
-                    lhsT=gw[g][:, 256 * m : 256 * (m + 1)].bitcast(E2M1X4),
-                    lhsT_scale=gsc[:, g, 128 * m : 128 * (m + 1)],
-                    rhs=zcodes[g][:, cols].bitcast(E4M3X4),
-                    rhs_scale=zscales[g][:, cols],
-                    start=False,
-                    stop=False,
-                )
-
-        def backproject_split(h, g):
-            if g == 0:
-                split[h] = psum.tile([NP, 2, 256], F32, name=f"split{h}", tag=img_tag[h])
-            for m in range(2):
-                for q in range(2):
-                    cols = slice(256 * h + 128 * q, 256 * h + 128 * (q + 1))
+        def project(j, h, tag):
+            ybank[j, h] = psum.tile([NP, 2, H], F32, name=f"y{j}_{h}", tag=tag)
+            for t in range(2):
+                cols = slice(128 * t, 128 * t + 128)
+                for c in range(NC):
                     nc.tensor.matmul_mx(
-                        out=split[h][:, m, 128 * q : 128 * (q + 1)],
-                        lhsT=gw[g][:, 256 * m : 256 * (m + 1)].bitcast(E2M1X4),
-                        lhsT_scale=gsc[:, g, 128 * m : 128 * (m + 1)],
-                        rhs=zcodes[g][:, cols].bitcast(E4M3X4),
-                        rhs_scale=zscales[g][:, cols],
-                        start=(g == 0 and m == 0 and q == 0),
-                        stop=(g == last and m == 1 and q == 1),
+                        out=ybank[j, h][:, t, :],
+                        lhsT=codes[j][:, c, cols].bitcast(E4M3X4),
+                        lhsT_scale=scales[j][:, c, cols],
+                        rhs=scodes[h][:, c, :].bitcast(E4M3X4),
+                        rhs_scale=sscales[h][:, c, :],
+                        start=(c == 0),
+                        stop=(c == NC - 1),
                     )
 
-        split = {}
-        done = [0] * NM
+        def whiten(j, h, tiles=range(2)):
+            g, r = divmod(j, 2)
+            if (g, h) not in zt:
+                zt[g, h] = keep.tile([NP, 4, H], BF16, name=f"zt{g}{h}", align_bytes=64)
+            for t in tiles:
+                s = 2 * r + t
+                nc.vector.scalar_tensor_tensor(
+                    out=zt[g, h][:, s, :],
+                    in0=ybank[j, h][:, t, :],
+                    scalar=darks[:, g, s : s + 1],
+                    in1=sig[g][:, s, H * h : H * (h + 1)],
+                    op0=ALU.subtract,
+                    op1=ALU.mult,
+                )
 
-        def backproject(m, g):
-            done[m] = g + 1
-            if g == 0:
-                img[m] = psum.tile([NP, B], F32, name=f"img{m}", tag=img_tag[m])
-            nc.tensor.matmul_mx(
-                out=img[m][:],
-                lhsT=gw[g][:, 256 * m : 256 * (m + 1)].bitcast(E2M1X4),
-                lhsT_scale=gsc[:, g, 128 * m : 128 * (m + 1)],
-                rhs=zcodes[g][:].bitcast(E4M3X4),
-                rhs_scale=zscales[g][:],
-                start=(g == 0),
-                stop=(g == last),
+        def weave_z(g, h, x0, x1, engine, tag=None):
+            if (g, h) not in zq:
+                zq[g, h] = keep.tile([NP, H, 4], BF16, name=f"zq{g}{h}", tag=tag or f"zq{g}{h}", align_bytes=64)
+            weave(zq[g, h][:, x0:x1, :], zt[g, h][:, :, x0:x1], engine)
+
+        def quant_z(g, h):
+            zcodes[g, h] = keep.tile([NP, H], U32, name=f"zcodes{g}{h}", align_bytes=64)
+            zscales[g, h] = keep.tile([NP, H], U8, name=f"zscales{g}{h}", align_bytes=64)
+            nc.vector.quantize_mx(
+                out=zcodes[g, h][:].bitcast(E4M3X4), scales=zscales[g, h][:], in_=zq[g, h][:].rearrange("p b t -> p (b t)")
             )
 
-        def whiten_pair(j):
-            whiten(j, 0)
-            whiten(j, 1)
+        def backproject(g, h, banks):
+            for q in banks:
+                tag, tiles = IMG[h][q]
+                if g == 0:
+                    img[h, q] = psum.tile([NP, len(tiles), H], F32, name=f"img{h}{q}", tag=tag)
+                for i, m in enumerate(tiles):
+                    nc.tensor.matmul_mx(
+                        out=img[h, q][:, i, :],
+                        lhsT=gw[g][:, 256 * m : 256 * (m + 1)].bitcast(E2M1X4),
+                        lhsT_scale=gsc[:, g, 128 * m : 128 * (m + 1)],
+                        rhs=zcodes[g, h][:].bitcast(E4M3X4),
+                        rhs_scale=zscales[g, h][:],
+                        start=(g == 0 and i == 0),
+                        stop=(g == NG - 1 and i == len(tiles) - 1),
+                    )
 
-        def project_pair(j, tags=(None, None)):
-            project(j, 0, tags[0])
-            project(j, 1, tags[1])
+        def emit(h, q, engine):
+            tiles = IMG[h][q][1]
+            res[h, q] = keep.tile([NP, len(tiles), H], F32, name=f"res{h}{q}")
+            if engine == "v":
+                nc.vector.tensor_copy(out=res[h, q][:], in_=img[h, q][:])
+            else:
+                nc.scalar.copy(out=res[h, q][:], in_=img[h, q][:])
+            nc.sync.dma_start(out=out_rows[:, tiles[0] : tiles[-1] + 1, H * h : H * (h + 1)], in_=res[h, q][:])
 
-        warm(4, "m3")
-        widen(0, 0, 0, 512, "v")
-        widen(0, 0, 512, P, "s")
-        turn_first(0, 0)
-        turn_first(0, 1)
-        widen(0, 1, 0, 512, "s")
-        widen(0, 1, 512, P, "v")
-        turn_first(1, 0)
-        turn_first(1, 1)
-        widen(1, 0, 0, P, "s")
-        widen(1, 1, 0, P, "s")
-        widen(2, 0, 0, P, "s")
-        widen(2, 1, 0, P, "g")
-        widen(3, 1, 0, 512, "g")
+        load_tile(0, 0)
+        load_mscale()
+        load_tile(0, 1)
+        load_scenes(0, 0)
+        load_scenes(0, 1)
+        for j in range(1, 5):
+            load_pair(j)
+        load_darks()
+        load_sig(0)
+        load_pair(5)
+        load_scenes(1, 0)
+        load_scenes(1, 1)
+        load_pair(6)
+        load_pair(7)
+        load_gscales()
+        load_gwords(0)
+        for g in range(1, NG):
+            load_sig(g)
+            load_gwords(g)
+
+        warm(4, "a3")
+        widen(0, 0, 512, "v")
+        widen(0, 512, 1024, "s")
+        turn_first(0, 0, "y0")
+        turn_first(0, 1, "y1")
+        widen(0, 1024, 1536, "s")
+        widen(0, 1536, 2048, "v")
+        turn_first(1, 0, "t0")
+        turn_first(1, 1, "t1")
+        warm(2, "a3")
+        turn_scenes(0, 0, "a0")
+        turn_scenes(0, 1, "a1")
+        widen(1, 0, 1024, "s")
+        widen(1, 1024, 1536, "g")
         for t, c in ((0, 0), (0, 1), (1, 0), (1, 1)):
             product_first(t, c)
-        warm(2, "m3")
-        turn_mask(1, 0, "m3")
-        turn_scenes(0, 0)
-        turn_scenes(1, 0)
-        turn_mask(1, 1, "t0")
-        widen(3, 0, 0, 512, "s")
         empty_scenes(0, 0)
-        empty_scenes(1, 0)
-        warm(2, "t1")
-        product(1, 0)
-        turn_scenes(0, 1)
-        turn_scenes(1, 1)
-        quant_mask(0)
-        widen(3, 1, 512, P, "g", "q0")
-        widen(3, 0, 512, P, "s")
-        widen(4, 0, 0, P, "s")
         empty_scenes(0, 1)
-        empty_scenes(1, 1)
-        product(1, 1)
-        warm(2, "t1")
-        turn_mask(2, 0)
-        turn_mask(2, 1)
+        widen(1, 1536, 2048, "s")
+        warm(2, "a3")
+        turn_mask(1, 0, "a2")
+        turn_mask(1, 1, "a3")
+        widen(2, 0, 2048, "s")
+        widen(3, 0, 2048, "s")
+        quant_mask(0)
         quant_scenes(0)
-        quant_mask(1)
-        quant_scenes(1)
-        widen(4, 1, 0, P, "g", "sq1")
-        widen(5, 0, 0, P, "g")
-        widen(7, 0, 0, P, "g")
-        project(0, 0, passes=[0])
-        project(0, 1, passes=[0])
-        project(0, 0, passes=[1])
-        project(0, 1, passes=[1])
-        widen(5, 1, 0, P, "s")
-        widen(6, 0, 0, P, "s")
-        widen(6, 1, 0, P, "s")
-        widen(7, 1, 0, P, "s")
-        turn_mask(3, 1, "m0")
+        widen(4, 0, 2048, "g", "sq0")
+        project(0, 0, "y0")
+        product(1, 0)
+        turn_mask(2, 0, "t0")
+        turn_mask(2, 1, "t1")
+        turn_mask(3, 1, "a1")
+        widen(5, 0, 2048, "s")
+        product(1, 1)
+        whiten(0, 0)
         product_planes(3, 1)
+        quant_mask(1)
+        widen(7, 0, 1024, "g", "qin10")
+        turn_scenes(1, 0, "a2")
+        project(1, 0, "y1")
+        turn_scenes(1, 1, "a3")
+        turn_mask(3, 0, "a0")
+        empty_scenes(1, 0)
         product(2, 0)
-        product(2, 1)
-        project(1, 0, "m2")
-        turn_mask(4, 1, "m1")
-        project(1, 1, "m3")
-        turn_mask(3, 0)
-        weave_planes(3, 1)
-        product_planes(4, 1)
-        whiten_pair(0)
         whiten(1, 0)
-        quant_mask(2)
-        project(2, 0)
-        turn_mask(5, 1)
-        weave_planes(4, 1)
-        product_planes(5, 1)
-        whiten(1, 1)
-        weave_z(0, 0, CUT, "g")
+        weave_z(0, 0, 0, 128, "s")
+        weave_z(0, 0, 128, H, "g")
+        empty_scenes(1, 1)
+        product(2, 1)
+        turn_mask(4, 1, "y0")
+        warm(1, "a2")
+        turn_mask(5, 1, "a1")
+        turn_mask(4, 0, "t0")
+        quant_mask(2, [0])
+        quant_z(0, 0)
+        quant_mask(2, [1])
+        weave_planes(3, 1, 0, 256, "g")
+        widen(6, 0, 2048, "s")
+        product_planes(4, 1)
+        project(2, 0, "y1")
+        backproject(0, 0, [2, 3])
+        turn_mask(6, 1, "t1")
         product(3, 0)
-        project(2, 1)
-        turn_mask(4, 0)
+        product_planes(5, 1)
+        widen(7, 1024, 2048, "s")
         whiten(2, 0)
+        quant_scenes(1)
         quant_mask(3)
-        weave_z(0, 256, B, "g")
-        project(3, 0)
-        turn_mask(6, 1, "m1")
-        weave_z(0, CUT, 256, "s")
-        weave_planes(5, 1)
-        product_planes(6, 1)
-        whiten(2, 1)
+        weave_planes(4, 1, 0, 256, "g")
+        backproject(0, 0, [0])
+        project(0, 1, "y0")
+        project(3, 0, "y1")
         product(4, 0)
-        project(3, 1)
-        turn_mask(5, 0)
-        turn_mask(7, 1)
-        product_planes(7, 1)
+        product_planes(6, 1)
+        turn_mask(7, 1, "a1")
+        turn_mask(5, 0, "t0")
+        turn_mask(7, 0, "t1")
+        whiten(0, 1)
         whiten(3, 0)
+        product_planes(7, 1)
+        weave_z(1, 0, 0, H, "s")
         quant_mask(4)
-        quant_z(0)
-        project(4, 0)
-        turn_mask(7, 0, "m3")
-        weave_planes(6, 1)
-        whiten(3, 1)
-        weave_z(1, 0, CUT, "g")
-        weave_z(1, CUT, 256, "s")
-        product_planes(7, 0)
+        weave_planes(5, 1, 0, 256, "g")
+        project(1, 1, "y0")
+        project(4, 0, "y1")
+        backproject(0, 0, [1])
         product(5, 0)
-        project(4, 1)
-        turn_mask(6, 0)
+        turn_mask(6, 0, "t0")
+        whiten(1, 1)
         whiten(4, 0)
+        product_planes(7, 0)
+        weave_planes(7, 1, 0, 256, "s")
+        project(2, 1, "y0")
+        quant_z(1, 0)
         quant_mask(5)
-        weave_planes(7, 1, 0, 256, "g")
-        project(5, 0)
-        backproject_split(0, 0)
-        backproject_split(1, 0)
-        backproject(2, 0)
-        backproject(5, 0)
-        weave_planes(7, 0)
-        weave_z(1, 256, B, "s")
-        whiten(4, 1)
+        weave_planes(6, 1, 0, 256, "g")
+        backproject(1, 0, [0, 1])
+        project(5, 0, "y1")
+        backproject(1, 0, [2, 3])
+        project(3, 1, "t1")
+        weave_planes(7, 0, 0, 256, "s")
         product(6, 0)
-        project(5, 1)
-        backproject(3, 0)
-        backproject(4, 0)
+        whiten(2, 1)
         whiten(5, 0)
+        weave_z(2, 0, 0, H, "s")
+        project(4, 1, "y0")
         quant_mask(6)
-        quant_z(1, 0, 256)
-        project(6, 0)
-        whiten(5, 1)
-        weave_z(2, 0, 256, "s")
-        project(6, 1)
-        backproject_split(0, 1)
-        weave_z(2, 256, B, "s")
         quant_mask(7)
+        quant_z(2, 0)
+        weave_z(0, 1, 0, H, "g", "zq20")
+        project(6, 0, "y1")
+        project(7, 0, "t0")
+        backproject(2, 0, [0, 1])
+        whiten(3, 1)
+        weave_z(1, 1, 0, H, "s")
+        project(5, 1, "t1")
         whiten(6, 0)
-        project(7, 0)
-        whiten(6, 1)
-        project(7, 1)
-        quant_z(1, 256, B)
-        backproject_split(1, 1)
-        for m in range(2, 6):
-            backproject(m, 1)
-        quant_z(2, 0, 256)
-        backproject_split(0, 2)
+        project(6, 1, "y1")
+        backproject(2, 0, [2, 3])
         whiten(7, 0)
-        whiten(7, 1, 0, 256)
-        weave_z(last, 0, 160)
-        whiten(7, 1, 256, B)
-        quant_z(2, 256, B)
-        backproject_split(1, 2)
-        backproject(2, 2)
-        backproject(3, 2)
-        weave_z(last, 160, 256, "v")
-        weave_z(last, 256, 448, "v")
-        weave_z(last, 448, B, "s")
-        quant_z(last, 0, 256)
-        backproject_split(0, last)
-        quant_z(last, 256, B)
-        backproject_split(1, last)
-        res = keep.tile([NP, NM, B], F32, name="res")
-        out_rows = out.rearrange("(m p) b -> p m b", p=NP)
-        for m in range(2):
-            nc.vector.tensor_copy(out=res[:, m, 0:256], in_=split[0][:, m, :])
-            nc.sync.dma_start(out=out_rows[:, m, 0:256], in_=res[:, m, 0:256])
-        nc.scalar.copy(out=res[:, 0:2, 256:B], in_=split[1][:])
-        nc.sync.dma_start(out=out_rows[:, 0:2, 256:B], in_=res[:, 0:2, 256:B])
-        for m in range(2, NM):
-            for g in range(done[m], NG):
-                backproject(m, g)
-            pieces = 2 if m == NM - 1 else 1
-            for h in range(pieces):
-                cols = slice(B // pieces * h, B // pieces * (h + 1))
-                if m % 2 == 0:
-                    nc.vector.tensor_copy(out=res[:, m, cols], in_=img[m][:, cols])
-                else:
-                    nc.scalar.copy(out=res[:, m, cols], in_=img[m][:, cols])
-                if m in (3, 5):
-                    nc.sync.dma_start(out=out_rows[:, m - 1 : m + 1, :], in_=res[:, m - 1 : m + 1, :])
-                elif m not in (2, 4):
-                    nc.sync.dma_start(out=out_rows[:, m, cols], in_=res[:, m, cols])
+        weave_z(3, 0, 0, H, "s")
+        whiten(4, 1)
+        quant_z(0, 1)
+        quant_z(1, 1)
+        project(7, 1, "y0")
+        backproject(0, 1, [0])
+        backproject(1, 1, [0])
+        whiten(5, 1)
+        quant_z(3, 0)
+        weave_z(2, 1, 0, 128, "g")
+        weave_z(2, 1, 128, H, "s")
+        backproject(3, 0, range(4))
+        whiten(6, 1)
+        emit(0, 0, "s")
+        whiten(7, 1)
+        quant_z(2, 1)
+        weave_z(3, 1, 128, H, "s")
+        weave_z(3, 1, 0, 128, "v")
+        emit(0, 1, "v")
+        quant_z(3, 1)
+        emit(0, 2, "s")
+        emit(0, 3, "v")
+        for q in (1, 2):
+            backproject(0, 1, [q])
+            backproject(1, 1, [q])
+        for q in range(5):
+            for g in range(0 if q >= 3 else 2, NG):
+                backproject(g, 1, [q])
+            emit(1, q, "sv"[q % 2])

@@ -265,9 +265,10 @@ def tile_coded_aperture_backprojection_s13_kernel(
         load_tile(0, 0)
         load_mscale()
         load_tile(0, 1)
+        load_pair(1)
         load_scenes(0, 0)
         load_scenes(0, 1)
-        for j in range(1, 5):
+        for j in range(2, 5):
             load_pair(j)
         load_darks()
         load_sig(0)
@@ -291,101 +292,99 @@ def tile_coded_aperture_backprojection_s13_kernel(
         widen(0, 1536, 2048, "v")
         turn_first(1, 0, "t0")
         turn_first(1, 1, "t1")
+        widen(1, 0, 1024, "s")
+        widen(1, 1024, 2048, "s")
         warm(2, "a3")
         turn_scenes(0, 0, "a0")
+        turn_mask(1, 0, "a2")
         turn_scenes(0, 1, "a1")
-        widen(1, 0, 1024, "s")
-        widen(1, 1024, 1536, "g")
+        turn_mask(1, 1, "a3")
         for t, c in ((0, 0), (0, 1), (1, 0), (1, 1)):
             product_first(t, c)
         empty_scenes(0, 0)
+        widen(2, 0, 1024, "s")
+        widen(2, 1024, 2048, "g")
         empty_scenes(0, 1)
-        widen(1, 1536, 2048, "s")
-        warm(2, "a3")
-        turn_mask(1, 0, "a2")
-        turn_mask(1, 1, "a3")
-        widen(2, 0, 2048, "s")
         widen(3, 0, 2048, "s")
+        product(1, 0)
+        warm(2, "y1")
+        turn_mask(2, 0, "t0")
+        turn_mask(2, 1, "t1")
         quant_mask(0)
         quant_scenes(0)
         widen(4, 0, 2048, "g", "sq0")
         project(0, 0, "y0")
-        product(1, 0)
-        turn_mask(2, 0, "t0")
-        turn_mask(2, 1, "t1")
-        turn_mask(3, 1, "a1")
-        widen(5, 0, 2048, "s")
         product(1, 1)
+        turn_mask(3, 1, "a1")
+        turn_mask(3, 0, "a0")
+        widen(5, 0, 2048, "s")
+        turn_scenes(1, 0, "a2")
+        turn_scenes(1, 1, "a3")
         whiten(0, 0)
+        product(2, 0)
         product_planes(3, 1)
         quant_mask(1)
-        widen(7, 0, 1024, "g", "qin10")
-        turn_scenes(1, 0, "a2")
+        widen(7, 0, 1024, "g", "qin11")
+        warm(2, "y1")
         project(1, 0, "y1")
-        turn_scenes(1, 1, "a3")
-        turn_mask(3, 0, "a0")
+        turn_mask(4, 1, "y0")
+        turn_mask(4, 0, "t0")
         empty_scenes(1, 0)
-        product(2, 0)
-        whiten(1, 0)
-        weave_z(0, 0, 0, 128, "s")
-        weave_z(0, 0, 128, H, "g")
         empty_scenes(1, 1)
         product(2, 1)
-        turn_mask(4, 1, "y0")
-        warm(1, "a2")
-        turn_mask(5, 1, "a1")
-        turn_mask(4, 0, "t0")
-        quant_mask(2, [0])
-        quant_z(0, 0)
-        quant_mask(2, [1])
-        weave_planes(3, 1, 0, 256, "g")
+        whiten(1, 0)
         widen(6, 0, 2048, "s")
-        product_planes(4, 1)
-        project(2, 0, "y1")
-        backproject(0, 0, [2, 3])
+        turn_mask(5, 1, "a1")
+        quant_scenes(1)
+        quant_mask(2)
+        weave_planes(3, 1, 0, 256, "g")
+        weave_z(0, 0, 0, H, "s")
+        project(0, 1, "y1")
+        project(2, 0, "a2")
         turn_mask(6, 1, "t1")
         product(3, 0)
-        product_planes(5, 1)
+        product_planes(4, 1)
         widen(7, 1024, 2048, "s")
+        whiten(0, 1)
         whiten(2, 0)
-        quant_scenes(1)
+        turn_mask(7, 1, "a3")
+        quant_z(0, 0)
         quant_mask(3)
         weave_planes(4, 1, 0, 256, "g")
+        product_planes(5, 1)
         backproject(0, 0, [0])
-        project(0, 1, "y0")
+        project(1, 1, "y0")
         project(3, 0, "y1")
+        backproject(0, 0, [2, 1])
         product(4, 0)
         product_planes(6, 1)
-        turn_mask(7, 1, "a1")
         turn_mask(5, 0, "t0")
         turn_mask(7, 0, "t1")
-        whiten(0, 1)
+        whiten(1, 1)
         whiten(3, 0)
         product_planes(7, 1)
         weave_z(1, 0, 0, H, "s")
         quant_mask(4)
         weave_planes(5, 1, 0, 256, "g")
-        project(1, 1, "y0")
-        project(4, 0, "y1")
-        backproject(0, 0, [1])
+        project(4, 0, "y0")
+        project(2, 1, "y1")
+        backproject(0, 0, [3])
         product(5, 0)
         turn_mask(6, 0, "t0")
-        whiten(1, 1)
         whiten(4, 0)
         product_planes(7, 0)
         weave_planes(7, 1, 0, 256, "s")
-        project(2, 1, "y0")
         quant_z(1, 0)
         quant_mask(5)
         weave_planes(6, 1, 0, 256, "g")
         backproject(1, 0, [0, 1])
-        project(5, 0, "y1")
+        project(5, 0, "y0")
         backproject(1, 0, [2, 3])
         project(3, 1, "t1")
         weave_planes(7, 0, 0, 256, "s")
         product(6, 0)
-        whiten(2, 1)
         whiten(5, 0)
+        whiten(2, 1)
         weave_z(2, 0, 0, H, "s")
         project(4, 1, "y0")
         quant_mask(6)
@@ -394,40 +393,40 @@ def tile_coded_aperture_backprojection_s13_kernel(
         weave_z(0, 1, 0, H, "g", "zq20")
         project(6, 0, "y1")
         project(7, 0, "t0")
-        backproject(2, 0, [0, 1])
+        backproject(2, 0, range(4))
         whiten(3, 1)
         weave_z(1, 1, 0, H, "s")
         project(5, 1, "t1")
         whiten(6, 0)
         project(6, 1, "y1")
-        backproject(2, 0, [2, 3])
         whiten(7, 0)
-        weave_z(3, 0, 0, H, "s")
+        weave_z(3, 0, 160, H, "s")
         whiten(4, 1)
-        quant_z(0, 1)
-        quant_z(1, 1)
         project(7, 1, "y0")
+        weave_z(3, 0, 0, 160, "v")
+        quant_z(0, 1)
+        quant_z(3, 0)
+        quant_z(1, 1)
         backproject(0, 1, [0])
+        backproject(3, 0, range(4))
         backproject(1, 1, [0])
         whiten(5, 1)
-        quant_z(3, 0)
+        emit(0, 0, "s")
         weave_z(2, 1, 0, 128, "g")
         weave_z(2, 1, 128, H, "s")
-        backproject(3, 0, range(4))
         whiten(6, 1)
-        emit(0, 0, "s")
+        emit(0, 1, "s")
         whiten(7, 1)
-        quant_z(2, 1)
-        weave_z(3, 1, 128, H, "s")
-        weave_z(3, 1, 0, 128, "v")
-        emit(0, 1, "v")
-        quant_z(3, 1)
+        weave_z(3, 1, 192, H, "s")
         emit(0, 2, "s")
+        weave_z(3, 1, 0, 192, "v")
+        quant_z(2, 1)
+        quant_z(3, 1)
         emit(0, 3, "v")
-        for q in (1, 2):
+        for q in range(1, 5):
             backproject(0, 1, [q])
             backproject(1, 1, [q])
         for q in range(5):
-            for g in range(0 if q >= 3 else 2, NG):
-                backproject(g, 1, [q])
+            backproject(2, 1, [q])
+            backproject(3, 1, [q])
             emit(1, q, "sv"[q % 2])

@@ -51,8 +51,6 @@ def tile_coded_aperture_backprojection_s13_kernel(
         sig = [keep.tile([NP, 4, B], BF16, name=f"sig{g}", align_bytes=64) for g in range(NG)]
         scn = {(h, c): keep.tile([NP, 2, 512], BF16, name=f"scn{h}{c}", align_bytes=64) for h in range(2) for c in range(NC)}
         gw = [keep.tile([NP, 2 * P], U8, name=f"gw{g}", align_bytes=64) for g in range(NG)]
-        warm_src = keep.tile([NP, 512], BF16, name="warm_src", align_bytes=64)
-        nc.vector.memset(warm_src[:], 0.0)
         make_identity(nc, ident[:])
         nc.vector.memset(gsc[:].bitcast(I32), 0)
 
@@ -89,11 +87,6 @@ def tile_coded_aperture_backprojection_s13_kernel(
         wide, tbank, qin, planes, codes, scales, ybank, zt, zq, zcodes, zscales, img, sbank, first, sq, scodes, sscales, res = (
             {} for i in range(18)
         )
-
-        def warm(count, tag):
-            bank = psum.tile([NP, 512], F32, name=f"warm_{tag}", tag=tag)
-            for i in range(count):
-                nc.tensor.matmul(bank[:], warm_src[:, 0:NP], warm_src[:], start=True, stop=True)
 
         def widen(j, x0, x1, engine, tag=None):
             piece = keep.tile([NP, x1 - x0], BF16, name=f"wide{j}_{x0}", tag=tag or f"wide{j}_{x0}", align_bytes=64)
@@ -277,13 +270,14 @@ def tile_coded_aperture_backprojection_s13_kernel(
         load_scenes(1, 1)
         load_pair(6)
         load_pair(7)
+        load_sig(1)
         load_gscales()
         load_gwords(0)
-        for g in range(1, NG):
+        for g in range(2, NG):
             load_sig(g)
-            load_gwords(g)
+            load_gwords(g - 1)
+        load_gwords(NG - 1)
 
-        warm(4, "a3")
         widen(0, 0, 512, "v")
         widen(0, 512, 1024, "s")
         turn_first(0, 0, "y0")
@@ -294,7 +288,6 @@ def tile_coded_aperture_backprojection_s13_kernel(
         turn_first(1, 1, "t1")
         widen(1, 0, 1024, "s")
         widen(1, 1024, 2048, "s")
-        warm(2, "a3")
         turn_scenes(0, 0, "a0")
         turn_mask(1, 0, "a2")
         turn_scenes(0, 1, "a1")
@@ -307,7 +300,6 @@ def tile_coded_aperture_backprojection_s13_kernel(
         empty_scenes(0, 1)
         widen(3, 0, 2048, "s")
         product(1, 0)
-        warm(2, "y1")
         turn_mask(2, 0, "t0")
         turn_mask(2, 1, "t1")
         quant_mask(0)
@@ -320,12 +312,11 @@ def tile_coded_aperture_backprojection_s13_kernel(
         widen(5, 0, 2048, "s")
         turn_scenes(1, 0, "a2")
         turn_scenes(1, 1, "a3")
-        whiten(0, 0)
         product(2, 0)
+        whiten(0, 0)
         product_planes(3, 1)
         quant_mask(1)
         widen(7, 0, 1024, "g", "qin11")
-        warm(2, "y1")
         project(1, 0, "y1")
         turn_mask(4, 1, "y0")
         turn_mask(4, 0, "t0")

@@ -21,13 +21,12 @@ NP = 128
 NG = D // 512
 NPAIR = 2 * NG
 NC = P // 512
-NBANK = P // 256
 H = B // 2
 IMG = [
     [("a0", (0, 1)), ("a1", (2, 3)), ("a2", (4, 5)), ("a3", (6, 7))],
-    [("t0", (0, 1)), ("t1", (2, 3)), ("y1", (4, 5)), ("y0", (6,)), ("a0", (7,))],
+    [("y0", (0,)), ("t1", (1, 2)), ("y1", (3, 4)), ("a0", (5, 6)), ("t0", (7,))],
 ]
-GATED = [(j, 1) for j in range(2, 7)]
+BOTH = (0, 1)
 
 
 def tile_coded_aperture_backprojection_s13_kernel(
@@ -55,18 +54,19 @@ def tile_coded_aperture_backprojection_s13_kernel(
         nc.vector.memset(gsc[:].bitcast(I32), 0)
 
         def load_pair(j):
-            g, h = divmod(j, 2)
-            nc.sync.dma_start(out=mb[j][:], in_=mask_v[g][:, 2 * h : 2 * h + 2, :])
+            g, r = divmod(j, 2)
+            nc.sync.dma_start(out=mb[j][:], in_=mask_v[g][:, 2 * r : 2 * r + 2, :])
 
         def load_tile(j, t):
-            g, h = divmod(j, 2)
-            nc.sync.dma_start(out=mb[j][:, t, :], in_=mask_v[g][:, 2 * h + t, :])
+            g, r = divmod(j, 2)
+            nc.sync.dma_start(out=mb[j][:, t, :], in_=mask_v[g][:, 2 * r + t, :])
 
         def load_mscale():
             nc.sync.dma_start(out=mscale[:], in_=mask_scale.rearrange("o (c p u e) -> p (o c) u e", c=NC, p=NP, u=2, e=2))
 
-        def load_scenes(h, c):
-            nc.sync.dma_start(out=scn[h, c][:], in_=scn_v[h, c])
+        def load_scenes(h):
+            for c in range(NC):
+                nc.sync.dma_start(out=scn[h, c][:], in_=scn_v[h, c])
 
         def load_darks():
             nc.sync.dma_start(out=darks[:], in_=dark.rearrange("(g p t) -> p g t", g=NG, p=NP, t=4))
@@ -84,34 +84,41 @@ def tile_coded_aperture_backprojection_s13_kernel(
         def load_gwords(g):
             nc.sync.dma_start(out=gw[g][:].bitcast(I32), in_=dec_words[g].bitcast(I32))
 
-        wide, tbank, qin, planes, codes, scales, ybank, zt, zq, zcodes, zscales, img, sbank, first, sq, scodes, sscales, res = (
-            {} for i in range(18)
+        halves, tbank, qin, planes, codes, scales, ybank, zt, zq, zcodes, zscales, img, sbank, first, sq, scodes, sscales = (
+            {} for i in range(17)
         )
 
-        def widen(j, x0, x1, engine, tag=None):
-            piece = keep.tile([NP, x1 - x0], BF16, name=f"wide{j}_{x0}", tag=tag or f"wide{j}_{x0}", align_bytes=64)
-            for q in range(x0 // 512, x1 // 512):
-                wide[j, q // 2, q % 2] = piece[:, 512 * q - x0 : 512 * (q + 1) - x0]
-            src = mb[j][:].rearrange("p t k -> p (t k)")[:, x0:x1].bitcast(FP8)
-            if engine == "v":
-                nc.vector.tensor_copy(out=piece[:], in_=src)
-            elif engine == "g":
+        def widen(j, tiles, passes, engine, tag=None):
+            name = f"wide{j}_{tiles[0]}{passes[0]}"
+            piece = keep.tile([NP, len(tiles), len(passes), 512], BF16, name=name, tag=tag or name, align_bytes=64)
+            src = mb[j][:].rearrange("p t (c k) -> p t c k", c=NC)[:, tiles[0] : tiles[-1] + 1, passes[0] : passes[-1] + 1, :].bitcast(FP8)
+            words = piece[:].bitcast(F32)
+            for a, t in enumerate(tiles):
+                for b, c in enumerate(passes):
+                    for u in range(2):
+                        halves[j, t, c, u] = words[:, a, b, u:256:2] if engine == "g" else words[:, a, b, NP * u : NP * (u + 1)]
+            if engine == "g":
                 nc.gpsimd.tensor_copy(out=piece[:], in_=src)
+                return
+            dst = piece[:].rearrange("p t c (u m e) -> p (t c) u m e", u=2, m=NP, e=2)
+            src = src.rearrange("p t c (m u e) -> p (t c) u m e", u=2, m=NP, e=2)
+            if engine == "v":
+                nc.vector.tensor_copy(out=dst.rearrange("p q u m e -> p q m u e"), in_=src.rearrange("p q u m e -> p q m u e"))
             else:
-                nc.scalar.copy(out=piece[:], in_=src)
-
-        def turn(bk, tiles):
-            for t in range(2):
-                for u in range(2):
-                    nc.tensor.transpose(bk[:, u, 128 * t : 128 * t + 128], tiles[t][:, u:256:2], ident[:])
+                nc.scalar.copy(out=dst, in_=src)
 
         def turn_mask(j, c, tag):
             tbank[j, c] = psum.tile([NP, 2, 256], F32, name=f"tb{j}_{c}", tag=tag)
-            turn(tbank[j, c], [wide[j, t, c].bitcast(F32) for t in range(2)])
+            for t in range(2):
+                for u in range(2):
+                    nc.tensor.transpose(tbank[j, c][:, u, NP * t : NP * (t + 1)], halves[j, t, c, u], ident[:])
 
         def turn_scenes(h, c, tag):
             sbank[h, c] = psum.tile([NP, 2, 256], F32, name=f"sb{h}_{c}", tag=tag)
-            turn(sbank[h, c], [scn[h, c][:, t, :].bitcast(F32) for t in range(2)])
+            for t in range(2):
+                words = scn[h, c][:, t, :].bitcast(F32)
+                for u in range(2):
+                    nc.tensor.transpose(sbank[h, c][:, u, NP * t : NP * (t + 1)], words[:, u:256:2], ident[:])
 
         def empty_scenes(h, c):
             if h not in sq:
@@ -128,14 +135,14 @@ def tile_coded_aperture_backprojection_s13_kernel(
                 in_=sq[h][:].rearrange("p c x t -> p (c x t)"),
             )
 
-        def quant_input(j, c):
+        def quant_input(j, c, tag=None):
             if (j, c) not in qin:
-                qin[j, c] = keep.tile([NP, 256, 4], BF16, name=f"qin{j}{c}", tag="gated" if (j, c) in GATED else f"qin{j}{c}", align_bytes=64)
+                qin[j, c] = keep.tile([NP, 256, 4], BF16, name=f"qin{j}{c}", tag=tag or f"qin{j}{c}", align_bytes=64)
             return qin[j, c]
 
-        def product(j, c):
+        def product(j, c, tag=None):
             nc.vector.tensor_tensor(
-                out=quant_input(j, c)[:].rearrange("p x (u e) -> p x u e", u=2),
+                out=quant_input(j, c, tag)[:].rearrange("p x (u e) -> p x u e", u=2),
                 in0=mscale[:, c : c + 1].to_broadcast([NP, 256, 2, 2]),
                 in1=tbank[j, c][:].bitcast(BF16).rearrange("p u (x e) -> p x u e", e=2),
                 op=ALU.mult,
@@ -144,7 +151,7 @@ def tile_coded_aperture_backprojection_s13_kernel(
         def turn_first(t, c, tag):
             first[t, c] = psum.tile([NP, 2, NP], F32, name=f"first{t}_{c}", tag=tag)
             for u in range(2):
-                nc.tensor.transpose(first[t, c][:, u, :], wide[0, t, c].bitcast(F32)[:, u:256:2], ident[:])
+                nc.tensor.transpose(first[t, c][:, u, :], halves[0, t, c, u], ident[:])
 
         def product_first(t, c):
             nc.vector.tensor_tensor(
@@ -155,7 +162,7 @@ def tile_coded_aperture_backprojection_s13_kernel(
             )
 
         def product_planes(j, c):
-            planes[j, c] = keep.tile([NP, 4, 256], BF16, name=f"planes{j}_{c}",  align_bytes=64)
+            planes[j, c] = keep.tile([NP, 4, 256], BF16, name=f"planes{j}_{c}", align_bytes=64)
             src = tbank[j, c][:].bitcast(BF16).rearrange("p u (x e) -> p u e x", e=2)
             for u in range(2):
                 for e in range(2):
@@ -176,8 +183,8 @@ def tile_coded_aperture_backprojection_s13_kernel(
             else:
                 nc.scalar.copy(out=dst, in_=src)
 
-        def weave_planes(j, c, x0, x1, engine):
-            weave(quant_input(j, c)[:, x0:x1], planes[j, c][:, :, x0:x1], engine)
+        def weave_planes(j, c, engine, tag=None, x0=0, x1=256):
+            weave(quant_input(j, c, tag)[:, x0:x1], planes[j, c][:, :, x0:x1], engine)
 
         def quant_mask(j, passes=range(NC)):
             if j not in codes:
@@ -188,26 +195,26 @@ def tile_coded_aperture_backprojection_s13_kernel(
                     out=codes[j][:, c, :].bitcast(E4M3X4), scales=scales[j][:, c, :], in_=qin[j, c][:].rearrange("p x t -> p (x t)")
                 )
 
-        def project(j, h, tag):
+        def project(j, h, tag, order=(1, 0)):
             ybank[j, h] = psum.tile([NP, 2, H], F32, name=f"y{j}_{h}", tag=tag)
             for t in range(2):
-                cols = slice(128 * t, 128 * t + 128)
-                for c in range(NC):
+                cols = slice(NP * t, NP * (t + 1))
+                for c in order:
                     nc.tensor.matmul_mx(
                         out=ybank[j, h][:, t, :],
                         lhsT=codes[j][:, c, cols].bitcast(E4M3X4),
                         lhsT_scale=scales[j][:, c, cols],
                         rhs=scodes[h][:, c, :].bitcast(E4M3X4),
                         rhs_scale=sscales[h][:, c, :],
-                        start=(c == 0),
-                        stop=(c == NC - 1),
+                        start=(c == order[0]),
+                        stop=(c == order[-1]),
                     )
 
-        def whiten(j, h, tiles=range(2)):
+        def whiten(j, h):
             g, r = divmod(j, 2)
             if (g, h) not in zt:
                 zt[g, h] = keep.tile([NP, 4, H], BF16, name=f"zt{g}{h}", align_bytes=64)
-            for t in tiles:
+            for t in range(2):
                 s = 2 * r + t
                 nc.vector.scalar_tensor_tensor(
                     out=zt[g, h][:, s, :],
@@ -218,7 +225,7 @@ def tile_coded_aperture_backprojection_s13_kernel(
                     op1=ALU.mult,
                 )
 
-        def weave_z(g, h, x0, x1, engine, tag=None):
+        def weave_z(g, h, engine, tag=None, x0=0, x1=H):
             if (g, h) not in zq:
                 zq[g, h] = keep.tile([NP, H, 4], BF16, name=f"zq{g}{h}", tag=tag or f"zq{g}{h}", align_bytes=64)
             weave(zq[g, h][:, x0:x1, :], zt[g, h][:, :, x0:x1], engine)
@@ -248,29 +255,26 @@ def tile_coded_aperture_backprojection_s13_kernel(
 
         def emit(h, q, engine):
             tiles = IMG[h][q][1]
-            res[h, q] = keep.tile([NP, len(tiles), H], F32, name=f"res{h}{q}")
+            res = keep.tile([NP, len(tiles), H], F32, name=f"res{h}{q}")
             if engine == "v":
-                nc.vector.tensor_copy(out=res[h, q][:], in_=img[h, q][:])
+                nc.vector.tensor_copy(out=res[:], in_=img[h, q][:])
             else:
-                nc.scalar.copy(out=res[h, q][:], in_=img[h, q][:])
-            nc.sync.dma_start(out=out_rows[:, tiles[0] : tiles[-1] + 1, H * h : H * (h + 1)], in_=res[h, q][:])
+                nc.scalar.copy(out=res[:], in_=img[h, q][:])
+            nc.sync.dma_start(out=out_rows[:, tiles[0] : tiles[-1] + 1, H * h : H * (h + 1)], in_=res[:])
+
 
         load_tile(0, 0)
         load_mscale()
         load_tile(0, 1)
-        load_pair(1)
-        load_scenes(0, 0)
-        load_scenes(0, 1)
-        for j in range(2, 5):
+        for j in range(1, 6):
             load_pair(j)
+        load_scenes(0)
         load_darks()
         load_sig(0)
-        load_pair(5)
-        load_scenes(1, 0)
-        load_scenes(1, 1)
         load_pair(6)
-        load_pair(7)
         load_sig(1)
+        load_scenes(1)
+        load_pair(7)
         load_gscales()
         load_gwords(0)
         for g in range(2, NG):
@@ -278,146 +282,145 @@ def tile_coded_aperture_backprojection_s13_kernel(
             load_gwords(g - 1)
         load_gwords(NG - 1)
 
-        widen(0, 0, 512, "v")
-        widen(0, 512, 1024, "s")
+        widen(0, (0,), (0,), "v")
+        widen(0, (0,), (1,), "s")
         turn_first(0, 0, "y0")
         turn_first(0, 1, "y1")
-        widen(0, 1024, 1536, "s")
-        widen(0, 1536, 2048, "v")
+        widen(0, (1,), (0,), "s")
+        widen(0, (1,), (1,), "v")
         turn_first(1, 0, "t0")
         turn_first(1, 1, "t1")
-        widen(1, 0, 1024, "s")
-        widen(1, 1024, 2048, "s")
-        turn_scenes(0, 0, "a0")
+        widen(1, BOTH, (0,), "s")
+        widen(1, BOTH, (1,), "s")
         turn_mask(1, 0, "a2")
-        turn_scenes(0, 1, "a1")
         turn_mask(1, 1, "a3")
         for t, c in ((0, 0), (0, 1), (1, 0), (1, 1)):
             product_first(t, c)
-        empty_scenes(0, 0)
-        widen(2, 0, 1024, "s")
-        widen(2, 1024, 2048, "g")
-        empty_scenes(0, 1)
-        widen(3, 0, 2048, "s")
-        product(1, 0)
-        turn_mask(2, 0, "t0")
+        widen(2, BOTH, BOTH, "s")
+        widen(3, BOTH, BOTH, "g")
+        widen(4, (1,), BOTH, "s")
+        widen(4, (0,), BOTH, "g")
+        widen(5, BOTH, BOTH, "s")
         turn_mask(2, 1, "t1")
+        turn_mask(2, 0, "t0")
+        turn_scenes(0, 0, "a0")
+        turn_scenes(0, 1, "a1")
+        turn_mask(3, 1, "y1")
+        turn_mask(3, 0, "y0")
+        product(1, 0)
+        product(1, 1, "gate1")
+        product(2, 0)
+        turn_mask(4, 1, "a3")
+        turn_mask(4, 0, "a2")
+        product_planes(2, 1)
+        empty_scenes(0, 0)
+        empty_scenes(0, 1)
+        product_planes(3, 1)
+        product_planes(4, 1)
         quant_mask(0)
+        quant_mask(1, (0, 1))
         quant_scenes(0)
-        widen(4, 0, 2048, "g", "sq0")
-        project(0, 0, "y0")
-        product(1, 1)
-        turn_mask(3, 1, "a1")
-        turn_mask(3, 0, "a0")
-        widen(5, 0, 2048, "s")
+        weave_planes(2, 1, "g", "gate1")
+        weave_planes(3, 1, "g", "gate0")
+        project(0, 0, "a0")
+        project(1, 0, "a1")
+        turn_mask(5, 1, "t1")
+        turn_mask(5, 0, "t0")
+        widen(6, BOTH, BOTH, "s")
+        product_planes(5, 1)
+        product(3, 0)
+        product(4, 0)
         turn_scenes(1, 0, "a2")
         turn_scenes(1, 1, "a3")
-        product(2, 0)
         whiten(0, 0)
-        product_planes(3, 1)
-        quant_mask(1)
-        widen(7, 0, 1024, "g", "qin11")
-        project(1, 0, "y1")
-        turn_mask(4, 1, "y0")
-        turn_mask(4, 0, "t0")
-        empty_scenes(1, 0)
-        empty_scenes(1, 1)
-        product(2, 1)
         whiten(1, 0)
-        widen(6, 0, 2048, "s")
-        turn_mask(5, 1, "a1")
-        quant_scenes(1)
-        quant_mask(2)
-        weave_planes(3, 1, 0, 256, "g")
-        weave_z(0, 0, 0, H, "s")
-        project(0, 1, "y1")
-        project(2, 0, "a2")
-        turn_mask(6, 1, "t1")
-        product(3, 0)
-        product_planes(4, 1)
-        widen(7, 1024, 2048, "s")
-        whiten(0, 1)
-        whiten(2, 0)
-        turn_mask(7, 1, "a3")
-        quant_z(0, 0)
-        quant_mask(3)
-        weave_planes(4, 1, 0, 256, "g")
-        product_planes(5, 1)
-        backproject(0, 0, [0])
-        project(1, 1, "y0")
+        weave_z(0, 0, "s")
+        widen(7, BOTH, BOTH, "s")
+        quant_mask(2, (1, 0))
+        quant_mask(3, (1, 0))
+        weave_planes(4, 1, "g", "gate0")
+        project(2, 0, "y0")
         project(3, 0, "y1")
-        backproject(0, 0, [2, 1])
-        product(4, 0)
-        product_planes(6, 1)
-        turn_mask(5, 0, "t0")
-        turn_mask(7, 0, "t1")
-        whiten(1, 1)
-        whiten(3, 0)
-        product_planes(7, 1)
-        weave_z(1, 0, 0, H, "s")
-        quant_mask(4)
-        weave_planes(5, 1, 0, 256, "g")
-        project(4, 0, "y0")
-        project(2, 1, "y1")
-        backproject(0, 0, [3])
         product(5, 0)
+        turn_mask(6, 1, "t1")
         turn_mask(6, 0, "t0")
-        whiten(4, 0)
-        product_planes(7, 0)
-        weave_planes(7, 1, 0, 256, "s")
-        quant_z(1, 0)
-        quant_mask(5)
-        weave_planes(6, 1, 0, 256, "g")
-        backproject(1, 0, [0, 1])
-        project(5, 0, "y0")
-        backproject(1, 0, [2, 3])
-        project(3, 1, "t1")
-        weave_planes(7, 0, 0, 256, "s")
+        whiten(2, 0)
+        quant_z(0, 0)
+        backproject(0, 0, [0, 1])
+        whiten(3, 0)
+        empty_scenes(1, 0)
+        weave_z(1, 0, "s")
+        empty_scenes(1, 1)
+        product_planes(6, 1)
+        turn_mask(7, 1, "y1")
+        quant_mask(4, (1, 0))
+        weave_planes(5, 1, "g", "gate0")
+        project(4, 0, "y0")
+        backproject(0, 0, [2])
         product(6, 0)
+        turn_mask(7, 0, "t0")
+        backproject(0, 0, [3])
+        whiten(4, 0)
+        product_planes(7, 1)
+        weave_planes(7, 1, "s")
+        quant_z(1, 0)
+        quant_mask(5, (0, 1))
+        quant_scenes(1)
+        weave_planes(6, 1, "g", "gate0")
+        backproject(1, 0, [0, 1])
+        project(5, 0, "y0", (0, 1))
+        project(0, 1, "t1")
+        project(2, 1, "y1")
+        product(7, 0)
         whiten(5, 0)
-        whiten(2, 1)
-        weave_z(2, 0, 0, H, "s")
-        project(4, 1, "y0")
-        quant_mask(6)
-        quant_mask(7)
+        whiten(0, 1)
+        project(1, 1, "t0")
+        backproject(1, 0, [2, 3])
+        quant_mask(6, (0, 1))
+        quant_mask(7, (1, 0))
+        weave_z(2, 0, "s")
+        project(6, 0, "y0", (0, 1))
+        project(7, 0, "t1")
+        whiten(1, 1)
+        project(3, 1, "t0")
         quant_z(2, 0)
-        weave_z(0, 1, 0, H, "g", "zq20")
-        project(6, 0, "y1")
-        project(7, 0, "t0")
-        backproject(2, 0, range(4))
-        whiten(3, 1)
-        weave_z(1, 1, 0, H, "s")
-        project(5, 1, "t1")
+        weave_z(0, 1, "g", "zq20")
         whiten(6, 0)
-        project(6, 1, "y1")
+        backproject(2, 0, [0, 1])
+        project(4, 1, "y0")
         whiten(7, 0)
-        weave_z(3, 0, 160, H, "s")
-        whiten(4, 1)
-        project(7, 1, "y0")
-        weave_z(3, 0, 0, 160, "v")
+        weave_z(3, 0, "s", x0=64)
+        whiten(2, 1)
+        backproject(2, 0, [2, 3])
+        project(5, 1, "t1")
+        project(6, 1, "y1")
+        whiten(3, 1)
+        weave_z(1, 1, "s")
+        weave_z(3, 0, "v", x1=64)
         quant_z(0, 1)
         quant_z(3, 0)
-        quant_z(1, 1)
-        backproject(0, 1, [0])
-        backproject(3, 0, range(4))
-        backproject(1, 1, [0])
+        backproject(3, 0, [0, 1])
+        project(7, 1, "t0")
+        backproject(3, 0, [2, 3])
+        whiten(4, 1)
         whiten(5, 1)
-        emit(0, 0, "s")
-        weave_z(2, 1, 0, 128, "g")
-        weave_z(2, 1, 128, H, "s")
+        for q in range(4):
+            emit(0, q, "s")
+        quant_z(1, 1)
+        weave_z(2, 1, "g", "zq11", x1=160)
         whiten(6, 1)
-        emit(0, 1, "s")
         whiten(7, 1)
-        weave_z(3, 1, 192, H, "s")
-        emit(0, 2, "s")
-        weave_z(3, 1, 0, 192, "v")
+        weave_z(2, 1, "v", x0=160)
+        weave_z(3, 1, "v")
+        for q in range(5):
+            backproject(0, 1, [q])
+            if q < 3:
+                backproject(1, 1, [q])
         quant_z(2, 1)
         quant_z(3, 1)
-        emit(0, 3, "v")
-        for q in range(1, 5):
-            backproject(0, 1, [q])
-            backproject(1, 1, [q])
+        backproject(2, 1, [0, 1])
         for q in range(5):
-            backproject(2, 1, [q])
-            backproject(3, 1, [q])
-            emit(1, q, "sv"[q % 2])
+            for g in range(1, NG):
+                if g == 3 or (g == 2 and q > 1) or (g == 1 and q > 2):
+                    backproject(g, 1, [q])
+            emit(1, q, "vs"[q % 2])

@@ -22,9 +22,14 @@ NG = D // 512
 NPAIR = 2 * NG
 NC = P // 512
 H = B // 2
+UNIT = 1024
+RING, ZRING = 6, 6
+PART = {(0, 0): 0, (0, 1): 1, (1, 0): 2, (1, 1): 3, (2, 1): 3, (2, 0): 4, (3, 0): 1, (3, 1): 2, (4, 1): 4, (4, 0): 5,
+        (5, 0): 3, (5, 1): 4, (6, 1): 3, (6, 0): 2, (7, 0): 0, (7, 1): 1}
+ZPART = {(0, 0): 2, (1, 0): 3, (2, 0): 2, (0, 1): 0, (3, 0): 1, (1, 1): 3, (2, 1): 4, (3, 1): 5}
 IMG = [
     [("a0", (0, 1)), ("a1", (2, 3)), ("a2", (4, 5)), ("a3", (6, 7))],
-    [("y0", (0,)), ("t1", (1, 2)), ("y1", (3, 4)), ("a0", (5, 6)), ("t0", (7,))],
+    [("y1", (0,)), ("y0", (1, 2)), ("t1", (3, 4)), ("a0", (5,)), ("t0", (6,)), ("a1", (7,))],
 ]
 BOTH = (0, 1)
 
@@ -84,8 +89,8 @@ def tile_coded_aperture_backprojection_s13_kernel(
         def load_gwords(g):
             nc.sync.dma_start(out=gw[g][:].bitcast(I32), in_=dec_words[g].bitcast(I32))
 
-        halves, tbank, qin, planes, codes, scales, ybank, zt, zq, zcodes, zscales, img, sbank, first, sq, scodes, sscales = (
-            {} for i in range(17)
+        halves, tbank, planes, codes, scales, ybank, zt, zcodes, zscales, img, sbank, first, sq, scodes, sscales = (
+            {} for i in range(15)
         )
 
         def widen(j, tiles, passes, engine, tag=None):
@@ -135,14 +140,31 @@ def tile_coded_aperture_backprojection_s13_kernel(
                 in_=sq[h][:].rearrange("p c x t -> p (c x t)"),
             )
 
-        def quant_input(j, c, tag=None):
-            if (j, c) not in qin:
-                qin[j, c] = keep.tile([NP, 256, 4], BF16, name=f"qin{j}{c}", tag=tag or f"qin{j}{c}", align_bytes=64)
-            return qin[j, c]
+        ring = keep.tile([NP, RING * UNIT], BF16, name="ring", align_bytes=64)
+        zring = keep.tile([NP, ZRING * UNIT], BF16, name="zring", align_bytes=64)
 
-        def product(j, c, tag=None):
+        def quant_input(j, c):
+            part = PART[j, c]
+            return ring[:, UNIT * part : UNIT * (part + 1)].rearrange("p (x t) -> p x t", t=4)
+
+        def z_input(g, h):
+            part = ZPART[g, h]
+            return zring[:, UNIT * part : UNIT * (part + 1)].rearrange("p (x t) -> p x t", t=4)
+
+        def quantise(buf, parts, keys, name, codes_of, scales_of):
+            keys = sorted(keys, key=parts.get)
+            n, lo = len(keys), parts[keys[0]]
+            assert [parts[k] for k in keys] == list(range(lo, lo + n))
+            words = keep.tile([NP, n * 256], U32, name=f"codes_{name}", align_bytes=64)
+            plane = keep.tile([NP, n * 256], U8, name=f"scales_{name}", align_bytes=64)
+            nc.vector.quantize_mx(out=words[:].bitcast(E4M3X4), scales=plane[:], in_=buf[:, UNIT * lo : UNIT * (lo + n)])
+            for i, k in enumerate(keys):
+                codes_of[k] = words[:, 256 * i : 256 * (i + 1)]
+                scales_of[k] = plane[:, 256 * i : 256 * (i + 1)]
+
+        def product(j, c):
             nc.vector.tensor_tensor(
-                out=quant_input(j, c, tag)[:].rearrange("p x (u e) -> p x u e", u=2),
+                out=quant_input(j, c).rearrange("p x (u e) -> p x u e", u=2),
                 in0=mscale[:, c : c + 1].to_broadcast([NP, 256, 2, 2]),
                 in1=tbank[j, c][:].bitcast(BF16).rearrange("p u (x e) -> p x u e", e=2),
                 op=ALU.mult,
@@ -183,17 +205,11 @@ def tile_coded_aperture_backprojection_s13_kernel(
             else:
                 nc.scalar.copy(out=dst, in_=src)
 
-        def weave_planes(j, c, engine, tag=None, x0=0, x1=256):
-            weave(quant_input(j, c, tag)[:, x0:x1], planes[j, c][:, :, x0:x1], engine)
+        def weave_planes(j, c, engine, x0=0, x1=256):
+            weave(quant_input(j, c)[:, x0:x1], planes[j, c][:, :, x0:x1], engine)
 
-        def quant_mask(j, passes=range(NC)):
-            if j not in codes:
-                codes[j] = keep.tile([NP, NC, 256], U32, name=f"codes{j}", align_bytes=64)
-                scales[j] = keep.tile([NP, NC, 256], U8, name=f"scales{j}", align_bytes=64)
-            for c in passes:
-                nc.vector.quantize_mx(
-                    out=codes[j][:, c, :].bitcast(E4M3X4), scales=scales[j][:, c, :], in_=qin[j, c][:].rearrange("p x t -> p (x t)")
-                )
+        def quant_mask(*units):
+            quantise(ring, PART, units, f"mask{units[0][0]}{units[0][1]}", codes, scales)
 
         def project(j, h, tag, order=(1, 0)):
             ybank[j, h] = psum.tile([NP, 2, H], F32, name=f"y{j}_{h}", tag=tag)
@@ -202,8 +218,8 @@ def tile_coded_aperture_backprojection_s13_kernel(
                 for c in order:
                     nc.tensor.matmul_mx(
                         out=ybank[j, h][:, t, :],
-                        lhsT=codes[j][:, c, cols].bitcast(E4M3X4),
-                        lhsT_scale=scales[j][:, c, cols],
+                        lhsT=codes[j, c][:, cols].bitcast(E4M3X4),
+                        lhsT_scale=scales[j, c][:, cols],
                         rhs=scodes[h][:, c, :].bitcast(E4M3X4),
                         rhs_scale=sscales[h][:, c, :],
                         start=(c == order[0]),
@@ -225,17 +241,11 @@ def tile_coded_aperture_backprojection_s13_kernel(
                     op1=ALU.mult,
                 )
 
-        def weave_z(g, h, engine, tag=None, x0=0, x1=H):
-            if (g, h) not in zq:
-                zq[g, h] = keep.tile([NP, H, 4], BF16, name=f"zq{g}{h}", tag=tag or f"zq{g}{h}", align_bytes=64)
-            weave(zq[g, h][:, x0:x1, :], zt[g, h][:, :, x0:x1], engine)
+        def weave_z(g, h, engine, x0=0, x1=H):
+            weave(z_input(g, h)[:, x0:x1, :], zt[g, h][:, :, x0:x1], engine)
 
-        def quant_z(g, h):
-            zcodes[g, h] = keep.tile([NP, H], U32, name=f"zcodes{g}{h}", align_bytes=64)
-            zscales[g, h] = keep.tile([NP, H], U8, name=f"zscales{g}{h}", align_bytes=64)
-            nc.vector.quantize_mx(
-                out=zcodes[g, h][:].bitcast(E4M3X4), scales=zscales[g, h][:], in_=zq[g, h][:].rearrange("p b t -> p (b t)")
-            )
+        def quant_z(*keys):
+            quantise(zring, ZPART, keys, f"z{keys[0][0]}{keys[0][1]}", zcodes, zscales)
 
         def backproject(g, h, banks):
             for q in banks:
@@ -247,8 +257,8 @@ def tile_coded_aperture_backprojection_s13_kernel(
                         out=img[h, q][:, i, :],
                         lhsT=gw[g][:, 256 * m : 256 * (m + 1)].bitcast(E2M1X4),
                         lhsT_scale=gsc[:, g, 128 * m : 128 * (m + 1)],
-                        rhs=zcodes[g, h][:].bitcast(E4M3X4),
-                        rhs_scale=zscales[g, h][:],
+                        rhs=zcodes[g, h].bitcast(E4M3X4),
+                        rhs_scale=zscales[g, h],
                         start=(g == 0 and i == 0),
                         stop=(g == NG - 1 and i == len(tiles) - 1),
                     )
@@ -308,7 +318,7 @@ def tile_coded_aperture_backprojection_s13_kernel(
         turn_mask(3, 1, "y1")
         turn_mask(3, 0, "y0")
         product(1, 0)
-        product(1, 1, "gate1")
+        product(1, 1)
         product(2, 0)
         turn_mask(4, 1, "a3")
         turn_mask(4, 0, "a2")
@@ -317,17 +327,16 @@ def tile_coded_aperture_backprojection_s13_kernel(
         empty_scenes(0, 1)
         product_planes(3, 1)
         product_planes(4, 1)
-        quant_mask(0)
-        quant_mask(1, (0, 1))
+        quant_mask((0, 0), (0, 1), (1, 0), (1, 1))
         quant_scenes(0)
-        weave_planes(2, 1, "g", "gate1")
-        weave_planes(3, 1, "g", "gate0")
+        weave_planes(2, 1, "g")
+        weave_planes(3, 1, "g")
         project(0, 0, "a0")
         project(1, 0, "a1")
         turn_mask(5, 1, "t1")
         turn_mask(5, 0, "t0")
         widen(6, BOTH, BOTH, "s")
-        product_planes(5, 1)
+        widen(7, BOTH, BOTH, "s")
         product(3, 0)
         product(4, 0)
         turn_scenes(1, 0, "a2")
@@ -335,40 +344,40 @@ def tile_coded_aperture_backprojection_s13_kernel(
         whiten(0, 0)
         whiten(1, 0)
         weave_z(0, 0, "s")
-        widen(7, BOTH, BOTH, "s")
-        quant_mask(2, (1, 0))
-        quant_mask(3, (1, 0))
-        weave_planes(4, 1, "g", "gate0")
+        product_planes(5, 1)
+        quant_mask((2, 0), (2, 1))
+        quant_mask((3, 0), (3, 1))
+        weave_planes(4, 1, "g")
         project(2, 0, "y0")
         project(3, 0, "y1")
         product(5, 0)
-        turn_mask(6, 1, "t1")
         turn_mask(6, 0, "t0")
+        turn_mask(6, 1, "t1")
         whiten(2, 0)
-        quant_z(0, 0)
+        quant_z((0, 0))
         backproject(0, 0, [0, 1])
         whiten(3, 0)
         empty_scenes(1, 0)
-        weave_z(1, 0, "s")
         empty_scenes(1, 1)
+        weave_z(1, 0, "s")
         product_planes(6, 1)
-        turn_mask(7, 1, "y1")
-        quant_mask(4, (1, 0))
-        weave_planes(5, 1, "g", "gate0")
+        quant_mask((4, 1))
+        quant_mask((4, 0))
+        weave_planes(5, 1, "g")
         project(4, 0, "y0")
-        backproject(0, 0, [2])
+        backproject(0, 0, [2, 3])
         product(6, 0)
+        turn_mask(7, 1, "y1")
         turn_mask(7, 0, "t0")
-        backproject(0, 0, [3])
         whiten(4, 0)
         product_planes(7, 1)
         weave_planes(7, 1, "s")
-        quant_z(1, 0)
-        quant_mask(5, (0, 1))
+        quant_z((1, 0))
+        quant_mask((5, 0), (5, 1))
         quant_scenes(1)
-        weave_planes(6, 1, "g", "gate0")
+        weave_planes(6, 1, "g")
         backproject(1, 0, [0, 1])
-        project(5, 0, "y0", (0, 1))
+        project(5, 0, "y0")
         project(0, 1, "t1")
         project(2, 1, "y1")
         product(7, 0)
@@ -376,51 +385,50 @@ def tile_coded_aperture_backprojection_s13_kernel(
         whiten(0, 1)
         project(1, 1, "t0")
         backproject(1, 0, [2, 3])
-        quant_mask(6, (0, 1))
-        quant_mask(7, (1, 0))
+        quant_mask((6, 0), (6, 1))
+        quant_mask((7, 0), (7, 1))
         weave_z(2, 0, "s")
-        project(6, 0, "y0", (0, 1))
+        project(6, 0, "y0")
         project(7, 0, "t1")
         whiten(1, 1)
         project(3, 1, "t0")
-        quant_z(2, 0)
-        weave_z(0, 1, "g", "zq20")
+        quant_z((2, 0))
+        weave_z(0, 1, "s")
         whiten(6, 0)
         backproject(2, 0, [0, 1])
         project(4, 1, "y0")
         whiten(7, 0)
-        weave_z(3, 0, "s", x0=64)
+        weave_z(3, 0, "g", x1=96)
+        weave_z(3, 0, "s", x0=96)
         whiten(2, 1)
         backproject(2, 0, [2, 3])
         project(5, 1, "t1")
         project(6, 1, "y1")
         whiten(3, 1)
         weave_z(1, 1, "s")
-        weave_z(3, 0, "v", x1=64)
-        quant_z(0, 1)
-        quant_z(3, 0)
+        quant_z((0, 1), (3, 0))
+        whiten(4, 1)
         backproject(3, 0, [0, 1])
         project(7, 1, "t0")
         backproject(3, 0, [2, 3])
-        whiten(4, 1)
         whiten(5, 1)
-        for q in range(4):
-            emit(0, q, "s")
-        quant_z(1, 1)
-        weave_z(2, 1, "g", "zq11", x1=160)
+        weave_z(2, 1, "g", x1=128)
+        emit(0, 0, "s")
+        emit(0, 1, "s")
+        weave_z(2, 1, "s", x0=128)
+        emit(0, 2, "s")
+        emit(0, 3, "s")
         whiten(6, 1)
         whiten(7, 1)
-        weave_z(2, 1, "v", x0=160)
+        quant_z((1, 1))
         weave_z(3, 1, "v")
-        for q in range(5):
-            backproject(0, 1, [q])
-            if q < 3:
-                backproject(1, 1, [q])
-        quant_z(2, 1)
-        quant_z(3, 1)
+        quant_z((2, 1))
+        quant_z((3, 1))
+        backproject(0, 1, [1, 2, 0, 3, 4])
+        backproject(1, 1, [0, 1, 2])
         backproject(2, 1, [0, 1])
-        for q in range(5):
-            for g in range(1, NG):
-                if g == 3 or (g == 2 and q > 1) or (g == 1 and q > 2):
+        for q in range(6):
+            for g in range(NG):
+                if g == 3 or (g == 2 and q > 1) or (g == 1 and q > 2) or q > 4:
                     backproject(g, 1, [q])
             emit(1, q, "vs"[q % 2])

@@ -28,10 +28,13 @@ PART = {(0, 0): 0, (0, 1): 1, (1, 0): 2, (1, 1): 3, (2, 1): 3, (2, 0): 4, (3, 0)
         (5, 0): 3, (5, 1): 4, (6, 1): 3, (6, 0): 2, (7, 0): 0, (7, 1): 1}
 ZPART = {(0, 0): 2, (1, 0): 3, (2, 0): 2, (0, 1): 0, (3, 0): 1, (1, 1): 3, (2, 1): 4, (3, 1): 5}
 IMG = [
-    [("a0", (0, 1)), ("a1", (2, 3)), ("a2", (4, 5)), ("a3", (6, 7))],
-    [("y1", (0,)), ("y0", (1, 2)), ("t1", (3, 4)), ("a0", (5,)), ("t0", (6,)), ("a1", (7,))],
+    [("a0", (0, 1), 0, H), ("a1", (2, 3), 0, H), ("a2", (4, 5), 0, H), ("a3", (6, 7), 0, H)],
+    [("y1", (0,), 0, H), ("y0", (1, 2), 0, H), ("t1", (3, 4), 0, H), ("a0", (5,), 0, H), ("t0", (6,), 0, H),
+     ("a1", (7,), 0, H // 2), ("a2", (7,), H // 2, H)],
 ]
 BOTH = (0, 1)
+GX = 224
+GZ = 96
 
 
 def tile_coded_aperture_backprojection_s13_kernel(
@@ -249,34 +252,35 @@ def tile_coded_aperture_backprojection_s13_kernel(
 
         def backproject(g, h, banks):
             for q in banks:
-                tag, tiles = IMG[h][q]
+                tag, tiles, x0, x1 = IMG[h][q]
                 if g == 0:
-                    img[h, q] = psum.tile([NP, len(tiles), H], F32, name=f"img{h}{q}", tag=tag)
+                    img[h, q] = psum.tile([NP, len(tiles), x1 - x0], F32, name=f"img{h}{q}", tag=tag)
                 for i, m in enumerate(tiles):
                     nc.tensor.matmul_mx(
                         out=img[h, q][:, i, :],
                         lhsT=gw[g][:, 256 * m : 256 * (m + 1)].bitcast(E2M1X4),
                         lhsT_scale=gsc[:, g, 128 * m : 128 * (m + 1)],
-                        rhs=zcodes[g, h].bitcast(E4M3X4),
-                        rhs_scale=zscales[g, h],
+                        rhs=zcodes[g, h][:, x0:x1].bitcast(E4M3X4),
+                        rhs_scale=zscales[g, h][:, x0:x1],
                         start=(g == 0 and i == 0),
                         stop=(g == NG - 1 and i == len(tiles) - 1),
                     )
 
         def emit(h, q, engine):
-            tiles = IMG[h][q][1]
-            res = keep.tile([NP, len(tiles), H], F32, name=f"res{h}{q}")
+            tag, tiles, x0, x1 = IMG[h][q]
+            res = keep.tile([NP, len(tiles), x1 - x0], F32, name=f"res{h}{q}")
             if engine == "v":
                 nc.vector.tensor_copy(out=res[:], in_=img[h, q][:])
             else:
                 nc.scalar.copy(out=res[:], in_=img[h, q][:])
-            nc.sync.dma_start(out=out_rows[:, tiles[0] : tiles[-1] + 1, H * h : H * (h + 1)], in_=res[:])
+            nc.sync.dma_start(out=out_rows[:, tiles[0] : tiles[-1] + 1, H * h + x0 : H * h + x1], in_=res[:])
 
 
         load_tile(0, 0)
-        load_mscale()
         load_tile(0, 1)
-        for j in range(1, 6):
+        load_pair(1)
+        load_mscale()
+        for j in (2, 4, 3, 5):
             load_pair(j)
         load_scenes(0)
         load_darks()
@@ -300,37 +304,40 @@ def tile_coded_aperture_backprojection_s13_kernel(
         widen(0, (1,), (1,), "v")
         turn_first(1, 0, "t0")
         turn_first(1, 1, "t1")
-        widen(1, BOTH, (0,), "s")
+        widen(1, (0,), (0,), "v")
+        widen(1, (1,), (0,), "s")
         widen(1, BOTH, (1,), "s")
         turn_mask(1, 0, "a2")
         turn_mask(1, 1, "a3")
         for t, c in ((0, 0), (0, 1), (1, 0), (1, 1)):
             product_first(t, c)
-        widen(2, BOTH, BOTH, "s")
+        widen(2, (0,), BOTH, "s")
+        widen(2, (1,), BOTH, "g")
         widen(3, BOTH, BOTH, "g")
-        widen(4, (1,), BOTH, "s")
-        widen(4, (0,), BOTH, "g")
+        widen(4, BOTH, BOTH, "s")
         widen(5, BOTH, BOTH, "s")
-        turn_mask(2, 1, "t1")
+        turn_mask(2, 1, "a1")
         turn_mask(2, 0, "t0")
         turn_scenes(0, 0, "a0")
-        turn_scenes(0, 1, "a1")
-        turn_mask(3, 1, "y1")
-        turn_mask(3, 0, "y0")
+        turn_scenes(0, 1, "t1")
         product(1, 0)
         product(1, 1)
         product(2, 0)
         turn_mask(4, 1, "a3")
+        turn_mask(3, 1, "y1")
+        turn_mask(3, 0, "y0")
         turn_mask(4, 0, "a2")
         product_planes(2, 1)
         empty_scenes(0, 0)
         empty_scenes(0, 1)
-        product_planes(3, 1)
         product_planes(4, 1)
         quant_mask((0, 0), (0, 1), (1, 0), (1, 1))
         quant_scenes(0)
-        weave_planes(2, 1, "g")
-        weave_planes(3, 1, "g")
+        weave_planes(2, 1, "g", x1=GX)
+        product_planes(3, 1)
+        weave_planes(3, 1, "g", x1=GX)
+        weave_planes(2, 1, "s", x0=GX)
+        weave_planes(3, 1, "s", x0=GX)
         project(0, 0, "a0")
         project(1, 0, "a1")
         turn_mask(5, 1, "t1")
@@ -344,31 +351,33 @@ def tile_coded_aperture_backprojection_s13_kernel(
         whiten(0, 0)
         whiten(1, 0)
         weave_z(0, 0, "s")
-        product_planes(5, 1)
         quant_mask((2, 0), (2, 1))
         quant_mask((3, 0), (3, 1))
-        weave_planes(4, 1, "g")
+        weave_planes(4, 1, "g", x1=GX)
+        weave_planes(4, 1, "s", x0=GX)
+        empty_scenes(1, 0)
+        product_planes(5, 1)
+        empty_scenes(1, 1)
         project(2, 0, "y0")
         project(3, 0, "y1")
         product(5, 0)
         turn_mask(6, 0, "t0")
-        turn_mask(6, 1, "t1")
         whiten(2, 0)
         quant_z((0, 0))
-        backproject(0, 0, [0, 1])
+        backproject(0, 0, [0, 1, 2])
         whiten(3, 0)
-        empty_scenes(1, 0)
-        empty_scenes(1, 1)
         weave_z(1, 0, "s")
-        product_planes(6, 1)
         quant_mask((4, 1))
         quant_mask((4, 0))
-        weave_planes(5, 1, "g")
+        weave_planes(5, 1, "g", x1=GX)
+        weave_planes(5, 1, "s", x0=GX)
         project(4, 0, "y0")
-        backproject(0, 0, [2, 3])
+        turn_mask(6, 1, "t1")
+        product_planes(6, 1)
         product(6, 0)
         turn_mask(7, 1, "y1")
         turn_mask(7, 0, "t0")
+        backproject(0, 0, [3])
         whiten(4, 0)
         product_planes(7, 1)
         weave_planes(7, 1, "s")
@@ -398,26 +407,22 @@ def tile_coded_aperture_backprojection_s13_kernel(
         backproject(2, 0, [0, 1])
         project(4, 1, "y0")
         whiten(7, 0)
-        weave_z(3, 0, "g", x1=96)
-        weave_z(3, 0, "s", x0=96)
+        weave_z(3, 0, "s")
         whiten(2, 1)
         backproject(2, 0, [2, 3])
         project(5, 1, "t1")
         project(6, 1, "y1")
         whiten(3, 1)
         weave_z(1, 1, "s")
-        quant_z((0, 1), (3, 0))
         whiten(4, 1)
-        backproject(3, 0, [0, 1])
+        quant_z((0, 1), (3, 0))
         project(7, 1, "t0")
-        backproject(3, 0, [2, 3])
+        backproject(3, 0, range(4))
         whiten(5, 1)
-        weave_z(2, 1, "g", x1=128)
-        emit(0, 0, "s")
-        emit(0, 1, "s")
-        weave_z(2, 1, "s", x0=128)
-        emit(0, 2, "s")
-        emit(0, 3, "s")
+        weave_z(2, 1, "g", x1=GZ)
+        weave_z(2, 1, "s", x0=GZ)
+        for q in range(4):
+            emit(0, q, "s")
         whiten(6, 1)
         whiten(7, 1)
         quant_z((1, 1))
@@ -425,10 +430,10 @@ def tile_coded_aperture_backprojection_s13_kernel(
         quant_z((2, 1))
         quant_z((3, 1))
         backproject(0, 1, [1, 2, 0, 3, 4])
-        backproject(1, 1, [0, 1, 2])
+        backproject(1, 1, [0, 1])
         backproject(2, 1, [0, 1])
-        for q in range(6):
+        for q in range(7):
             for g in range(NG):
-                if g == 3 or (g == 2 and q > 1) or (g == 1 and q > 2) or q > 4:
+                if g == 3 or (g > 0 and q > 1) or q > 4:
                     backproject(g, 1, [q])
             emit(1, q, "vs"[q % 2])

@@ -30,11 +30,10 @@ ZPART = {(0, 0): 2, (1, 0): 3, (2, 0): 2, (0, 1): 0, (3, 0): 1, (1, 1): 3, (2, 1
 IMG = [
     [("a0", (0, 1), 0, H), ("a1", (2, 3), 0, H), ("a2", (4, 5), 0, H), ("a3", (6, 7), 0, H)],
     [("y1", (0,), 0, H), ("y0", (1, 2), 0, H), ("t1", (3, 4), 0, H), ("a0", (5,), 0, H), ("t0", (6,), 0, H),
-     ("a1", (7,), 0, H // 2), ("a2", (7,), H // 2, H)],
+     ("a1", (7,), 0, H)],
 ]
 BOTH = (0, 1)
 GX = 224
-GZ = 96
 
 
 def tile_coded_aperture_backprojection_s13_kernel(
@@ -277,9 +276,9 @@ def tile_coded_aperture_backprojection_s13_kernel(
 
 
         load_tile(0, 0)
+        load_mscale()
         load_tile(0, 1)
         load_pair(1)
-        load_mscale()
         for j in (2, 4, 3, 5):
             load_pair(j)
         load_scenes(0)
@@ -304,8 +303,7 @@ def tile_coded_aperture_backprojection_s13_kernel(
         widen(0, (1,), (1,), "v")
         turn_first(1, 0, "t0")
         turn_first(1, 1, "t1")
-        widen(1, (0,), (0,), "v")
-        widen(1, (1,), (0,), "s")
+        widen(1, BOTH, (0,), "s")
         widen(1, BOTH, (1,), "s")
         turn_mask(1, 0, "a2")
         turn_mask(1, 1, "a3")
@@ -407,22 +405,26 @@ def tile_coded_aperture_backprojection_s13_kernel(
         backproject(2, 0, [0, 1])
         project(4, 1, "y0")
         whiten(7, 0)
-        weave_z(3, 0, "s")
+        weave_z(3, 0, "g", x1=96)
+        weave_z(3, 0, "s", x0=96)
         whiten(2, 1)
         backproject(2, 0, [2, 3])
         project(5, 1, "t1")
         project(6, 1, "y1")
         whiten(3, 1)
         weave_z(1, 1, "s")
-        whiten(4, 1)
         quant_z((0, 1), (3, 0))
+        whiten(4, 1)
+        backproject(3, 0, [0, 1])
         project(7, 1, "t0")
-        backproject(3, 0, range(4))
+        backproject(3, 0, [2, 3])
         whiten(5, 1)
-        weave_z(2, 1, "g", x1=GZ)
-        weave_z(2, 1, "s", x0=GZ)
-        for q in range(4):
-            emit(0, q, "s")
+        weave_z(2, 1, "g", x1=128)
+        emit(0, 0, "s")
+        emit(0, 1, "s")
+        weave_z(2, 1, "s", x0=128)
+        emit(0, 2, "s")
+        emit(0, 3, "s")
         whiten(6, 1)
         whiten(7, 1)
         quant_z((1, 1))
@@ -430,10 +432,10 @@ def tile_coded_aperture_backprojection_s13_kernel(
         quant_z((2, 1))
         quant_z((3, 1))
         backproject(0, 1, [1, 2, 0, 3, 4])
-        backproject(1, 1, [0, 1])
+        backproject(1, 1, range(3))
         backproject(2, 1, [0, 1])
-        for q in range(7):
+        for q in range(len(IMG[1])):
             for g in range(NG):
-                if g == 3 or (g > 0 and q > 1) or q > 4:
+                if g == 3 or (g == 2 and q > 1) or (g == 1 and q >= 3) or q > 4:
                     backproject(g, 1, [q])
             emit(1, q, "vs"[q % 2])

@@ -49,8 +49,10 @@ def tile_coded_aperture_backprojection_s13_kernel(
         scn_v = scenes.rearrange("(h t p) (c k) -> h c p t k", h=2, t=2, p=NP, c=NC)
         out_rows = out.rearrange("(m p) b -> p m b", p=NP)
 
-        mscale = keep.tile([NP, NC, 2, 2], F32, name="mscale")
-        darks = keep.tile([NP, NG, 4], BF16, name="darks")
+        mscale_rows = keep.tile([NP, NC, 8], F32, name="mscale")
+        mscale = mscale_rows[:, :, 0:4].rearrange("p c (u e) -> p c u e", u=2)
+        dark_rows = keep.tile([NP, NG, 16], BF16, name="darks")
+        darks = dark_rows[:, :, 0:4]
         ident = keep.tile([NP, NP], F32, name="ident")
         gsc = keep.tile([NP, NG, P], U8, name="gsc", align_bytes=64)
         mb = [keep.tile([NP, 2, P], U8, name=f"mb{j}", align_bytes=64) for j in range(NPAIR)]
@@ -69,14 +71,14 @@ def tile_coded_aperture_backprojection_s13_kernel(
             nc.sync.dma_start(out=mb[j][:, t, :], in_=mask_v[g][:, 2 * r + t, :])
 
         def load_mscale():
-            nc.sync.dma_start(out=mscale[:], in_=mask_scale.rearrange("o (c p u e) -> p (o c) u e", c=NC, p=NP, u=2, e=2))
+            nc.sync.dma_start(out=mscale, in_=mask_scale.rearrange("o (c p u e) -> p (o c) u e", c=NC, p=NP, u=2, e=2))
 
         def load_scenes(h):
             for c in range(NC):
                 nc.sync.dma_start(out=scn[h, c][:], in_=scn_v[h, c])
 
         def load_darks():
-            nc.sync.dma_start(out=darks[:], in_=dark.rearrange("(g p t) -> p g t", g=NG, p=NP, t=4))
+            nc.sync.dma_start(out=darks, in_=dark.rearrange("(g p t) -> p g t", g=NG, p=NP, t=4))
 
         def load_sig(g):
             nc.sync.dma_start(out=sig[g][:], in_=sig_v[g])

@@ -29,8 +29,7 @@ PART = {(0, 0): 0, (0, 1): 1, (1, 0): 2, (1, 1): 3, (2, 1): 3, (2, 0): 4, (3, 0)
 ZPART = {(0, 0): 2, (1, 0): 3, (2, 0): 2, (0, 1): 0, (3, 0): 1, (1, 1): 3, (2, 1): 4, (3, 1): 5}
 IMG = [
     [("a0", (0, 1), 0, H), ("a1", (2, 3), 0, H), ("a2", (4, 5), 0, H), ("a3", (6, 7), 0, H)],
-    [("y1", (0,), 0, H), ("y0", (1, 2), 0, H), ("t1", (3, 4), 0, H), ("a0", (5,), 0, H), ("t0", (6,), 0, H),
-     ("a1", (7,), 0, H)],
+    [(tag, (m,), 0, H) for m, tag in enumerate(("y0", "t1", "a0", "y1", "a1", "t0", "a2", "a3"))],
 ]
 BOTH = (0, 1)
 GX = 224
@@ -330,13 +329,13 @@ def tile_coded_aperture_backprojection_s13_kernel(
         product_planes(2, 1)
         empty_scenes(0, 0)
         empty_scenes(0, 1)
-        product_planes(4, 1)
+        product_planes(3, 1)
         quant_mask((0, 0), (0, 1), (1, 0), (1, 1))
         quant_scenes(0)
         weave_planes(2, 1, "g", x1=GX)
-        product_planes(3, 1)
         weave_planes(3, 1, "g", x1=GX)
         weave_planes(2, 1, "s", x0=GX)
+        product_planes(4, 1)
         weave_planes(3, 1, "s", x0=GX)
         project(0, 0, "a0")
         project(1, 0, "a1")
@@ -433,11 +432,13 @@ def tile_coded_aperture_backprojection_s13_kernel(
         weave_z(3, 1, "v")
         quant_z((2, 1))
         quant_z((3, 1))
-        backproject(0, 1, [1, 2, 0, 3, 4])
-        backproject(1, 1, range(3))
-        backproject(2, 1, [0, 1])
+        early = (7, 5, 2, 0)
+        backproject(0, 1, range(6))
+        backproject(1, 1, range(early[1]))
+        backproject(0, 1, [6])
+        backproject(2, 1, range(early[2]))
         for q in range(len(IMG[1])):
             for g in range(NG):
-                if g == 3 or (g == 2 and q > 1) or (g == 1 and q >= 3) or q > 4:
+                if q >= early[g]:
                     backproject(g, 1, [q])
             emit(1, q, "vs"[q % 2])

@@ -69,6 +69,9 @@ def tile_coded_aperture_backprojection_s13_kernel(
             g, r = divmod(j, 2)
             nc.sync.dma_start(out=mb[j][:, t, :], in_=mask_v[g][:, 2 * r + t, :])
 
+        def load_piece(c):
+            nc.sync.dma_start(out=mb[0][:, 0, 512 * c : 512 * (c + 1)], in_=mask_v[0][:, 0, 512 * c : 512 * (c + 1)])
+
         def load_mscale():
             nc.sync.dma_start(out=mscale, in_=mask_scale.rearrange("o (c p u e) -> p (o c) u e", c=NC, p=NP, u=2, e=2))
 
@@ -276,7 +279,8 @@ def tile_coded_aperture_backprojection_s13_kernel(
             nc.sync.dma_start(out=out_rows[:, tiles[0] : tiles[-1] + 1, H * h + x0 : H * h + x1], in_=res[:])
 
 
-        load_tile(0, 0)
+        load_piece(0)
+        load_piece(1)
         load_mscale()
         load_tile(0, 1)
         load_pair(1)
@@ -315,10 +319,10 @@ def tile_coded_aperture_backprojection_s13_kernel(
         widen(3, BOTH, BOTH, "g")
         widen(4, BOTH, BOTH, "s")
         widen(5, BOTH, BOTH, "s")
-        turn_mask(2, 1, "a1")
         turn_mask(2, 0, "t0")
         turn_scenes(0, 0, "a0")
         turn_scenes(0, 1, "t1")
+        turn_mask(2, 1, "a1")
         product(1, 0)
         product(1, 1)
         product(2, 0)
@@ -326,9 +330,9 @@ def tile_coded_aperture_backprojection_s13_kernel(
         turn_mask(3, 1, "y1")
         turn_mask(3, 0, "y0")
         turn_mask(4, 0, "a2")
-        product_planes(2, 1)
         empty_scenes(0, 0)
         empty_scenes(0, 1)
+        product_planes(2, 1)
         product_planes(3, 1)
         quant_mask((0, 0), (0, 1), (1, 0), (1, 1))
         quant_scenes(0)
@@ -399,21 +403,21 @@ def tile_coded_aperture_backprojection_s13_kernel(
         project(6, 0, "y0")
         project(7, 0, "t1")
         whiten(1, 1)
-        project(3, 1, "t0")
-        quant_z((2, 0))
         weave_z(0, 1, "s")
+        project(3, 1, "t0")
         whiten(6, 0)
-        backproject(2, 0, [0, 1])
         project(4, 1, "y0")
         whiten(7, 0)
+        quant_z((2, 0))
         weave_z(3, 0, "g", x1=96)
         weave_z(3, 0, "s", x0=96)
-        whiten(2, 1)
-        backproject(2, 0, [2, 3])
         project(5, 1, "t1")
+        backproject(2, 0, [0, 1])
+        whiten(2, 1)
         project(6, 1, "y1")
         whiten(3, 1)
         weave_z(1, 1, "s")
+        backproject(2, 0, [2, 3])
         quant_z((0, 1), (3, 0))
         whiten(4, 1)
         backproject(3, 0, [0, 1])

from contextlib import ExitStack

import concourse.mybir as mybir
from concourse.masks import make_identity

F32 = mybir.dt.float32
BF16 = mybir.dt.bfloat16
U32 = mybir.dt.uint32
I32 = mybir.dt.int32
U8 = mybir.dt.uint8
FP8 = mybir.dt.float8_e4m3fn
E4M3X4 = mybir.dt.float8_e4m3fn_x4
E2M1X4 = mybir.dt.float4_e2m1fn_x4
ALU = mybir.AluOpType
COPY = mybir.ActivationFunctionType.Copy

D, P, B = 2048, 1024, 512
FLOPS = 2 * 2 * D * P * B

NP = 128
NG = D // 512
NPAIR = 2 * NG
NC = P // 512
H = B // 2
UNIT = 1024
RING, ZRING = 6, 6
PART = {(0, 0): 0, (0, 1): 1, (1, 0): 2, (1, 1): 3, (2, 1): 3, (2, 0): 4, (3, 0): 1, (3, 1): 2, (4, 1): 4, (4, 0): 5,
        (5, 0): 3, (5, 1): 4, (6, 1): 3, (6, 0): 2, (7, 0): 0, (7, 1): 1}
ZPART = {(0, 0): 2, (1, 0): 3, (2, 0): 2, (0, 1): 0, (3, 0): 1, (1, 1): 3, (2, 1): 4, (3, 1): 5}
IMG = [
    [("a0", (0, 1), 0, H), ("a1", (2, 3), 0, H), ("a2", (4, 5), 0, H), ("a3", (6, 7), 0, H)],
    [(tag, (m,), 0, H) for m, tag in enumerate(("y0", "t1", "a0", "y1", "a1", "t0", "a2", "a3"))],
]
BOTH = (0, 1)
GX = 224


def tile_coded_aperture_backprojection_s13_kernel(
    tc, mask_bytes, mask_scale, scenes, dark, inv_sigma, dec_words, dec_scales, out
):
    nc = tc.nc
    with ExitStack() as ctx, tc.manual_schedule():
        keep = ctx.enter_context(tc.tile_pool(name="keep", bufs=1))
        psum = ctx.enter_context(tc.psum_pool(name="psum", bufs=1))

        mask_v = mask_bytes.rearrange("(g p t) k -> g p t k", g=NG, p=NP, t=4)
        sig_v = inv_sigma.rearrange("(g p t) b -> g p t b", g=NG, p=NP, t=4)
        scn_v = scenes.rearrange("(h t p) (c k) -> h c p t k", h=2, t=2, p=NP, c=NC)
        out_rows = out.rearrange("(m p) b -> p m b", p=NP)

        mscale_rows = keep.tile([NP, NC, 8], F32, name="mscale")
        mscale = mscale_rows[:, :, 0:4].rearrange("p c (u e) -> p c u e", u=2)
        dark_rows = keep.tile([NP, NG, 16], BF16, name="darks")
        darks = dark_rows[:, :, 0:4]
        ident = keep.tile([NP, NP], F32, name="ident")
        gsc = keep.tile([NP, NG, P], U8, name="gsc", align_bytes=64)
        mb = [keep.tile([NP, 2, P], U8, name=f"mb{j}", align_bytes=64) for j in range(NPAIR)]
        sig = [keep.tile([NP, 4, B], BF16, name=f"sig{g}", align_bytes=64) for g in range(NG)]
        scn = {(h, c): keep.tile([NP, 2, 512], BF16, name=f"scn{h}{c}", align_bytes=64) for h in range(2) for c in range(NC)}
        gw = [keep.tile([NP, 2 * P], U8, name=f"gw{g}", align_bytes=64) for g in range(NG)]
        make_identity(nc, ident[:])
        nc.vector.memset(gsc[:].bitcast(I32), 0)

        def load_pair(j):
            g, r = divmod(j, 2)
            nc.sync.dma_start(out=mb[j][:], in_=mask_v[g][:, 2 * r : 2 * r + 2, :])

        def load_tile(j, t):
            g, r = divmod(j, 2)
            nc.sync.dma_start(out=mb[j][:, t, :], in_=mask_v[g][:, 2 * r + t, :])

        def load_piece(c):
            nc.sync.dma_start(out=mb[0][:, 0, 512 * c : 512 * (c + 1)], in_=mask_v[0][:, 0, 512 * c : 512 * (c + 1)])

        def load_mscale():
            nc.sync.dma_start(out=mscale, in_=mask_scale.rearrange("o (c p u e) -> p (o c) u e", c=NC, p=NP, u=2, e=2))

        def load_scenes(h):
            for c in range(NC):
                nc.sync.dma_start(out=scn[h, c][:], in_=scn_v[h, c])

        def load_darks():
            nc.sync.dma_start(out=darks, in_=dark.rearrange("(g p t) -> p g t", g=NG, p=NP, t=4))

        def load_sig(g):
            nc.sync.dma_start(out=sig[g][:], in_=sig_v[g])

        def load_gscales():
            for q in range(4):
                nc.sync.dma_start(
                    out=gsc[32 * q : 32 * q + 4].bitcast(I32),
                    in_=dec_scales[:, 4 * q : 4 * q + 4, :].bitcast(I32).rearrange("g q n -> q g n"),
                )

        def load_gwords(g):
            nc.sync.dma_start(out=gw[g][:].bitcast(I32), in_=dec_words[g].bitcast(I32))

        halves, tbank, planes, codes, scales, ybank, zt, zcodes, zscales, img, sbank, first, sq, scodes, sscales = (
            {} for i in range(15)
        )

        def widen(j, tiles, passes, engine, tag=None):
            name = f"wide{j}_{tiles[0]}{passes[0]}"
            piece = keep.tile([NP, len(tiles), len(passes), 512], BF16, name=name, tag=tag or name, align_bytes=64)
            src = mb[j][:].rearrange("p t (c k) -> p t c k", c=NC)[:, tiles[0] : tiles[-1] + 1, passes[0] : passes[-1] + 1, :].bitcast(FP8)
            words = piece[:].bitcast(F32)
            for a, t in enumerate(tiles):
                for b, c in enumerate(passes):
                    for u in range(2):
                        halves[j, t, c, u] = words[:, a, b, u:256:2] if engine == "g" else words[:, a, b, NP * u : NP * (u + 1)]
            if engine == "g":
                nc.gpsimd.tensor_copy(out=piece[:], in_=src)
                return
            dst = piece[:].rearrange("p t c (u m e) -> p (t c) u m e", u=2, m=NP, e=2)
            src = src.rearrange("p t c (m u e) -> p (t c) u m e", u=2, m=NP, e=2)
            if engine == "v":
                nc.vector.tensor_copy(out=dst.rearrange("p q u m e -> p q m u e"), in_=src.rearrange("p q u m e -> p q m u e"))
            else:
                nc.scalar.copy(out=dst, in_=src)

        def turn_mask(j, c, tag):
            tbank[j, c] = psum.tile([NP, 2, 256], F32, name=f"tb{j}_{c}", tag=tag)
            for t in range(2):
                for u in range(2):
                    nc.tensor.transpose(tbank[j, c][:, u, NP * t : NP * (t + 1)], halves[j, t, c, u], ident[:])

        def turn_scenes(h, c, tag):
            sbank[h, c] = psum.tile([NP, 2, 256], F32, name=f"sb{h}_{c}", tag=tag)
            for t in range(2):
                words = scn[h, c][:, t, :].bitcast(F32)
                for u in range(2):
                    nc.tensor.transpose(sbank[h, c][:, u, NP * t : NP * (t + 1)], words[:, u:256:2], ident[:])

        def empty_scenes(h, c):
            if h not in sq:
                sq[h] = keep.tile([NP, NC, H, 4], BF16, name=f"sq{h}", tag=f"sq{h}", align_bytes=64)
            dst = sq[h][:, c].rearrange("p x t -> p (x t)").bitcast(F32)
            nc.scalar.copy(out=dst.rearrange("p (x u) -> p x u", u=2), in_=sbank[h, c][:].rearrange("p u x -> p x u"))

        def quant_scenes(h):
            scodes[h] = keep.tile([NP, NC, H], U32, name=f"scodes{h}", align_bytes=64)
            sscales[h] = keep.tile([NP, NC, H], U8, name=f"sscales{h}", align_bytes=64)
            nc.vector.quantize_mx(
                out=scodes[h][:].rearrange("p c x -> p (c x)").bitcast(E4M3X4),
                scales=sscales[h][:].rearrange("p c x -> p (c x)"),
                in_=sq[h][:].rearrange("p c x t -> p (c x t)"),
            )

        ring = keep.tile([NP, RING * UNIT], BF16, name="ring", align_bytes=64)
        zring = keep.tile([NP, ZRING * UNIT], BF16, name="zring", align_bytes=64)

        def quant_input(j, c):
            part = PART[j, c]
            return ring[:, UNIT * part : UNIT * (part + 1)].rearrange("p (x t) -> p x t", t=4)

        def z_input(g, h):
            part = ZPART[g, h]
            return zring[:, UNIT * part : UNIT * (part + 1)].rearrange("p (x t) -> p x t", t=4)

        def quantise(buf, parts, keys, name, codes_of, scales_of):
            keys = sorted(keys, key=parts.get)
            n, lo = len(keys), parts[keys[0]]
            assert [parts[k] for k in keys] == list(range(lo, lo + n))
            words = keep.tile([NP, n * 256], U32, name=f"codes_{name}", align_bytes=64)
            plane = keep.tile([NP, n * 256], U8, name=f"scales_{name}", align_bytes=64)
            nc.vector.quantize_mx(out=words[:].bitcast(E4M3X4), scales=plane[:], in_=buf[:, UNIT * lo : UNIT * (lo + n)])
            for i, k in enumerate(keys):
                codes_of[k] = words[:, 256 * i : 256 * (i + 1)]
                scales_of[k] = plane[:, 256 * i : 256 * (i + 1)]

        def product(j, c):
            nc.vector.tensor_tensor(
                out=quant_input(j, c).rearrange("p x (u e) -> p x u e", u=2),
                in0=mscale[:, c : c + 1].to_broadcast([NP, 256, 2, 2]),
                in1=tbank[j, c][:].bitcast(BF16).rearrange("p u (x e) -> p x u e", e=2),
                op=ALU.mult,
            )

        def turn_first(t, c, tag):
            first[t, c] = psum.tile([NP, 2, NP], F32, name=f"first{t}_{c}", tag=tag)
            for u in range(2):
                nc.tensor.transpose(first[t, c][:, u, :], halves[0, t, c, u], ident[:])

        def product_first(t, c):
            nc.vector.tensor_tensor(
                out=quant_input(0, c)[:, NP * t : NP * (t + 1)].rearrange("p x (u e) -> p x u e", u=2),
                in0=mscale[:, c : c + 1].to_broadcast([NP, NP, 2, 2]),
                in1=first[t, c][:].bitcast(BF16).rearrange("p u (x e) -> p x u e", e=2),
                op=ALU.mult,
            )

        def product_planes(j, c):
            planes[j, c] = keep.tile([NP, 4, 256], BF16, name=f"planes{j}_{c}", align_bytes=64)
            src = tbank[j, c][:].bitcast(BF16).rearrange("p u (x e) -> p u e x", e=2)
            for u in range(2):
                for e in range(2):
                    nc.scalar.activation(
                        out=planes[j, c][:, 2 * u + e, :], in_=src[:, u, e, :], func=COPY, scale=mscale[:, c, u, e : e + 1]
                    )

        def weave(dst, src, engine):
            if engine == "g":
                nc.gpsimd.tensor_scalar(
                    out=dst, in0=src.rearrange("p t x -> p x t"), scalar1=1.0, scalar2=0.0, op0=ALU.mult, op1=ALU.add
                )
                return
            dst = dst.rearrange("p (c i) t -> p c t i", i=4)
            src = src.rearrange("p t (c i) -> p c t i", i=4)
            if engine == "v":
                nc.vector.tensor_copy(out=dst, in_=src)
            else:
                nc.scalar.copy(out=dst, in_=src)

        def weave_planes(j, c, engine, x0=0, x1=256):
            weave(quant_input(j, c)[:, x0:x1], planes[j, c][:, :, x0:x1], engine)

        def quant_mask(*units):
            quantise(ring, PART, units, f"mask{units[0][0]}{units[0][1]}", codes, scales)

        def project(j, h, tag, order=(1, 0)):
            ybank[j, h] = psum.tile([NP, 2, H], F32, name=f"y{j}_{h}", tag=tag)
            for t in range(2):
                cols = slice(NP * t, NP * (t + 1))
                for c in order:
                    nc.tensor.matmul_mx(
                        out=ybank[j, h][:, t, :],
                        lhsT=codes[j, c][:, cols].bitcast(E4M3X4),
                        lhsT_scale=scales[j, c][:, cols],
                        rhs=scodes[h][:, c, :].bitcast(E4M3X4),
                        rhs_scale=sscales[h][:, c, :],
                        start=(c == order[0]),
                        stop=(c == order[-1]),
                    )

        def whiten(j, h):
            g, r = divmod(j, 2)
            if (g, h) not in zt:
                zt[g, h] = keep.tile([NP, 4, H], BF16, name=f"zt{g}{h}", align_bytes=64)
            for t in range(2):
                s = 2 * r + t
                nc.vector.scalar_tensor_tensor(
                    out=zt[g, h][:, s, :],
                    in0=ybank[j, h][:, t, :],
                    scalar=darks[:, g, s : s + 1],
                    in1=sig[g][:, s, H * h : H * (h + 1)],
                    op0=ALU.subtract,
                    op1=ALU.mult,
                )

        def weave_z(g, h, engine, x0=0, x1=H):
            weave(z_input(g, h)[:, x0:x1, :], zt[g, h][:, :, x0:x1], engine)

        def quant_z(*keys):
            quantise(zring, ZPART, keys, f"z{keys[0][0]}{keys[0][1]}", zcodes, zscales)

        def backproject(g, h, banks):
            for q in banks:
                tag, tiles, x0, x1 = IMG[h][q]
                if g == 0:
                    img[h, q] = psum.tile([NP, len(tiles), x1 - x0], F32, name=f"img{h}{q}", tag=tag)
                for i, m in enumerate(tiles):
                    nc.tensor.matmul_mx(
                        out=img[h, q][:, i, :],
                        lhsT=gw[g][:, 256 * m : 256 * (m + 1)].bitcast(E2M1X4),
                        lhsT_scale=gsc[:, g, 128 * m : 128 * (m + 1)],
                        rhs=zcodes[g, h][:, x0:x1].bitcast(E4M3X4),
                        rhs_scale=zscales[g, h][:, x0:x1],
                        start=(g == 0 and i == 0),
                        stop=(g == NG - 1 and i == len(tiles) - 1),
                    )

        def emit(h, q, engine):
            tag, tiles, x0, x1 = IMG[h][q]
            res = keep.tile([NP, len(tiles), x1 - x0], F32, name=f"res{h}{q}")
            if engine == "v":
                nc.vector.tensor_copy(out=res[:], in_=img[h, q][:])
            else:
                nc.scalar.copy(out=res[:], in_=img[h, q][:])
            nc.sync.dma_start(out=out_rows[:, tiles[0] : tiles[-1] + 1, H * h + x0 : H * h + x1], in_=res[:])


        load_piece(0)
        load_piece(1)
        load_mscale()
        load_tile(0, 1)
        load_pair(1)
        for j in (2, 4, 3, 5):
            load_pair(j)
        load_scenes(0)
        load_darks()
        load_sig(0)
        load_pair(6)
        load_sig(1)
        load_scenes(1)
        load_pair(7)
        load_gscales()
        load_gwords(0)
        for g in range(2, NG):
            load_sig(g)
            load_gwords(g - 1)
        load_gwords(NG - 1)

        widen(0, (0,), (0,), "v")
        widen(0, (0,), (1,), "s")
        turn_first(0, 0, "y0")
        turn_first(0, 1, "y1")
        widen(0, (1,), (0,), "s")
        widen(0, (1,), (1,), "v")
        turn_first(1, 0, "t0")
        turn_first(1, 1, "t1")
        widen(1, BOTH, (0,), "s")
        widen(1, BOTH, (1,), "s")
        turn_mask(1, 0, "a2")
        turn_mask(1, 1, "a3")
        for t, c in ((0, 0), (0, 1), (1, 0), (1, 1)):
            product_first(t, c)
        widen(2, (0,), BOTH, "s")
        widen(2, (1,), BOTH, "g")
        widen(3, BOTH, BOTH, "g")
        widen(4, BOTH, BOTH, "s")
        widen(5, BOTH, BOTH, "s")
        turn_mask(2, 0, "t0")
        turn_scenes(0, 0, "a0")
        turn_scenes(0, 1, "t1")
        turn_mask(2, 1, "a1")
        product(1, 0)
        product(1, 1)
        product(2, 0)
        turn_mask(4, 1, "a3")
        turn_mask(3, 1, "y1")
        turn_mask(3, 0, "y0")
        turn_mask(4, 0, "a2")
        empty_scenes(0, 0)
        empty_scenes(0, 1)
        product_planes(2, 1)
        product_planes(3, 1)
        quant_mask((0, 0), (0, 1), (1, 0), (1, 1))
        quant_scenes(0)
        weave_planes(2, 1, "g", x1=GX)
        weave_planes(3, 1, "g", x1=GX)
        weave_planes(2, 1, "s", x0=GX)
        product_planes(4, 1)
        weave_planes(3, 1, "s", x0=GX)
        project(0, 0, "a0")
        project(1, 0, "a1")
        turn_mask(5, 1, "t1")
        turn_mask(5, 0, "t0")
        widen(6, BOTH, BOTH, "s")
        widen(7, BOTH, BOTH, "s")
        product(3, 0)
        product(4, 0)
        turn_scenes(1, 0, "a2")
        turn_scenes(1, 1, "a3")
        whiten(0, 0)
        whiten(1, 0)
        weave_z(0, 0, "s")
        quant_mask((2, 0), (2, 1))
        quant_mask((3, 0), (3, 1))
        weave_planes(4, 1, "g", x1=GX)
        weave_planes(4, 1, "s", x0=GX)
        empty_scenes(1, 0)
        product_planes(5, 1)
        empty_scenes(1, 1)
        project(2, 0, "y0")
        project(3, 0, "y1")
        product(5, 0)
        turn_mask(6, 0, "t0")
        whiten(2, 0)
        quant_z((0, 0))
        backproject(0, 0, [0, 1, 2])
        whiten(3, 0)
        weave_z(1, 0, "s")
        quant_mask((4, 1))
        quant_mask((4, 0))
        weave_planes(5, 1, "g", x1=GX)
        weave_planes(5, 1, "s", x0=GX)
        project(4, 0, "y0")
        turn_mask(6, 1, "t1")
        product_planes(6, 1)
        product(6, 0)
        turn_mask(7, 1, "y1")
        turn_mask(7, 0, "t0")
        backproject(0, 0, [3])
        whiten(4, 0)
        product_planes(7, 1)
        weave_planes(7, 1, "s")
        quant_z((1, 0))
        quant_mask((5, 0), (5, 1))
        quant_scenes(1)
        weave_planes(6, 1, "g")
        backproject(1, 0, [0, 1])
        project(5, 0, "y0")
        project(0, 1, "t1")
        project(2, 1, "y1")
        product(7, 0)
        whiten(5, 0)
        whiten(0, 1)
        project(1, 1, "t0")
        backproject(1, 0, [2, 3])
        quant_mask((6, 0), (6, 1))
        quant_mask((7, 0), (7, 1))
        weave_z(2, 0, "s")
        project(6, 0, "y0")
        project(7, 0, "t1")
        whiten(1, 1)
        weave_z(0, 1, "s")
        project(3, 1, "t0")
        whiten(6, 0)
        project(4, 1, "y0")
        whiten(7, 0)
        quant_z((2, 0))
        weave_z(3, 0, "g", x1=96)
        weave_z(3, 0, "s", x0=96)
        project(5, 1, "t1")
        backproject(2, 0, [0, 1])
        whiten(2, 1)
        project(6, 1, "y1")
        whiten(3, 1)
        weave_z(1, 1, "s")
        backproject(2, 0, [2, 3])
        quant_z((0, 1), (3, 0))
        whiten(4, 1)
        backproject(3, 0, [0, 1])
        project(7, 1, "t0")
        backproject(3, 0, [2, 3])
        whiten(5, 1)
        weave_z(2, 1, "g", x1=128)
        emit(0, 0, "s")
        emit(0, 1, "s")
        weave_z(2, 1, "s", x0=128)
        emit(0, 2, "s")
        emit(0, 3, "s")
        whiten(6, 1)
        whiten(7, 1)
        quant_z((1, 1))
        weave_z(3, 1, "v")
        quant_z((2, 1))
        quant_z((3, 1))
        early = (7, 5, 2, 0)
        backproject(0, 1, range(6))
        backproject(1, 1, range(early[1]))
        backproject(0, 1, [6])
        backproject(2, 1, range(early[2]))
        for q in range(len(IMG[1])):
            for g in range(NG):
                if q >= early[g]:
                    backproject(g, 1, [q])
            emit(1, q, "vs"[q % 2])
